import numpy as np
import ml_dtypes


def mxq(x, axis, fmt="e4m3"):
    dtype, down = {"e4m3": (ml_dtypes.float8_e4m3fn, 7), "e5m2": (ml_dtypes.float8_e5m2, 14)}[fmt]
    v = np.moveaxis(np.asarray(x, np.float32).astype(ml_dtypes.bfloat16).astype(np.float64), axis, -1)
    blocks = v.reshape(v.shape[:-1] + (-1, 32))
    amax = np.abs(blocks).max(-1, keepdims=True)
    byte = np.maximum(np.where(amax > 0, np.frexp(amax)[1] - 1 + 127, 0) - down, 1)
    scale = np.exp2(byte - 127.0)
    codes = (blocks / scale).astype(np.float32).astype(dtype).astype(np.float64)
    return np.moveaxis((codes * scale).reshape(v.shape), -1, axis)


WIDE = False


def mx_kscale(k):
    if not WIDE:
        return np.ones(k)
    levels = np.array([10, -10, 5, -5, 0])
    if k % 512:
        return np.exp2(np.random.permutation(np.resize(levels, k // 32))).repeat(32)
    a = np.empty((k // 512, 16))
    for p in range(k // 512):
        a[p, :8] = np.random.permutation(np.resize(levels, 8))
        for g in range(8):
            far = levels[np.abs(levels - a[p, g]) >= 10]
            a[p, g + 8] = far[np.random.randint(len(far))]
    return np.exp2(a.ravel()).repeat(32)


def f64(x):
    return np.asarray(x).astype(np.float64)


def striped(idx):
    return np.tile(idx.reshape(-1, 16).T, (8, 1)).astype(np.uint16)


def unstriped(offs):
    return offs[:16].T.reshape(-1).astype(np.int64)


def pack_weight(w):
    k, n = w.shape
    w = f64(np.asarray(w, np.float32).astype(ml_dtypes.bfloat16)).reshape(k // 32, 32, n)
    amax = np.abs(w).max(1)
    byte = np.clip(np.where(amax > 0, np.frexp(amax)[1] - 1 + 127 - 7, 1), 1, 254)
    scaled = (w * np.exp2(127.0 - byte)[:, None, :]).reshape(k, n).astype(np.float32)
    words = np.ascontiguousarray(scaled.reshape(k // 512, 128, 4, n).transpose(0, 1, 3, 2)).astype(ml_dtypes.float8_e4m3fn).view(np.uint8)
    return words, np.ascontiguousarray(byte.astype(np.uint8).reshape(k // 512, 16, n))


def unpack_weight(words, scales):
    g, p, n, _ = words.shape
    vals = np.ascontiguousarray(words).view(ml_dtypes.float8_e4m3fn).astype(np.float64) * np.repeat(np.exp2(scales.astype(np.float64) - 127.0), 8, axis=1)[..., None]
    return vals.transpose(0, 1, 3, 2).reshape(g * 512, n)


def planes(y):
    n, m = y.shape
    v = y.astype(np.float32).astype(ml_dtypes.bfloat16).astype(np.float64).reshape(n // 32, 32, m)
    top = np.abs(v).max(1)
    byte = np.clip(np.where(top > 0, np.frexp(top)[1] - 1 + 127 - 7, 1), 1, 254)
    codes = (v * np.exp2(127.0 - byte)[:, None, :]).reshape(n, m).astype(np.float32).astype(ml_dtypes.float8_e4m3fn).view(np.uint8)
    words = codes.reshape(n // 512, 128, 4, m).transpose(0, 1, 3, 2)
    return np.ascontiguousarray(words), np.ascontiguousarray(byte.astype(np.uint8).reshape(n // 512, 16, m))


def sigmoid(v):
    return 1.0 / (1.0 + np.exp(-np.maximum(v, -700.0)))


K, T, S, V, N, D = 512, 4096, 1024, 512, 512, 3
P = 2 ** 7


def setup_inputs():
    n = np.random.standard_normal
    s = mx_kscale(K)[:, None]
    near = np.random.permutation(S)
    packed_xT = pack_weight(n((K, T)) * s)
    return {
        "x_words": packed_xT[0],
        "x_scales": packed_xT[1],
        "w1": (n((K, N)) / np.sqrt(K) / s).astype(np.float32),
        "op": (np.tile(np.random.uniform(0.2, 0.95, S), (P, 1))).astype(np.float32),
        "fall": (np.tile(np.random.uniform(0.2, 1.0, (D, 1, V)), (1, P, 1))).astype(np.float32),
        "offs": striped(np.random.permutation(T)[:S]),
        "pos1": striped(near[:V]),
        "pos2": striped(near[V:]),
        "pos3": striped(np.random.permutation(S)[:V]),
    }


def reference(x_words, x_scales, w1, op, fall, offs, pos1, pos2, pos3):
    xq = unpack_weight(x_words, x_scales)[:, unstriped(offs)]
    h = sigmoid(mxq(f64(w1), 0, "e4m3").T @ xq)
    a0 = (f64(op)[:1][:, unstriped(pos1)]) * f64(fall)[0, :1]
    a1 = (f64(op)[:1][:, unstriped(pos2)]) * f64(fall)[1, :1]
    t0 = -1.0 * a0 + 1.0
    c1 = a1 * t0
    a2 = (f64(op)[:1][:, unstriped(pos3)]) * f64(fall)[2, :1]
    t1 = t0 - (t0 * a1)
    c2 = a2 * t1
    out_0 = h[:, unstriped(pos1)] * a0 + h[:, unstriped(pos2)] * c1 + h[:, unstriped(pos3)] * c2
    return (out_0,) + planes(out_0)

@@ -1,0 +1,197 @@
+from contextlib import ExitStack
+
+import concourse.mybir as mybir
+from concourse.masks import make_identity
+
+K, T, S, V, N, D = 512, 4096, 1024, 512, 512, 3
+P = 128
+PACK = 4
+FLOPS = 2 * K * N * S
+
+F32 = mybir.dt.float32
+BF16 = mybir.dt.bfloat16
+I32 = mybir.dt.int32
+U32 = mybir.dt.uint32
+U16 = mybir.dt.uint16
+U8 = mybir.dt.uint8
+FP8X4 = mybir.dt.float8_e4m3fn_x4
+ACT = mybir.ActivationFunctionType
+MULT, ADD, SUB = mybir.AluOpType.mult, mybir.AluOpType.add, mybir.AluOpType.subtract
+
+HALF = S // 2
+FUSED = 0
+WIDTHS = [128,128,128,128]
+VECTOR_EVAC = [[1,0],[1,1],[1,2],[1,3]]
+
+
+def tile_picked_ysplat_sigmoid_po_kernel(
+    tc, x_words, x_scales, w1, op, fall, offs, pos1, pos2, pos3, out_0, out_1, out_2
+):
+    nc = tc.nc
+    with ExitStack() as ctx:
+        keep = ctx.enter_context(tc.tile_pool(name="keep", bufs=1))
+        ring = ctx.enter_context(tc.tile_pool(name="ring", bufs=3))
+        psum = ctx.enter_context(tc.psum_pool(name="psum", bufs=1))
+
+        def bank(number):
+            return psum.tile([P, 4, P], F32, name=f"bank{number}")
+
+        pos = [keep.tile([P, V // 16], U16, name=f"pos{d}") for d in range(D)]
+        picks = keep.tile([P, S // 16], U16, name="picks")
+        w_raw = keep.tile([P, PACK, N], F32, name="w_raw")
+        x_table = keep.tile([P, T], I32, name="x_table")
+        scale_table = keep.tile([P, T], U8, name="scale_table")
+        op_table = keep.tile([P, S], F32, name="op_table")
+        fall_rows = keep.tile([P, V], F32, name="fall_rows")
+        ident = keep.tile([P, P], F32, name="ident")
+        warm = keep.tile([P, 2], F32, name="warm")
+        x_scale_rows = keep.tile([P, S], U8, name="x_scale_rows")
+        x_scale = keep.tile([P, S], U8, name="x_scale", align_bytes=64)
+
+        nc.sync.dma_start(picks[:], offs)
+        nc.sync.dma_start(scale_table[P - 16 :, :].bitcast(I32), x_scales[0].bitcast(I32))
+        nc.scalar.dma_start(op_table[P - 1 :, :], op[0:1, :])
+        nc.sync.dma_start(pos[0][:], pos1)
+        nc.scalar.dma_start(fall_rows[P - D :, :], fall[:, 0, :])
+        nc.sync.dma_start(pos[1][:], pos2)
+        nc.sync.dma_start(pos[2][:], pos3)
+        nc.sync.dma_start(w_raw[:], w1.rearrange("(p j) c -> p j c", j=PACK))
+        nc.sync.dma_start(x_table[:], x_words[0].rearrange("p n t -> p (n t)").bitcast(I32))
+
+        nc.vector.memset(scale_table[: P - 16, :].bitcast(I32), 0)
+        nc.vector.memset(op_table[: P - 1, :], 0.0)
+        nc.vector.memset(x_scale[:].bitcast(I32), 0)
+        nc.gpsimd.memset(fall_rows[: P - D, :], 0.0)
+        make_identity(nc, ident[:])
+        nc.scalar.activation(warm[:, 0:1], ident[:, 0:1], ACT.Sigmoid)
+
+        nc.vector.tensor_copy(x_scale_rows[:], scale_table[:].indirect(picks[:]))
+        for q in range(4):
+            nc.sync.dma_start(
+                x_scale[32 * q : 32 * q + 4, :].bitcast(I32),
+                x_scale_rows[P - 16 + 4 * q : P - 12 + 4 * q, :].bitcast(I32),
+            )
+
+        op_rows = [keep.tile([P, V], F32, name=f"op_rows{d}") for d in range(D)]
+        for d in range(D):
+            nc.vector.tensor_copy(op_rows[d][:], op_table[:].indirect(pos[d][:]))
+
+        fall_cols = keep.tile([P, D, 4], F32, name="fall_cols")
+        turned = bank(0)
+        for c in range(4):
+            nc.tensor.transpose(turned[:, c, :], fall_rows[:, c * P : (c + 1) * P], ident[:])
+        nc.scalar.copy(fall_cols[:], turned[:, :, P - D :].rearrange("p c d -> p d c"))
+
+        w_bf = keep.tile([P, PACK, P, PACK], BF16, name="w_bf", align_bytes=64)
+        w_codes = keep.tile([P, N], U32, name="w_codes", align_bytes=64)
+        w_scales = keep.tile([P, N], U8, name="w_scales", align_bytes=64)
+        nc.scalar.copy(
+            w_bf[:].rearrange("p t m j -> p m j t"), w_raw[:].rearrange("p j (m t) -> p m j t", t=PACK)
+        )
+
+        op_cols = keep.tile([P, D, 4], F32, name="op_cols")
+        seen = keep.tile([P, D, 4], F32, name="seen")
+        through = keep.tile([P, 2, 4], F32, name="through")
+        weight_cols = keep.tile([P, D, 4], F32, name="weight_cols")
+        weights = keep.tile([P, D, V], F32, name="weights")
+
+        def weight_column(d):
+            turned = bank(1 + d)
+            for c in range(4):
+                nc.tensor.transpose(turned[:, c, :], op_rows[d][:, c * P : (c + 1) * P], ident[:])
+            nc.scalar.copy(op_cols[:, d, :], turned[:, :, P - 1])
+            factor = fall_cols if d == 0 else seen
+            nc.gpsimd.tensor_tensor(weight_cols[:, d, :], op_cols[:, d, :], factor[:, d, :], MULT)
+            if d == 0:
+                nc.gpsimd.tensor_scalar(through[:, 0, :], weight_cols[:, 0, :], -1.0, 1.0, MULT, ADD)
+            if d == 1:
+                nc.gpsimd.tensor_tensor(through[:, 1, :], through[:, 0, :], weight_cols[:, 1, :], SUB)
+            if d + 1 < D:
+                nc.gpsimd.tensor_tensor(seen[:, d + 1, :], fall_cols[:, d + 1, :], through[:, d, :], MULT)
+
+        def spread_weight(d, number):
+            spread = bank(number)
+            for c in range(4):
+                nc.tensor.transpose(spread[:, c, :], weight_cols[:, d, c : c + 1].to_broadcast([P, P]), ident[:])
+            nc.scalar.copy(weights[:, d, :], spread[:].rearrange("p c n -> p (c n)"))
+
+        for d in range(D):
+            weight_column(d)
+            if d + 1 < D:
+                spread_weight(d, 4 + d)
+
+        nc.vector.quantize_mx(
+            out=w_codes[:].bitcast(FP8X4), scales=w_scales[:], in_=w_bf[:].rearrange("p t m j -> p (t m j)")
+        )
+
+        x_codes = [keep.tile([P, HALF], U32, name=f"x_codes{h}", align_bytes=64) for h in range(2)]
+        for h in range(2):
+            nc.vector.tensor_copy(
+                x_codes[h][:], x_table[:].bitcast(U32).indirect(picks[:, h * HALF // 16 : (h + 1) * HALF // 16])
+            )
+
+        rows = [keep.tile([P, S], F32, name=f"rows{t}") for t in range(PACK)]
+        for h in range(2):
+            cols = slice(h * HALF, (h + 1) * HALF)
+            for t in range(PACK):
+                acc = bank(t if h == 0 else 4 + (t + 2) % 4)[:].rearrange("p c n -> p (c n)")
+                nc.tensor.matmul_mx(
+                    out=acc,
+                    lhsT=w_codes[:, t * P : (t + 1) * P].bitcast(FP8X4),
+                    lhsT_scale=w_scales[:, t * P : (t + 1) * P],
+                    rhs=x_codes[h][:].bitcast(FP8X4),
+                    rhs_scale=x_scale[:, cols],
+                    start=True,
+                    stop=True,
+                )
+                if t < FUSED:
+                    nc.scalar.activation(rows[t][:, cols], acc, ACT.Sigmoid)
+                elif [h, t] in VECTOR_EVAC:
+                    nc.vector.tensor_copy(rows[t][:, cols], acc)
+                else:
+                    nc.scalar.copy(rows[t][:, cols], acc)
+        spread_weight(D - 1, 0)
+
+        y_codes = keep.tile([P, V], U32, name="y_codes", align_bytes=64)
+        y_scales = keep.tile([P, V], U8, name="y_scales", align_bytes=64)
+        out_rows = out_0.rearrange("(p t) v -> p t v", t=PACK)
+        out_words = out_1[0].rearrange("p n t -> p (n t)").bitcast(I32)
+        v0 = 0
+        for width in WIDTHS:
+            vs = slice(v0, v0 + width)
+            terms = [ring.tile([P, PACK, width], F32, name=f"terms{d}") for d in range(D)]
+            y = ring.tile([P, PACK, width], F32, name="y")
+            y_bf = ring.tile([P, width, PACK], BF16, name="y_bf", align_bytes=64)
+            for d in range(D):
+                offsets = pos[d][:, v0 // 16 : (v0 + width) // 16]
+                for t in range(PACK):
+                    if t < FUSED:
+                        nc.vector.tensor_tensor(
+                            terms[d][:, t, :], rows[t][:].indirect(offsets), weights[:, d, vs], MULT
+                        )
+                    else:
+                        nc.scalar.activation(terms[d][:, t, :], rows[t][:].indirect(offsets), ACT.Sigmoid)
+                if FUSED < PACK:
+                    nc.vector.tensor_tensor(
+                        terms[d][:, FUSED:, :],
+                        terms[d][:, FUSED:, :],
+                        weights[:, d : d + 1, vs].to_broadcast([P, PACK - FUSED, width]),
+                        MULT,
+                    )
+                if d == 1:
+                    nc.vector.tensor_tensor(y[:], terms[0][:], terms[1][:], ADD)
+            nc.vector.tensor_tensor(y[:], y[:], terms[2][:], ADD)
+            nc.sync.dma_start(out_rows[:, :, vs], y[:])
+            nc.vector.tensor_copy(
+                y_bf[:].rearrange("p (c i) t -> p c t i", i=4), y[:].rearrange("p t (c i) -> p c t i", i=4)
+            )
+            nc.vector.quantize_mx(
+                out=y_codes[:, vs].bitcast(FP8X4), scales=y_scales[:, vs], in_=y_bf[:].rearrange("p v t -> p (v t)")
+            )
+            nc.sync.dma_start(out_words[:, vs], y_codes[:, vs].bitcast(I32))
+            v0 += width
+        for q in range(4):
+            queue = nc.scalar if q % 2 else nc.sync
+            queue.dma_start(
+                out_2[0, 4 * q : 4 * q + 4, :].bitcast(I32), y_scales[32 * q : 32 * q + 4, :].bitcast(I32)
+            )

@@ -16,12 +16,12 @@ U16 = mybir.dt.uint16
 U8 = mybir.dt.uint8
 FP8X4 = mybir.dt.float8_e4m3fn_x4
 ACT = mybir.ActivationFunctionType
-MULT, ADD, SUB = mybir.AluOpType.mult, mybir.AluOpType.add, mybir.AluOpType.subtract
+MULT, ADD = mybir.AluOpType.mult, mybir.AluOpType.add
 
 HALF = S // 2
-FUSED = 0
-WIDTHS = [128,128,128,128]
-VECTOR_EVAC = [[1,0],[1,1],[1,2],[1,3]]
+FUSED = 1
+WIDTHS = [128,128,128,64,64]
+VECTOR_EVAC = [[1,1]]
 
 
 def tile_picked_ysplat_sigmoid_po_kernel(
@@ -30,7 +30,7 @@ def tile_picked_ysplat_sigmoid_po_kernel(
     nc = tc.nc
     with ExitStack() as ctx:
         keep = ctx.enter_context(tc.tile_pool(name="keep", bufs=1))
-        ring = ctx.enter_context(tc.tile_pool(name="ring", bufs=3))
+        ring = ctx.enter_context(tc.tile_pool(name="ring", bufs=4))
         psum = ctx.enter_context(tc.psum_pool(name="psum", bufs=1))
 
         def bank(number):
@@ -89,7 +89,6 @@ def tile_picked_ysplat_sigmoid_po_kernel(
             w_bf[:].rearrange("p t m j -> p m j t"), w_raw[:].rearrange("p j (m t) -> p m j t", t=PACK)
         )
 
-        op_cols = keep.tile([P, D, 4], F32, name="op_cols")
         seen = keep.tile([P, D, 4], F32, name="seen")
         through = keep.tile([P, 2, 4], F32, name="through")
         weight_cols = keep.tile([P, D, 4], F32, name="weight_cols")
@@ -99,15 +98,25 @@ def tile_picked_ysplat_sigmoid_po_kernel(
             turned = bank(1 + d)
             for c in range(4):
                 nc.tensor.transpose(turned[:, c, :], op_rows[d][:, c * P : (c + 1) * P], ident[:])
-            nc.scalar.copy(op_cols[:, d, :], turned[:, :, P - 1])
             factor = fall_cols if d == 0 else seen
-            nc.gpsimd.tensor_tensor(weight_cols[:, d, :], op_cols[:, d, :], factor[:, d, :], MULT)
+            for c in range(4):
+                nc.scalar.activation(
+                    weight_cols[:, d, c : c + 1], turned[:, c, P - 1 :], ACT.Copy, scale=factor[:, d, c : c + 1]
+                )
+
+        def see_through(d):
             if d == 0:
-                nc.gpsimd.tensor_scalar(through[:, 0, :], weight_cols[:, 0, :], -1.0, 1.0, MULT, ADD)
-            if d == 1:
-                nc.gpsimd.tensor_tensor(through[:, 1, :], through[:, 0, :], weight_cols[:, 1, :], SUB)
-            if d + 1 < D:
-                nc.gpsimd.tensor_tensor(seen[:, d + 1, :], fall_cols[:, d + 1, :], through[:, d, :], MULT)
+                nc.scalar.activation(through[:, 0, :], weight_cols[:, 0, :], ACT.Copy, scale=-1.0, bias=1.0)
+            for c in range(4):
+                if d == 1:
+                    nc.scalar.activation(
+                        through[:, 1, c : c + 1], weight_cols[:, 1, c : c + 1], ACT.Identity,
+                        scale=-1.0, bias=through[:, 0, c : c + 1],
+                    )
+            for c in range(4):
+                nc.scalar.activation(
+                    seen[:, d + 1, c : c + 1], fall_cols[:, d + 1, c : c + 1], ACT.Copy, scale=through[:, d, c : c + 1]
+                )
 
         def spread_weight(d, number):
             spread = bank(number)
@@ -118,6 +127,7 @@ def tile_picked_ysplat_sigmoid_po_kernel(
         for d in range(D):
             weight_column(d)
             if d + 1 < D:
+                see_through(d)
                 spread_weight(d, 4 + d)
 
         nc.vector.quantize_mx(
@@ -131,9 +141,9 @@ def tile_picked_ysplat_sigmoid_po_kernel(
             )
 
         rows = [keep.tile([P, S], F32, name=f"rows{t}") for t in range(PACK)]
-        for h in range(2):
+        for h, t in [(0, 0), (0, 1), (1, 0), (1, 1), (0, 2), (1, 2), (0, 3), (1, 3)]:
             cols = slice(h * HALF, (h + 1) * HALF)
-            for t in range(PACK):
+            if True:
                 acc = bank(t if h == 0 else 4 + (t + 2) % 4)[:].rearrange("p c n -> p (c n)")
                 nc.tensor.matmul_mx(
                     out=acc,
@@ -156,31 +166,28 @@ def tile_picked_ysplat_sigmoid_po_kernel(
         y_scales = keep.tile([P, V], U8, name="y_scales", align_bytes=64)
         out_rows = out_0.rearrange("(p t) v -> p t v", t=PACK)
         out_words = out_1[0].rearrange("p n t -> p (n t)").bitcast(I32)
+        terms = [keep.tile([P, PACK, V], F32, name=f"terms{d}") for d in range(D)]
+        for t in range(FUSED):
+            for d in range(D):
+                nc.vector.tensor_tensor(terms[d][:, t, :], rows[t][:].indirect(pos[d][:]), weights[:, d, :], MULT)
         v0 = 0
         for width in WIDTHS:
             vs = slice(v0, v0 + width)
-            terms = [ring.tile([P, PACK, width], F32, name=f"terms{d}") for d in range(D)]
             y = ring.tile([P, PACK, width], F32, name="y")
             y_bf = ring.tile([P, width, PACK], BF16, name="y_bf", align_bytes=64)
             for d in range(D):
                 offsets = pos[d][:, v0 // 16 : (v0 + width) // 16]
-                for t in range(PACK):
-                    if t < FUSED:
-                        nc.vector.tensor_tensor(
-                            terms[d][:, t, :], rows[t][:].indirect(offsets), weights[:, d, vs], MULT
-                        )
-                    else:
-                        nc.scalar.activation(terms[d][:, t, :], rows[t][:].indirect(offsets), ACT.Sigmoid)
-                if FUSED < PACK:
-                    nc.vector.tensor_tensor(
-                        terms[d][:, FUSED:, :],
-                        terms[d][:, FUSED:, :],
-                        weights[:, d : d + 1, vs].to_broadcast([P, PACK - FUSED, width]),
-                        MULT,
-                    )
-                if d == 1:
-                    nc.vector.tensor_tensor(y[:], terms[0][:], terms[1][:], ADD)
-            nc.vector.tensor_tensor(y[:], y[:], terms[2][:], ADD)
+                for t in range(FUSED, PACK):
+                    nc.scalar.activation(terms[d][:, t, vs], rows[t][:].indirect(offsets), ACT.Sigmoid)
+                if d == 2:
+                    nc.vector.tensor_tensor(y[:], terms[0][:, :, vs], terms[1][:, :, vs], ADD)
+                nc.vector.tensor_tensor(
+                    terms[d][:, FUSED:, vs],
+                    terms[d][:, FUSED:, vs],
+                    weights[:, d : d + 1, vs].to_broadcast([P, PACK - FUSED, width]),
+                    MULT,
+                )
+            nc.vector.tensor_tensor(y[:], y[:], terms[2][:, :, vs], ADD)
             nc.sync.dma_start(out_rows[:, :, vs], y[:])
             nc.vector.tensor_copy(
                 y_bf[:].rearrange("p (c i) t -> p c t i", i=4), y[:].rearrange("p t (c i) -> p c t i", i=4)

@@ -4,8 +4,6 @@ import concourse.mybir as mybir
 from concourse.masks import make_identity
 
 K, T, S, V, N, D = 512, 4096, 1024, 512, 512, 3
-P = 128
-PACK = 4
 FLOPS = 2 * K * N * S
 
 F32 = mybir.dt.float32
@@ -18,10 +16,18 @@ FP8X4 = mybir.dt.float8_e4m3fn_x4
 ACT = mybir.ActivationFunctionType
 MULT, ADD = mybir.AluOpType.mult, mybir.AluOpType.add
 
+P = 128
+PACK = 4
+GROUP = 16
+QUADRANT = 32
+SCALE_ROWS = 4
+BLOCKS = K // 32
+CHUNKS = V // P
+DIRECT = CHUNKS - 1
 HALF = S // 2
-FUSED = 1
-WIDTHS = [128,128,128,64,64]
-VECTOR_EVAC = [[1,1]]
+SCALAR_TILE = PACK - 1
+PRODUCTS = [(0, 0), (0, 3), (0, 1), (1, 0), (1, 1), (0, 2), (1, 2), (1, 3)]
+SUM_BANKS = [7, 0, 4]
 
 
 def tile_picked_ysplat_sigmoid_po_kernel(
@@ -30,105 +36,96 @@ def tile_picked_ysplat_sigmoid_po_kernel(
     nc = tc.nc
     with ExitStack() as ctx:
         keep = ctx.enter_context(tc.tile_pool(name="keep", bufs=1))
-        ring = ctx.enter_context(tc.tile_pool(name="ring", bufs=4))
+        ring = ctx.enter_context(tc.tile_pool(name="ring", bufs=CHUNKS))
         psum = ctx.enter_context(tc.psum_pool(name="psum", bufs=1))
 
         def bank(number):
             return psum.tile([P, 4, P], F32, name=f"bank{number}")
 
-        pos = [keep.tile([P, V // 16], U16, name=f"pos{d}") for d in range(D)]
-        picks = keep.tile([P, S // 16], U16, name="picks")
+        def pixels(c):
+            return slice(c * P, (c + 1) * P)
+
+        pos = [keep.tile([P, V // GROUP], U16, name=f"pos{d}") for d in range(D)]
+        picks = keep.tile([P, S // GROUP], U16, name="picks")
         w_raw = keep.tile([P, PACK, N], F32, name="w_raw")
         x_table = keep.tile([P, T], I32, name="x_table")
         scale_table = keep.tile([P, T], U8, name="scale_table")
         op_table = keep.tile([P, S], F32, name="op_table")
         fall_rows = keep.tile([P, V], F32, name="fall_rows")
         ident = keep.tile([P, P], F32, name="ident")
-        warm = keep.tile([P, 2], F32, name="warm")
         x_scale_rows = keep.tile([P, S], U8, name="x_scale_rows")
         x_scale = keep.tile([P, S], U8, name="x_scale", align_bytes=64)
 
-        nc.sync.dma_start(picks[:], offs)
-        nc.sync.dma_start(scale_table[P - 16 :, :].bitcast(I32), x_scales[0].bitcast(I32))
-        nc.scalar.dma_start(op_table[P - 1 :, :], op[0:1, :])
         nc.sync.dma_start(pos[0][:], pos1)
+        nc.scalar.dma_start(op_table[P - 1 :, :], op[0:1, :])
+        nc.sync.dma_start(picks[:], offs)
+        nc.sync.dma_start(scale_table[P - BLOCKS :, :].bitcast(I32), x_scales[0].bitcast(I32))
         nc.scalar.dma_start(fall_rows[P - D :, :], fall[:, 0, :])
         nc.sync.dma_start(pos[1][:], pos2)
         nc.sync.dma_start(pos[2][:], pos3)
         nc.sync.dma_start(w_raw[:], w1.rearrange("(p j) c -> p j c", j=PACK))
-        nc.sync.dma_start(x_table[:], x_words[0].rearrange("p n t -> p (n t)").bitcast(I32))
+        nc.sync.dma_start(x_table[:], x_words[0].rearrange("p n j -> p (n j)").bitcast(I32))
 
-        nc.vector.memset(scale_table[: P - 16, :].bitcast(I32), 0)
         nc.vector.memset(op_table[: P - 1, :], 0.0)
+        nc.vector.memset(scale_table[: P - BLOCKS, :].bitcast(I32), 0)
         nc.vector.memset(x_scale[:].bitcast(I32), 0)
         nc.gpsimd.memset(fall_rows[: P - D, :], 0.0)
         make_identity(nc, ident[:])
-        nc.scalar.activation(warm[:, 0:1], ident[:, 0:1], ACT.Sigmoid)
-
-        nc.vector.tensor_copy(x_scale_rows[:], scale_table[:].indirect(picks[:]))
-        for q in range(4):
-            nc.sync.dma_start(
-                x_scale[32 * q : 32 * q + 4, :].bitcast(I32),
-                x_scale_rows[P - 16 + 4 * q : P - 12 + 4 * q, :].bitcast(I32),
-            )
 
         op_rows = [keep.tile([P, V], F32, name=f"op_rows{d}") for d in range(D)]
-        for d in range(D):
+        nc.vector.tensor_copy(op_rows[0][:], op_table[:].indirect(pos[0][:]))
+
+        nc.vector.tensor_copy(x_scale_rows[:], scale_table[:].indirect(picks[:]))
+        for q in range(P // QUADRANT):
+            first_row = P - BLOCKS + SCALE_ROWS * q
+            nc.sync.dma_start(
+                x_scale[QUADRANT * q : QUADRANT * q + SCALE_ROWS, :].bitcast(I32),
+                x_scale_rows[first_row : first_row + SCALE_ROWS, :].bitcast(I32),
+            )
+
+        for d in range(1, D):
             nc.vector.tensor_copy(op_rows[d][:], op_table[:].indirect(pos[d][:]))
 
-        fall_cols = keep.tile([P, D, 4], F32, name="fall_cols")
-        turned = bank(0)
-        for c in range(4):
-            nc.tensor.transpose(turned[:, c, :], fall_rows[:, c * P : (c + 1) * P], ident[:])
-        nc.scalar.copy(fall_cols[:], turned[:, :, P - D :].rearrange("p c d -> p d c"))
+        fall_cols = keep.tile([P, D, CHUNKS], F32, name="fall_cols")
+        fall_turned = bank(0)
+        for c in range(CHUNKS):
+            nc.tensor.transpose(fall_turned[:, c, :], fall_rows[:, pixels(c)], ident[:])
+        nc.scalar.copy(fall_cols[:], fall_turned[:, :, P - D :].rearrange("p c d -> p d c"))
 
         w_bf = keep.tile([P, PACK, P, PACK], BF16, name="w_bf", align_bytes=64)
         w_codes = keep.tile([P, N], U32, name="w_codes", align_bytes=64)
         w_scales = keep.tile([P, N], U8, name="w_scales", align_bytes=64)
-        nc.scalar.copy(
-            w_bf[:].rearrange("p t m j -> p m j t"), w_raw[:].rearrange("p j (m t) -> p m j t", t=PACK)
-        )
+        nc.scalar.copy(w_bf[:].rearrange("p t m j -> p m j t"), w_raw[:].rearrange("p j (m t) -> p m j t", t=PACK))
 
-        seen = keep.tile([P, D, 4], F32, name="seen")
-        through = keep.tile([P, 2, 4], F32, name="through")
-        weight_cols = keep.tile([P, D, 4], F32, name="weight_cols")
-        weights = keep.tile([P, D, V], F32, name="weights")
-
-        def weight_column(d):
-            turned = bank(1 + d)
-            for c in range(4):
-                nc.tensor.transpose(turned[:, c, :], op_rows[d][:, c * P : (c + 1) * P], ident[:])
+        seen = keep.tile([P, D, CHUNKS], F32, name="seen")
+        through = keep.tile([P, D - 1, CHUNKS], F32, name="through")
+        weight_cols = keep.tile([P, D, CHUNKS], F32, name="weight_cols")
+        for d in range(D):
+            op_turned = bank(1 + d)
+            for c in range(CHUNKS):
+                nc.tensor.transpose(op_turned[:, c, :], op_rows[d][:, pixels(c)], ident[:])
             factor = fall_cols if d == 0 else seen
-            for c in range(4):
+            for c in range(CHUNKS):
                 nc.scalar.activation(
-                    weight_cols[:, d, c : c + 1], turned[:, c, P - 1 :], ACT.Copy, scale=factor[:, d, c : c + 1]
+                    weight_cols[:, d, c : c + 1], op_turned[:, c, P - 1 :], ACT.Copy, scale=factor[:, d, c : c + 1]
                 )
-
-        def see_through(d):
+            if d == D - 1:
+                break
             if d == 0:
                 nc.scalar.activation(through[:, 0, :], weight_cols[:, 0, :], ACT.Copy, scale=-1.0, bias=1.0)
-            for c in range(4):
-                if d == 1:
+            else:
+                for c in range(CHUNKS):
                     nc.scalar.activation(
-                        through[:, 1, c : c + 1], weight_cols[:, 1, c : c + 1], ACT.Identity,
-                        scale=-1.0, bias=through[:, 0, c : c + 1],
+                        through[:, d, c : c + 1],
+                        weight_cols[:, d, c : c + 1],
+                        ACT.Identity,
+                        scale=-1.0,
+                        bias=through[:, d - 1, c : c + 1],
                     )
-            for c in range(4):
+            for c in range(CHUNKS):
                 nc.scalar.activation(
                     seen[:, d + 1, c : c + 1], fall_cols[:, d + 1, c : c + 1], ACT.Copy, scale=through[:, d, c : c + 1]
                 )
-
-        def spread_weight(d, number):
-            spread = bank(number)
-            for c in range(4):
-                nc.tensor.transpose(spread[:, c, :], weight_cols[:, d, c : c + 1].to_broadcast([P, P]), ident[:])
-            nc.scalar.copy(weights[:, d, :], spread[:].rearrange("p c n -> p (c n)"))
-
-        for d in range(D):
-            weight_column(d)
-            if d + 1 < D:
-                see_through(d)
-                spread_weight(d, 4 + d)
 
         nc.vector.quantize_mx(
             out=w_codes[:].bitcast(FP8X4), scales=w_scales[:], in_=w_bf[:].rearrange("p t m j -> p (t m j)")
@@ -136,69 +133,163 @@ def tile_picked_ysplat_sigmoid_po_kernel(
 
         x_codes = [keep.tile([P, HALF], U32, name=f"x_codes{h}", align_bytes=64) for h in range(2)]
         for h in range(2):
-            nc.vector.tensor_copy(
-                x_codes[h][:], x_table[:].bitcast(U32).indirect(picks[:, h * HALF // 16 : (h + 1) * HALF // 16])
-            )
+            entries = picks[:, h * HALF // GROUP : (h + 1) * HALF // GROUP]
+            nc.vector.tensor_copy(x_codes[h][:], x_table[:].bitcast(U32).indirect(entries))
 
         rows = [keep.tile([P, S], F32, name=f"rows{t}") for t in range(PACK)]
-        for h, t in [(0, 0), (0, 1), (1, 0), (1, 1), (0, 2), (1, 2), (0, 3), (1, 3)]:
+        for number, (h, t) in enumerate(PRODUCTS):
             cols = slice(h * HALF, (h + 1) * HALF)
-            if True:
-                acc = bank(t if h == 0 else 4 + (t + 2) % 4)[:].rearrange("p c n -> p (c n)")
-                nc.tensor.matmul_mx(
-                    out=acc,
-                    lhsT=w_codes[:, t * P : (t + 1) * P].bitcast(FP8X4),
-                    lhsT_scale=w_scales[:, t * P : (t + 1) * P],
-                    rhs=x_codes[h][:].bitcast(FP8X4),
-                    rhs_scale=x_scale[:, cols],
-                    start=True,
-                    stop=True,
-                )
-                if t < FUSED:
-                    nc.scalar.activation(rows[t][:, cols], acc, ACT.Sigmoid)
-                elif [h, t] in VECTOR_EVAC:
-                    nc.vector.tensor_copy(rows[t][:, cols], acc)
-                else:
-                    nc.scalar.copy(rows[t][:, cols], acc)
-        spread_weight(D - 1, 0)
+            acc = bank(number)[:].rearrange("p c n -> p (c n)")
+            nc.tensor.matmul_mx(
+                out=acc,
+                lhsT=w_codes[:, t * P : (t + 1) * P].bitcast(FP8X4),
+                lhsT_scale=w_scales[:, t * P : (t + 1) * P],
+                rhs=x_codes[h][:].bitcast(FP8X4),
+                rhs_scale=x_scale[:, cols],
+                start=True,
+                stop=True,
+            )
+            if t != SCALAR_TILE:
+                nc.scalar.activation(rows[t][:, cols], acc, ACT.Sigmoid)
+            elif h == 0:
+                nc.vector.tensor_copy(rows[t][:, cols], acc)
+            else:
+                nc.scalar.copy(rows[t][:, cols], acc)
+
+        direct_weights = keep.tile([P, D, P], F32, name="direct_weights")
+        spread = bank(0)
+        for d in range(D):
+            column = weight_cols[:, d, DIRECT : DIRECT + 1]
+            nc.tensor.transpose(spread[:, d, :], column.to_broadcast([P, P]), ident[:])
+        nc.scalar.copy(direct_weights[:], spread[:, 0:D, :])
 
         y_codes = keep.tile([P, V], U32, name="y_codes", align_bytes=64)
         y_scales = keep.tile([P, V], U8, name="y_scales", align_bytes=64)
         out_rows = out_0.rearrange("(p t) v -> p t v", t=PACK)
-        out_words = out_1[0].rearrange("p n t -> p (n t)").bitcast(I32)
-        terms = [keep.tile([P, PACK, V], F32, name=f"terms{d}") for d in range(D)]
-        for t in range(FUSED):
+        out_words = out_1[0].rearrange("p n j -> p (n j)").bitcast(I32)
+
+        fetched = {}
+
+        def offsets(d, c):
+            return pos[d][:, c * P // GROUP : (c + 1) * P // GROUP]
+
+        def fetch_on_vector(c):
+            for t in range(SCALAR_TILE):
+                for d in range(D):
+                    nc.vector.tensor_copy(fetched[c, d, t], rows[t][:].indirect(offsets(d, c)))
+
+        def fetch_on_scalar(c):
+            values = keep.tile([P, D, P], F32, name=f"from_scalar{c}", tag=f"from_scalar{c % 2}")
             for d in range(D):
-                nc.vector.tensor_tensor(terms[d][:, t, :], rows[t][:].indirect(pos[d][:]), weights[:, d, :], MULT)
-        v0 = 0
-        for width in WIDTHS:
-            vs = slice(v0, v0 + width)
-            y = ring.tile([P, PACK, width], F32, name="y")
-            y_bf = ring.tile([P, width, PACK], BF16, name="y_bf", align_bytes=64)
+                fetched[c, d, SCALAR_TILE] = values[:, d, :]
+                nc.scalar.activation(values[:, d, :], rows[SCALAR_TILE][:].indirect(offsets(d, c)), ACT.Sigmoid)
+            return values
+
+        def turn(c):
+            banks = [bank(1 + D * (c % 2) + d) for d in range(D)]
+            for t in range(PACK):
+                for d in range(D):
+                    nc.tensor.transpose(banks[d][:, t, :], fetched[c, d, t], ident[:])
+            return banks
+
+        def weigh(c, banks):
+            scaled = [keep.tile([P, PACK, P], F32, name=f"scaled{c}{d}") for d in range(D)]
             for d in range(D):
-                offsets = pos[d][:, v0 // 16 : (v0 + width) // 16]
-                for t in range(FUSED, PACK):
-                    nc.scalar.activation(terms[d][:, t, vs], rows[t][:].indirect(offsets), ACT.Sigmoid)
-                if d == 2:
-                    nc.vector.tensor_tensor(y[:], terms[0][:, :, vs], terms[1][:, :, vs], ADD)
-                nc.vector.tensor_tensor(
-                    terms[d][:, FUSED:, vs],
-                    terms[d][:, FUSED:, vs],
-                    weights[:, d : d + 1, vs].to_broadcast([P, PACK - FUSED, width]),
-                    MULT,
-                )
-            nc.vector.tensor_tensor(y[:], y[:], terms[2][:, :, vs], ADD)
-            nc.sync.dma_start(out_rows[:, :, vs], y[:])
+                nc.scalar.activation(scaled[d][:], banks[d][:], ACT.Copy, scale=weight_cols[:, d, c : c + 1])
+            return scaled
+
+        def turn_back(c, scaled):
+            total = bank(SUM_BANKS[c])
+            for d in range(D):
+                for t in range(PACK):
+                    nc.tensor.matmul(
+                        total[:, t, :],
+                        lhsT=scaled[d][:, t, :],
+                        rhs=ident[:],
+                        is_transpose=True,
+                        start=(d == 0 and t == 0),
+                        stop=(d == D - 1 and t == PACK - 1),
+                    )
+            return total
+
+        def sum_directly(c, from_scalar, products, y):
+            for d in range(D):
+                for t in range(SCALAR_TILE):
+                    nc.vector.tensor_tensor(
+                        products[:, d, t, :], rows[t][:].indirect(offsets(d, c)), direct_weights[:, d, :], MULT
+                    )
+            nc.vector.tensor_tensor(products[:, :, SCALAR_TILE, :], from_scalar[:], direct_weights[:], MULT)
+            nc.vector.tensor_tensor(y, products[:, 0, :, :], products[:, 1, :, :], ADD)
+            nc.vector.tensor_tensor(y, y, products[:, 2, :, :], ADD)
+
+        def round_on_vector(y):
+            y_bf = ring.tile([P, P, PACK], BF16, name="y_bf", align_bytes=64)
             nc.vector.tensor_copy(
-                y_bf[:].rearrange("p (c i) t -> p c t i", i=4), y[:].rearrange("p t (c i) -> p c t i", i=4)
+                y_bf[:].rearrange("p (c i) t -> p c t i", i=4), y.rearrange("p t (c i) -> p c t i", i=4)
             )
+            return y_bf
+
+        def quantise(c, y_bf):
             nc.vector.quantize_mx(
-                out=y_codes[:, vs].bitcast(FP8X4), scales=y_scales[:, vs], in_=y_bf[:].rearrange("p v t -> p (v t)")
+                out=y_codes[:, pixels(c)].bitcast(FP8X4),
+                scales=y_scales[:, pixels(c)],
+                in_=y_bf[:].rearrange("p v t -> p (v t)"),
             )
-            nc.sync.dma_start(out_words[:, vs], y_codes[:, vs].bitcast(I32))
-            v0 += width
-        for q in range(4):
+
+        first = keep.tile([P, D, PACK, P], F32, name="first")
+        tags = ["middle", "products", "held"]
+        held = [keep.tile([P, P], F32, name=f"held{d}", tag=tags[d]) for d in range(D)]
+        for d in range(D):
+            for t in range(SCALAR_TILE):
+                fetched[0, d, t] = held[d][:] if t == SCALAR_TILE - 1 else first[:, d, t, :]
+        fetch_on_vector(0)
+        fetch_on_scalar(0)
+        banks0 = turn(0)
+
+        middle = keep.tile([P, D, PACK, 2 * P], F32, name="middle", tag="middle")
+        products = keep.tile([P, D, PACK, P], F32, name="products", tag="products")
+        for c in (1, 2):
+            for d in range(D):
+                for t in range(SCALAR_TILE):
+                    fetched[c, d, t] = middle[:, d, t, pixels(c - 1)]
+
+        fetch_on_vector(1)
+        fetch_on_scalar(1)
+        banks1 = turn(1)
+        scaled0 = weigh(0, banks0)
+        fetch_on_vector(2)
+        fetch_on_scalar(2)
+        total0 = turn_back(0, scaled0)
+        y0 = keep.tile([P, PACK, P], F32, name="y0")
+        nc.scalar.copy(y0[:], total0[:])
+        banks2 = turn(2)
+        nc.sync.dma_start(out_rows[:, :, pixels(0)], y0[:])
+        quantise(0, round_on_vector(y0[:]))
+
+        total1 = turn_back(1, weigh(1, banks1))
+        y23 = keep.tile([P, PACK, 2 * P], F32, name="y23", tag="scaled12")
+        y2, y3 = y23[:, :, 0:P], y23[:, :, P : 2 * P]
+        from_scalar3 = fetch_on_scalar(DIRECT)
+        scaled2 = weigh(2, banks2)
+        y1 = keep.tile([P, PACK, P], F32, name="y1")
+        nc.scalar.copy(y1[:], total1[:])
+        sum_directly(DIRECT, from_scalar3, products, y3)
+        nc.sync.dma_start(out_rows[:, :, pixels(1)], y1[:])
+        quantise(1, round_on_vector(y1[:]))
+
+        total2 = turn_back(2, scaled2)
+        nc.scalar.copy(y2, total2[:])
+        y2_bf = ring.tile([P, P, PACK], BF16, name="y_bf", align_bytes=64)
+        nc.scalar.copy(y2_bf[:], total2[:].rearrange("p t v -> p v t"))
+        quantise(DIRECT, round_on_vector(y3))
+        nc.sync.dma_start(out_rows[:, :, 2 * P :], y23[:])
+        quantise(2, y2_bf)
+
+        for half in (slice(0, V // 2), slice(V // 2, V)):
+            nc.sync.dma_start(out_words[:, half], y_codes[:, half].bitcast(I32))
+        for q in range(P // QUADRANT):
             queue = nc.scalar if q % 2 else nc.sync
             queue.dma_start(
-                out_2[0, 4 * q : 4 * q + 4, :].bitcast(I32), y_scales[32 * q : 32 * q + 4, :].bitcast(I32)
+                out_2[0, SCALE_ROWS * q : SCALE_ROWS * (q + 1), :].bitcast(I32),
+                y_scales[QUADRANT * q : QUADRANT * q + SCALE_ROWS, :].bitcast(I32),
             )

@@ -26,8 +26,7 @@ CHUNKS = V // P
 DIRECT = CHUNKS - 1
 HALF = S // 2
 SCALAR_TILE = PACK - 1
-PRODUCTS = [(0, 0), (0, 3), (0, 1), (1, 0), (1, 1), (0, 2), (1, 2), (1, 3)]
-SUM_BANKS = [7, 0, 4]
+PRODUCTS = [(0, 0), (0, 3), (1, 0), (1, 3), (0, 1), (1, 1), (0, 2), (1, 2)]
 
 
 def tile_picked_ysplat_sigmoid_po_kernel(
@@ -36,7 +35,6 @@ def tile_picked_ysplat_sigmoid_po_kernel(
     nc = tc.nc
     with ExitStack() as ctx:
         keep = ctx.enter_context(tc.tile_pool(name="keep", bufs=1))
-        ring = ctx.enter_context(tc.tile_pool(name="ring", bufs=CHUNKS))
         psum = ctx.enter_context(tc.psum_pool(name="psum", bufs=1))
 
         def bank(number):
@@ -50,31 +48,41 @@ def tile_picked_ysplat_sigmoid_po_kernel(
         w_raw = keep.tile([P, PACK, N], F32, name="w_raw")
         x_table = keep.tile([P, T], I32, name="x_table")
         scale_table = keep.tile([P, T], U8, name="scale_table")
-        op_table = keep.tile([P, S], F32, name="op_table")
-        fall_rows = keep.tile([P, V], F32, name="fall_rows")
+        op_table = keep.tile([P, S], F32, name="op_table", align_bytes=64)
+        fall_rows = keep.tile([P, D * V], F32, name="fall_rows")
         ident = keep.tile([P, P], F32, name="ident")
         x_scale_rows = keep.tile([P, S], U8, name="x_scale_rows")
         x_scale = keep.tile([P, S], U8, name="x_scale", align_bytes=64)
 
         nc.sync.dma_start(pos[0][:], pos1)
-        nc.scalar.dma_start(op_table[P - 1 :, :], op[0:1, :])
+        nc.sync.dma_start(op_table[P - 1 :, :], op[0:1, :])
+        nc.sync.dma_start(fall_rows[P - 1 :, 0:V], fall[0, 0:1, :])
         nc.sync.dma_start(picks[:], offs)
         nc.sync.dma_start(scale_table[P - BLOCKS :, :].bitcast(I32), x_scales[0].bitcast(I32))
-        nc.scalar.dma_start(fall_rows[P - D :, :], fall[:, 0, :])
+        nc.sync.dma_start(w_raw[:], w1.rearrange("(p j) c -> p j c", j=PACK))
         nc.sync.dma_start(pos[1][:], pos2)
         nc.sync.dma_start(pos[2][:], pos3)
-        nc.sync.dma_start(w_raw[:], w1.rearrange("(p j) c -> p j c", j=PACK))
+        nc.sync.dma_start(
+            fall_rows[P - 1 :, V:].rearrange("p (d v) -> p d v", d=D - 1), fall[1:, 0:1, :].rearrange("d p v -> p d v")
+        )
         nc.sync.dma_start(x_table[:], x_words[0].rearrange("p n j -> p (n j)").bitcast(I32))
 
         nc.vector.memset(op_table[: P - 1, :], 0.0)
         nc.vector.memset(scale_table[: P - BLOCKS, :].bitcast(I32), 0)
         nc.vector.memset(x_scale[:].bitcast(I32), 0)
-        nc.gpsimd.memset(fall_rows[: P - D, :], 0.0)
-        make_identity(nc, ident[:])
+        for d in range(D):
+            nc.gpsimd.memset(fall_rows[: P - 1, d * V : (d + 1) * V], 0.0)
+            if d == 0:
+                make_identity(nc, ident[:])
 
-        op_rows = [keep.tile([P, V], F32, name=f"op_rows{d}") for d in range(D)]
-        nc.vector.tensor_copy(op_rows[0][:], op_table[:].indirect(pos[0][:]))
+        alpha_rows = [keep.tile([P, V], F32, name=f"alpha_rows{d}", align_bytes=64) for d in range(D)]
 
+        def look_up_alpha(d):
+            nc.vector.tensor_tensor(
+                alpha_rows[d][:], op_table[:].indirect(pos[d][:]), fall_rows[:, d * V : (d + 1) * V], MULT
+            )
+
+        look_up_alpha(0)
         nc.vector.tensor_copy(x_scale_rows[:], scale_table[:].indirect(picks[:]))
         for q in range(P // QUADRANT):
             first_row = P - BLOCKS + SCALE_ROWS * q
@@ -82,59 +90,57 @@ def tile_picked_ysplat_sigmoid_po_kernel(
                 x_scale[QUADRANT * q : QUADRANT * q + SCALE_ROWS, :].bitcast(I32),
                 x_scale_rows[first_row : first_row + SCALE_ROWS, :].bitcast(I32),
             )
-
         for d in range(1, D):
-            nc.vector.tensor_copy(op_rows[d][:], op_table[:].indirect(pos[d][:]))
+            look_up_alpha(d)
 
-        fall_cols = keep.tile([P, D, CHUNKS], F32, name="fall_cols")
-        fall_turned = bank(0)
-        for c in range(CHUNKS):
-            nc.tensor.transpose(fall_turned[:, c, :], fall_rows[:, pixels(c)], ident[:])
-        nc.scalar.copy(fall_cols[:], fall_turned[:, :, P - D :].rearrange("p c d -> p d c"))
-
-        w_bf = keep.tile([P, PACK, P, PACK], BF16, name="w_bf", align_bytes=64)
-        w_codes = keep.tile([P, N], U32, name="w_codes", align_bytes=64)
-        w_scales = keep.tile([P, N], U8, name="w_scales", align_bytes=64)
-        nc.scalar.copy(w_bf[:].rearrange("p t m j -> p m j t"), w_raw[:].rearrange("p j (m t) -> p m j t", t=PACK))
-
-        seen = keep.tile([P, D, CHUNKS], F32, name="seen")
         through = keep.tile([P, D - 1, CHUNKS], F32, name="through")
-        weight_cols = keep.tile([P, D, CHUNKS], F32, name="weight_cols")
+        front_cols = keep.tile([P, CHUNKS], F32, name="front_cols")
+        back_cols = keep.tile([P, D - 1, CHUNKS], F32, name="back_cols", tag="w_raw")
+        weight_cols = [front_cols[:]] + [back_cols[:, d, :] for d in range(D - 1)]
+        weight_rows = keep.tile([P, D, V], F32, name="weight_rows")
         for d in range(D):
-            op_turned = bank(1 + d)
+            turned = bank(4)
             for c in range(CHUNKS):
-                nc.tensor.transpose(op_turned[:, c, :], op_rows[d][:, pixels(c)], ident[:])
-            factor = fall_cols if d == 0 else seen
-            for c in range(CHUNKS):
-                nc.scalar.activation(
-                    weight_cols[:, d, c : c + 1], op_turned[:, c, P - 1 :], ACT.Copy, scale=factor[:, d, c : c + 1]
-                )
-            if d == D - 1:
-                break
+                nc.tensor.transpose(turned[:, c, :], alpha_rows[d][:, pixels(c)], ident[:])
+            alpha = turned[:, :, P - 1]
             if d == 0:
-                nc.scalar.activation(through[:, 0, :], weight_cols[:, 0, :], ACT.Copy, scale=-1.0, bias=1.0)
+                nc.scalar.copy(weight_cols[0], alpha)
+                nc.scalar.activation(through[:, 0, :], alpha, ACT.Copy, scale=-1.0, bias=1.0)
             else:
                 for c in range(CHUNKS):
                     nc.scalar.activation(
-                        through[:, d, c : c + 1],
-                        weight_cols[:, d, c : c + 1],
+                        weight_cols[d][:, c : c + 1], alpha[:, c : c + 1], ACT.Copy, scale=through[:, d - 1, c : c + 1]
+                    )
+            spread = bank(5 + d)
+            for c in range(CHUNKS):
+                nc.tensor.transpose(spread[:, c, :], weight_cols[d][:, c : c + 1].to_broadcast([P, P]), ident[:])
+            if d == 0:
+                w_bf = keep.tile([P, PACK, P, PACK], BF16, name="w_bf", tag="alpha_rows0", align_bytes=64)
+                nc.scalar.copy(
+                    w_bf[:].rearrange("p t m j -> p m j t"), w_raw[:].rearrange("p j (m t) -> p m j t", t=PACK)
+                )
+            if d == 1:
+                for c in range(CHUNKS):
+                    nc.scalar.activation(
+                        through[:, 1, c : c + 1],
+                        weight_cols[1][:, c : c + 1],
                         ACT.Identity,
                         scale=-1.0,
-                        bias=through[:, d - 1, c : c + 1],
+                        bias=through[:, 0, c : c + 1],
                     )
-            for c in range(CHUNKS):
-                nc.scalar.activation(
-                    seen[:, d + 1, c : c + 1], fall_cols[:, d + 1, c : c + 1], ACT.Copy, scale=through[:, d, c : c + 1]
-                )
+            nc.scalar.copy(weight_rows[:, d, :], spread[:].rearrange("p c v -> p (c v)"))
 
+        w_codes = keep.tile([P, N], U32, name="w_codes", tag="op_table", align_bytes=64)
+        w_scales = keep.tile([P, N], U8, name="w_scales", align_bytes=64)
         nc.vector.quantize_mx(
             out=w_codes[:].bitcast(FP8X4), scales=w_scales[:], in_=w_bf[:].rearrange("p t m j -> p (t m j)")
         )
 
-        x_codes = [keep.tile([P, HALF], U32, name=f"x_codes{h}", align_bytes=64) for h in range(2)]
+        x_words_picked = keep.tile([P, S], U32, name="x_words_picked", tag="alpha_rows0", align_bytes=64)
+        x_codes = [x_words_picked[:, h * HALF : (h + 1) * HALF] for h in range(2)]
         for h in range(2):
             entries = picks[:, h * HALF // GROUP : (h + 1) * HALF // GROUP]
-            nc.vector.tensor_copy(x_codes[h][:], x_table[:].bitcast(U32).indirect(entries))
+            nc.vector.tensor_copy(x_codes[h], x_table[:].bitcast(U32).indirect(entries))
 
         rows = [keep.tile([P, S], F32, name=f"rows{t}") for t in range(PACK)]
         for number, (h, t) in enumerate(PRODUCTS):
@@ -144,86 +150,98 @@ def tile_picked_ysplat_sigmoid_po_kernel(
                 out=acc,
                 lhsT=w_codes[:, t * P : (t + 1) * P].bitcast(FP8X4),
                 lhsT_scale=w_scales[:, t * P : (t + 1) * P],
-                rhs=x_codes[h][:].bitcast(FP8X4),
+                rhs=x_codes[h].bitcast(FP8X4),
                 rhs_scale=x_scale[:, cols],
                 start=True,
                 stop=True,
             )
             if t != SCALAR_TILE:
                 nc.scalar.activation(rows[t][:, cols], acc, ACT.Sigmoid)
-            elif h == 0:
-                nc.vector.tensor_copy(rows[t][:, cols], acc)
             else:
-                nc.scalar.copy(rows[t][:, cols], acc)
-
-        direct_weights = keep.tile([P, D, P], F32, name="direct_weights")
-        spread = bank(0)
-        for d in range(D):
-            column = weight_cols[:, d, DIRECT : DIRECT + 1]
-            nc.tensor.transpose(spread[:, d, :], column.to_broadcast([P, P]), ident[:])
-        nc.scalar.copy(direct_weights[:], spread[:, 0:D, :])
+                nc.vector.tensor_copy(rows[t][:, cols], acc)
 
         y_codes = keep.tile([P, V], U32, name="y_codes", align_bytes=64)
         y_scales = keep.tile([P, V], U8, name="y_scales", align_bytes=64)
         out_rows = out_0.rearrange("(p t) v -> p t v", t=PACK)
         out_words = out_1[0].rearrange("p n j -> p (n j)").bitcast(I32)
 
-        fetched = {}
-
         def offsets(d, c):
             return pos[d][:, c * P // GROUP : (c + 1) * P // GROUP]
 
+        turned_pixels = DIRECT * P
+        whole = keep.tile([P, D, turned_pixels], F32, name="whole")
+        for d in range(D):
+            entries = pos[d][:, 0 : turned_pixels // GROUP]
+            nc.vector.tensor_tensor(whole[:, d, :], rows[0][:].indirect(entries), weight_rows[:, d, 0:turned_pixels], MULT)
+        weighed = {(0, c): whole[:, :, pixels(c)] for c in range(DIRECT)}
+
         def fetch_on_vector(c):
-            for t in range(SCALAR_TILE):
+            for t in range(0 if c == DIRECT else 1, SCALAR_TILE):
                 for d in range(D):
-                    nc.vector.tensor_copy(fetched[c, d, t], rows[t][:].indirect(offsets(d, c)))
+                    nc.vector.tensor_tensor(
+                        weighed[t, c][:, d, :], rows[t][:].indirect(offsets(d, c)), weight_rows[:, d, pixels(c)], MULT
+                    )
 
         def fetch_on_scalar(c):
-            values = keep.tile([P, D, P], F32, name=f"from_scalar{c}", tag=f"from_scalar{c % 2}")
+            values = keep.tile([P, D, P], F32, name=f"from_scalar{c}")
             for d in range(D):
-                fetched[c, d, SCALAR_TILE] = values[:, d, :]
                 nc.scalar.activation(values[:, d, :], rows[SCALAR_TILE][:].indirect(offsets(d, c)), ACT.Sigmoid)
             return values
 
-        def turn(c):
-            banks = [bank(1 + D * (c % 2) + d) for d in range(D)]
-            for t in range(PACK):
-                for d in range(D):
-                    nc.tensor.transpose(banks[d][:, t, :], fetched[c, d, t], ident[:])
-            return banks
+        def add_turned(total, parts):
+            for i, (quarter, values) in enumerate(parts):
+                nc.tensor.matmul(
+                    total[:, quarter, :],
+                    lhsT=values,
+                    rhs=ident[:],
+                    is_transpose=True,
+                    start=(i == 0),
+                    stop=(i == len(parts) - 1),
+                )
 
-        def weigh(c, banks):
-            scaled = [keep.tile([P, PACK, P], F32, name=f"scaled{c}{d}") for d in range(D)]
+        def turn_scalar(values, number):
+            turned = bank(number)
             for d in range(D):
-                nc.scalar.activation(scaled[d][:], banks[d][:], ACT.Copy, scale=weight_cols[:, d, c : c + 1])
+                nc.tensor.transpose(turned[:, d, :], values[:, d, :], ident[:])
+            return turned
+
+        def weigh(c, turned):
+            scaled = keep.tile([P, D, P], F32, name=f"scaled{c}")
+            for d in range(D):
+                nc.scalar.activation(scaled[:, d, :], turned[:, d, :], ACT.Copy, scale=weight_cols[d][:, c : c + 1])
             return scaled
 
-        def turn_back(c, scaled):
-            total = bank(SUM_BANKS[c])
-            for d in range(D):
-                for t in range(PACK):
-                    nc.tensor.matmul(
-                        total[:, t, :],
-                        lhsT=scaled[d][:, t, :],
-                        rhs=ident[:],
-                        is_transpose=True,
-                        start=(d == 0 and t == 0),
-                        stop=(d == D - 1 and t == PACK - 1),
-                    )
+        def turn_vector(c, number):
+            total = bank(number)
+            add_turned(total, [(t, weighed[t, c][:, d, :]) for t in range(SCALAR_TILE) for d in range(D)])
             return total
 
-        def sum_directly(c, from_scalar, products, y):
-            for d in range(D):
-                for t in range(SCALAR_TILE):
-                    nc.vector.tensor_tensor(
-                        products[:, d, t, :], rows[t][:].indirect(offsets(d, c)), direct_weights[:, d, :], MULT
-                    )
-            nc.vector.tensor_tensor(products[:, :, SCALAR_TILE, :], from_scalar[:], direct_weights[:], MULT)
-            nc.vector.tensor_tensor(y, products[:, 0, :, :], products[:, 1, :, :], ADD)
-            nc.vector.tensor_tensor(y, y, products[:, 2, :, :], ADD)
+        def leave(c, total):
+            sums = keep.tile([P, SCALAR_TILE, P], F32, name=f"sums{c}")
+            nc.scalar.copy(sums[:], total[:, 0:SCALAR_TILE, :])
+            return sums
 
-        def round_on_vector(y):
-            y_bf = ring.tile([P, P, PACK], BF16, name="y_bf", align_bytes=64)
+        def turn_back(sums, scaled, number):
+            total = bank(number)
+            add_turned(
+                total,
+                [(SCALAR_TILE, scaled[:, d, :]) for d in range(D)] + [(t, sums[:, t, :]) for t in range(SCALAR_TILE)],
+            )
+            return total
+
+        def hand_out(c, total, queue):
+            y = keep.tile([P, PACK, P], F32, name=f"y{c}")
+            nc.scalar.copy(y[:], total[:])
+            queue.dma_start(out_rows[:, :, pixels(c)], y[:])
+            return y
+
+        def round_on_scalar(c, total):
+            y_bf = keep.tile([P, P, PACK], BF16, name=f"y_bf{c}", align_bytes=64)
+            nc.scalar.copy(y_bf[:], total[:].rearrange("p t v -> p v t"))
+            return y_bf
+
+        def round_on_vector(c, y):
+            y_bf = keep.tile([P, P, PACK], BF16, name=f"y_bf{c}", align_bytes=64)
             nc.vector.tensor_copy(
                 y_bf[:].rearrange("p (c i) t -> p c t i", i=4), y.rearrange("p t (c i) -> p c t i", i=4)
             )
@@ -236,54 +254,59 @@ def tile_picked_ysplat_sigmoid_po_kernel(
                 in_=y_bf[:].rearrange("p v t -> p (v t)"),
             )
 
-        first = keep.tile([P, D, PACK, P], F32, name="first")
-        tags = ["middle", "products", "held"]
-        held = [keep.tile([P, P], F32, name=f"held{d}", tag=tags[d]) for d in range(D)]
-        for d in range(D):
-            for t in range(SCALAR_TILE):
-                fetched[0, d, t] = held[d][:] if t == SCALAR_TILE - 1 else first[:, d, t, :]
+        first = keep.tile([P, D, P], F32, name="first", tag="tile1")
+        tile2 = keep.tile([P, DIRECT, D, P], F32, name="tile2")
+        weighed[1, 0] = first[:]
+        for c in range(DIRECT):
+            weighed[2, c] = tile2[:, c, :, :]
         fetch_on_vector(0)
-        fetch_on_scalar(0)
-        banks0 = turn(0)
+        values0 = fetch_on_scalar(0)
+        turned0 = turn_scalar(values0, 0)
+        values1 = fetch_on_scalar(1)
+        turned1 = turn_scalar(values1, 1)
+        total0 = turn_vector(0, 7)
 
-        middle = keep.tile([P, D, PACK, 2 * P], F32, name="middle", tag="middle")
-        products = keep.tile([P, D, PACK, P], F32, name="products", tag="products")
-        for c in (1, 2):
-            for d in range(D):
-                for t in range(SCALAR_TILE):
-                    fetched[c, d, t] = middle[:, d, t, pixels(c - 1)]
+        later = keep.tile([P, DIRECT - 1 + PACK, D, P], F32, name="later", tag="tile1")
+        for c in range(1, DIRECT):
+            weighed[1, c] = later[:, c - 1, :, :]
+        direct = later[:, DIRECT - 1 :, :, :]
+        for t in range(PACK):
+            weighed[t, DIRECT] = direct[:, t, :, :]
+        for c in range(1, CHUNKS):
+            fetch_on_vector(c)
 
-        fetch_on_vector(1)
-        fetch_on_scalar(1)
-        banks1 = turn(1)
-        scaled0 = weigh(0, banks0)
-        fetch_on_vector(2)
-        fetch_on_scalar(2)
-        total0 = turn_back(0, scaled0)
-        y0 = keep.tile([P, PACK, P], F32, name="y0")
-        nc.scalar.copy(y0[:], total0[:])
-        banks2 = turn(2)
-        nc.sync.dma_start(out_rows[:, :, pixels(0)], y0[:])
-        quantise(0, round_on_vector(y0[:]))
+        scaled0 = weigh(0, turned0)
+        values2 = fetch_on_scalar(2)
+        sums0 = leave(0, total0)
+        back0 = turn_back(sums0, scaled0, 2)
+        total1 = turn_vector(1, 0)
+        scaled1 = weigh(1, turned1)
+        turned2 = turn_scalar(values2, 3)
+        hand_out(0, back0, nc.sync)
+        y_bf0 = round_on_scalar(0, back0)
+        sums1 = leave(1, total1)
+        back1 = turn_back(sums1, scaled1, 4)
+        total2 = turn_vector(2, 1)
+        values3 = fetch_on_scalar(DIRECT)
+        scaled2 = weigh(2, turned2)
+        y1 = hand_out(1, back1, nc.sync)
+        sums2 = leave(2, total2)
+        back2 = turn_back(sums2, scaled2, 5)
+        y_bf1 = round_on_scalar(1, back1)
+        hand_out(2, back2, nc.scalar)
+        y_bf2 = round_on_scalar(2, back2)
 
-        total1 = turn_back(1, weigh(1, banks1))
-        y23 = keep.tile([P, PACK, 2 * P], F32, name="y23", tag="scaled12")
-        y2, y3 = y23[:, :, 0:P], y23[:, :, P : 2 * P]
-        from_scalar3 = fetch_on_scalar(DIRECT)
-        scaled2 = weigh(2, banks2)
-        y1 = keep.tile([P, PACK, P], F32, name="y1")
-        nc.scalar.copy(y1[:], total1[:])
-        sum_directly(DIRECT, from_scalar3, products, y3)
-        nc.sync.dma_start(out_rows[:, :, pixels(1)], y1[:])
-        quantise(1, round_on_vector(y1[:]))
-
-        total2 = turn_back(2, scaled2)
-        nc.scalar.copy(y2, total2[:])
-        y2_bf = ring.tile([P, P, PACK], BF16, name="y_bf", align_bytes=64)
-        nc.scalar.copy(y2_bf[:], total2[:].rearrange("p t v -> p v t"))
-        quantise(DIRECT, round_on_vector(y3))
-        nc.sync.dma_start(out_rows[:, :, 2 * P :], y23[:])
-        quantise(2, y2_bf)
+        nc.vector.tensor_tensor(direct[:, SCALAR_TILE, :, :], values3[:], weight_rows[:, :, pixels(DIRECT)], MULT)
+        pair = keep.tile([P, PACK, P], F32, name="pair")
+        y3 = keep.tile([P, PACK, P], F32, name="y3", tag="sums2")
+        nc.vector.tensor_tensor(pair[:], direct[:, :, 0, :], direct[:, :, 1, :], ADD)
+        quantise(0, y_bf0)
+        nc.vector.tensor_tensor(y3[:], pair[:], direct[:, :, 2, :], ADD)
+        nc.sync.dma_start(out_rows[:, :, pixels(DIRECT)], y3[:])
+        y_bf3 = round_on_vector(DIRECT, y3[:])
+        quantise(1, y_bf1)
+        quantise(DIRECT, y_bf3)
+        quantise(2, y_bf2)
 
         for half in (slice(0, V // 2), slice(V // 2, V)):
             nc.sync.dma_start(out_words[:, half], y_codes[:, half].bitcast(I32))

@@ -14,7 +14,7 @@ U16 = mybir.dt.uint16
 U8 = mybir.dt.uint8
 FP8X4 = mybir.dt.float8_e4m3fn_x4
 ACT = mybir.ActivationFunctionType
-MULT, ADD = mybir.AluOpType.mult, mybir.AluOpType.add
+MULT, ADD, SUBTRACT = mybir.AluOpType.mult, mybir.AluOpType.add, mybir.AluOpType.subtract
 
 P = 128
 PACK = 4
@@ -24,6 +24,7 @@ SCALE_ROWS = 4
 BLOCKS = K // 32
 CHUNKS = V // P
 DIRECT = CHUNKS - 1
+PAIR = 2 * P
 HALF = S // 2
 SCALAR_TILE = PACK - 1
 PRODUCTS = [(0, 0), (0, 3), (1, 0), (1, 3), (0, 1), (1, 1), (0, 2), (1, 2)]
@@ -35,6 +36,7 @@ def tile_picked_ysplat_sigmoid_po_kernel(
     nc = tc.nc
     with ExitStack() as ctx:
         keep = ctx.enter_context(tc.tile_pool(name="keep", bufs=1))
+        placed = ctx.enter_context(tc.tile_pool(name="placed", bufs=1))
         psum = ctx.enter_context(tc.psum_pool(name="psum", bufs=1))
 
         def bank(number):
@@ -93,50 +95,46 @@ def tile_picked_ysplat_sigmoid_po_kernel(
         for d in range(1, D):
             look_up_alpha(d)
 
-        through = keep.tile([P, D - 1, CHUNKS], F32, name="through")
-        front_cols = keep.tile([P, CHUNKS], F32, name="front_cols")
-        back_cols = keep.tile([P, D - 1, CHUNKS], F32, name="back_cols", tag="w_raw")
-        weight_cols = [front_cols[:]] + [back_cols[:, d, :] for d in range(D - 1)]
+        through = placed.tile([P, D - 1, CHUNKS], F32, name="through", offset=2 * K * PACK, align_bytes=64)
+        weight_cols = keep.tile([P, D, CHUNKS], F32, name="weight_cols")
         weight_rows = keep.tile([P, D, V], F32, name="weight_rows")
-        for d in range(D):
-            turned = bank(4)
+
+        def turn_alpha(d, number):
+            turned = bank(number)
             for c in range(CHUNKS):
                 nc.tensor.transpose(turned[:, c, :], alpha_rows[d][:, pixels(c)], ident[:])
-            alpha = turned[:, :, P - 1]
-            if d == 0:
-                nc.scalar.copy(weight_cols[0], alpha)
-                nc.scalar.activation(through[:, 0, :], alpha, ACT.Copy, scale=-1.0, bias=1.0)
-            else:
-                for c in range(CHUNKS):
-                    nc.scalar.activation(
-                        weight_cols[d][:, c : c + 1], alpha[:, c : c + 1], ACT.Copy, scale=through[:, d - 1, c : c + 1]
-                    )
-            spread = bank(5 + d)
-            for c in range(CHUNKS):
-                nc.tensor.transpose(spread[:, c, :], weight_cols[d][:, c : c + 1].to_broadcast([P, P]), ident[:])
-            if d == 0:
-                w_bf = keep.tile([P, PACK, P, PACK], BF16, name="w_bf", tag="alpha_rows0", align_bytes=64)
-                nc.scalar.copy(
-                    w_bf[:].rearrange("p t m j -> p m j t"), w_raw[:].rearrange("p j (m t) -> p m j t", t=PACK)
-                )
-            if d == 1:
-                for c in range(CHUNKS):
-                    nc.scalar.activation(
-                        through[:, 1, c : c + 1],
-                        weight_cols[1][:, c : c + 1],
-                        ACT.Identity,
-                        scale=-1.0,
-                        bias=through[:, 0, c : c + 1],
-                    )
-            nc.scalar.copy(weight_rows[:, d, :], spread[:].rearrange("p c v -> p (c v)"))
+            return turned[:, :, P - 1]
 
+        def spread(d, number):
+            rows_of = bank(number)
+            for c in range(CHUNKS):
+                nc.tensor.transpose(rows_of[:, c, :], weight_cols[:, d, c : c + 1].to_broadcast([P, P]), ident[:])
+            return rows_of[:].rearrange("p c v -> p (c v)")
+
+        w_bf = placed.tile([P, PACK, P, PACK], BF16, name="w_bf", offset=0, align_bytes=64)
+
+        def round_w(part):
+            nc.scalar.copy(
+                w_bf[:, :, part, :].rearrange("p t m j -> p m j t"),
+                w_raw[:].rearrange("p j (m t) -> p m j t", t=PACK)[:, part, :, :],
+            )
+
+        alpha = [turn_alpha(d, 2 + d) for d in range(D)]
+        round_w(slice(0, P))
+        nc.vector.tensor_copy(weight_cols[:, 0, :], alpha[0])
+        nc.vector.tensor_scalar(through[:, 0, :], alpha[0], -1.0, 1.0, MULT, ADD)
+        nc.vector.tensor_tensor(weight_cols[:, 1, :], alpha[1], through[:, 0, :], MULT)
+        nc.vector.tensor_tensor(through[:, 1, :], through[:, 0, :], weight_cols[:, 1, :], SUBTRACT)
         w_codes = keep.tile([P, N], U32, name="w_codes", tag="op_table", align_bytes=64)
         w_scales = keep.tile([P, N], U8, name="w_scales", align_bytes=64)
         nc.vector.quantize_mx(
             out=w_codes[:].bitcast(FP8X4), scales=w_scales[:], in_=w_bf[:].rearrange("p t m j -> p (t m j)")
         )
+        nc.vector.tensor_tensor(weight_cols[:, 2, :], alpha[2], through[:, 1, :], MULT)
+        for d in range(D):
+            nc.scalar.copy(weight_rows[:, d, :], spread(d, 5 + d))
 
-        x_words_picked = keep.tile([P, S], U32, name="x_words_picked", tag="alpha_rows0", align_bytes=64)
+        x_words_picked = placed.tile([P, S], U32, name="x_words_picked", offset=64, align_bytes=64)
         x_codes = [x_words_picked[:, h * HALF : (h + 1) * HALF] for h in range(2)]
         for h in range(2):
             entries = picks[:, h * HALF // GROUP : (h + 1) * HALF // GROUP]
@@ -165,27 +163,26 @@ def tile_picked_ysplat_sigmoid_po_kernel(
         out_rows = out_0.rearrange("(p t) v -> p t v", t=PACK)
         out_words = out_1[0].rearrange("p n j -> p (n j)").bitcast(I32)
 
-        def offsets(d, c):
-            return pos[d][:, c * P // GROUP : (c + 1) * P // GROUP]
+        def entries_of(d, half):
+            return pos[d][:, half * PAIR // GROUP : (half + 1) * PAIR // GROUP]
 
-        turned_pixels = DIRECT * P
-        whole = keep.tile([P, D, turned_pixels], F32, name="whole")
-        for d in range(D):
-            entries = pos[d][:, 0 : turned_pixels // GROUP]
-            nc.vector.tensor_tensor(whole[:, d, :], rows[0][:].indirect(entries), weight_rows[:, d, 0:turned_pixels], MULT)
-        weighed = {(0, c): whole[:, :, pixels(c)] for c in range(DIRECT)}
+        def within(c):
+            return pixels(c % 2)
 
-        def fetch_on_vector(c):
-            for t in range(0 if c == DIRECT else 1, SCALAR_TILE):
+        def fetch_on_vector(half, weighed):
+            for t in range(SCALAR_TILE):
                 for d in range(D):
                     nc.vector.tensor_tensor(
-                        weighed[t, c][:, d, :], rows[t][:].indirect(offsets(d, c)), weight_rows[:, d, pixels(c)], MULT
+                        weighed[t][d],
+                        rows[t][:].indirect(entries_of(d, half)),
+                        weight_rows[:, d, half * PAIR : (half + 1) * PAIR],
+                        MULT,
                     )
 
-        def fetch_on_scalar(c):
-            values = keep.tile([P, D, P], F32, name=f"from_scalar{c}")
+        def fetch_on_scalar(half, tag):
+            values = keep.tile([P, D, PAIR], F32, name=f"from_scalar{half}", tag=tag)
             for d in range(D):
-                nc.scalar.activation(values[:, d, :], rows[SCALAR_TILE][:].indirect(offsets(d, c)), ACT.Sigmoid)
+                nc.scalar.activation(values[:, d, :], rows[SCALAR_TILE][:].indirect(entries_of(d, half)), ACT.Sigmoid)
             return values
 
         def add_turned(total, parts):
@@ -199,21 +196,21 @@ def tile_picked_ysplat_sigmoid_po_kernel(
                     stop=(i == len(parts) - 1),
                 )
 
-        def turn_scalar(values, number):
+        def turn_scalar(c, values, number):
             turned = bank(number)
             for d in range(D):
-                nc.tensor.transpose(turned[:, d, :], values[:, d, :], ident[:])
+                nc.tensor.transpose(turned[:, d, :], values[:, d, within(c)], ident[:])
             return turned
 
         def weigh(c, turned):
             scaled = keep.tile([P, D, P], F32, name=f"scaled{c}")
             for d in range(D):
-                nc.scalar.activation(scaled[:, d, :], turned[:, d, :], ACT.Copy, scale=weight_cols[d][:, c : c + 1])
+                nc.scalar.activation(scaled[:, d, :], turned[:, d, :], ACT.Copy, scale=weight_cols[:, d, c : c + 1])
             return scaled
 
-        def turn_vector(c, number):
+        def turn_vector(c, weighed, number):
             total = bank(number)
-            add_turned(total, [(t, weighed[t, c][:, d, :]) for t in range(SCALAR_TILE) for d in range(D)])
+            add_turned(total, [(t, weighed[t][d][:, within(c)]) for t in range(SCALAR_TILE) for d in range(D)])
             return total
 
         def leave(c, total):
@@ -229,11 +226,10 @@ def tile_picked_ysplat_sigmoid_po_kernel(
             )
             return total
 
-        def hand_out(c, total, queue):
+        def hand_out(c, total):
             y = keep.tile([P, PACK, P], F32, name=f"y{c}")
             nc.scalar.copy(y[:], total[:])
-            queue.dma_start(out_rows[:, :, pixels(c)], y[:])
-            return y
+            nc.sync.dma_start(out_rows[:, :, pixels(c)], y[:])
 
         def round_on_scalar(c, total):
             y_bf = keep.tile([P, P, PACK], BF16, name=f"y_bf{c}", align_bytes=64)
@@ -254,58 +250,52 @@ def tile_picked_ysplat_sigmoid_po_kernel(
                 in_=y_bf[:].rearrange("p v t -> p (v t)"),
             )
 
-        first = keep.tile([P, D, P], F32, name="first", tag="tile1")
-        tile2 = keep.tile([P, DIRECT, D, P], F32, name="tile2")
-        weighed[1, 0] = first[:]
-        for c in range(DIRECT):
-            weighed[2, c] = tile2[:, c, :, :]
-        fetch_on_vector(0)
-        values0 = fetch_on_scalar(0)
-        turned0 = turn_scalar(values0, 0)
-        values1 = fetch_on_scalar(1)
-        turned1 = turn_scalar(values1, 1)
-        total0 = turn_vector(0, 7)
+        opener = keep.tile([P, PAIR], F32, name="opener", tag="second")
+        first = keep.tile([P, SCALAR_TILE, D, PAIR], F32, name="first")
+        weighed0 = [[opener[:] if (t, d) == (0, 0) else first[:, t, d, :] for d in range(D)] for t in range(SCALAR_TILE)]
+        fetch_on_vector(0, weighed0)
+        values0 = fetch_on_scalar(0, "from_scalar0")
+        turned0 = turn_scalar(0, values0, 0)
+        turned1 = turn_scalar(1, values0, 1)
+        total0 = turn_vector(0, weighed0, 7)
+        total1 = turn_vector(1, weighed0, 6)
 
-        later = keep.tile([P, DIRECT - 1 + PACK, D, P], F32, name="later", tag="tile1")
-        for c in range(1, DIRECT):
-            weighed[1, c] = later[:, c - 1, :, :]
-        direct = later[:, DIRECT - 1 :, :, :]
-        for t in range(PACK):
-            weighed[t, DIRECT] = direct[:, t, :, :]
-        for c in range(1, CHUNKS):
-            fetch_on_vector(c)
+        second = keep.tile([P, PACK, D, PAIR], F32, name="second", tag="second")
+        weighed1 = [[second[:, t, d, :] for d in range(D)] for t in range(SCALAR_TILE)]
+        fetch_on_vector(1, weighed1)
 
         scaled0 = weigh(0, turned0)
-        values2 = fetch_on_scalar(2)
+        scaled1 = weigh(1, turned1)
         sums0 = leave(0, total0)
         back0 = turn_back(sums0, scaled0, 2)
-        total1 = turn_vector(1, 0)
-        scaled1 = weigh(1, turned1)
-        turned2 = turn_scalar(values2, 3)
-        hand_out(0, back0, nc.sync)
-        y_bf0 = round_on_scalar(0, back0)
         sums1 = leave(1, total1)
-        back1 = turn_back(sums1, scaled1, 4)
-        total2 = turn_vector(2, 1)
-        values3 = fetch_on_scalar(DIRECT)
+        back1 = turn_back(sums1, scaled1, 3)
+        hand_out(0, back0)
+        values1 = fetch_on_scalar(1, "sums0")
+        turned2 = turn_scalar(2, values1, 0)
+        total2 = turn_vector(2, weighed1, 4)
+        hand_out(1, back1)
         scaled2 = weigh(2, turned2)
-        y1 = hand_out(1, back1, nc.sync)
+        y_bf0 = round_on_scalar(0, back0)
         sums2 = leave(2, total2)
         back2 = turn_back(sums2, scaled2, 5)
         y_bf1 = round_on_scalar(1, back1)
-        hand_out(2, back2, nc.scalar)
+        hand_out(2, back2)
         y_bf2 = round_on_scalar(2, back2)
 
-        nc.vector.tensor_tensor(direct[:, SCALAR_TILE, :, :], values3[:], weight_rows[:, :, pixels(DIRECT)], MULT)
+        direct = second[:, :, :, within(DIRECT)]
+        nc.vector.tensor_tensor(
+            direct[:, SCALAR_TILE, :, :], values1[:, :, within(DIRECT)], weight_rows[:, :, pixels(DIRECT)], MULT
+        )
         pair = keep.tile([P, PACK, P], F32, name="pair")
-        y3 = keep.tile([P, PACK, P], F32, name="y3", tag="sums2")
+        y3 = keep.tile([P, PACK, P], F32, name="y3")
         nc.vector.tensor_tensor(pair[:], direct[:, :, 0, :], direct[:, :, 1, :], ADD)
-        quantise(0, y_bf0)
         nc.vector.tensor_tensor(y3[:], pair[:], direct[:, :, 2, :], ADD)
         nc.sync.dma_start(out_rows[:, :, pixels(DIRECT)], y3[:])
         y_bf3 = round_on_vector(DIRECT, y3[:])
-        quantise(1, y_bf1)
+        quantise(0, y_bf0)
         quantise(DIRECT, y_bf3)
+        quantise(1, y_bf1)
         quantise(2, y_bf2)
 
         for half in (slice(0, V // 2), slice(V // 2, V)):

@@ -69,13 +69,17 @@ def tile_picked_ysplat_sigmoid_po_kernel(
         )
         nc.sync.dma_start(x_table[:], x_words[0].rearrange("p n j -> p (n j)").bitcast(I32))
 
-        nc.vector.memset(op_table[: P - 1, :], 0.0)
-        nc.vector.memset(scale_table[: P - BLOCKS, :].bitcast(I32), 0)
-        nc.vector.memset(x_scale[:].bitcast(I32), 0)
-        for d in range(D):
-            nc.gpsimd.memset(fall_rows[: P - 1, d * V : (d + 1) * V], 0.0)
-            if d == 0:
-                make_identity(nc, ident[:])
+        warm = keep.tile([P, 2], F32, name="warm")
+        nc.vector.memset(warm[:, 0:1], 0.0)
+        nc.scalar.activation(warm[:, 1:2], warm[:, 0:1], ACT.Sigmoid)
+
+        for table, width in ((op_table, S), (fall_rows, V)):
+            nc.vector.memset(table[: P - 1, 0 : width - 1], 0.0)
+            nc.vector.memset(table[: P - 1, width - 1 : width], 0.0)
+        nc.gpsimd.memset(scale_table[: P - BLOCKS, :].bitcast(I32), 0)
+        nc.gpsimd.memset(fall_rows[: P - 1, V:], 0.0)
+        nc.gpsimd.memset(x_scale[:].bitcast(I32), 0)
+        make_identity(nc, ident[:])
 
         alpha_rows = [keep.tile([P, V], F32, name=f"alpha_rows{d}", align_bytes=64) for d in range(D)]
 

@@ -145,7 +145,9 @@ def tile_picked_ysplat_sigmoid_po_kernel(
             nc.vector.tensor_copy(x_codes[h], x_table[:].bitcast(U32).indirect(entries))
 
         rows = [keep.tile([P, S], F32, name=f"rows{t}") for t in range(PACK)]
-        for number, (h, t) in enumerate(PRODUCTS):
+
+        def product(number):
+            h, t = PRODUCTS[number]
             cols = slice(h * HALF, (h + 1) * HALF)
             acc = bank(number)[:].rearrange("p c n -> p (c n)")
             nc.tensor.matmul_mx(
@@ -167,27 +169,25 @@ def tile_picked_ysplat_sigmoid_po_kernel(
         out_rows = out_0.rearrange("(p t) v -> p t v", t=PACK)
         out_words = out_1[0].rearrange("p n j -> p (n j)").bitcast(I32)
 
-        def entries_of(d, half):
-            return pos[d][:, half * PAIR // GROUP : (half + 1) * PAIR // GROUP]
+        def entries_of(d, span):
+            return pos[d][:, span.start // GROUP : span.stop // GROUP]
 
         def within(c):
             return pixels(c % 2)
 
-        def fetch_on_vector(half, weighed):
-            for t in range(SCALAR_TILE):
-                for d in range(D):
-                    nc.vector.tensor_tensor(
-                        weighed[t][d],
-                        rows[t][:].indirect(entries_of(d, half)),
-                        weight_rows[:, d, half * PAIR : (half + 1) * PAIR],
-                        MULT,
-                    )
+        def pair_of(half):
+            return slice(half * PAIR, (half + 1) * PAIR)
 
-        def fetch_on_scalar(half, tag):
-            values = keep.tile([P, D, PAIR], F32, name=f"from_scalar{half}", tag=tag)
-            for d in range(D):
-                nc.scalar.activation(values[:, d, :], rows[SCALAR_TILE][:].indirect(entries_of(d, half)), ACT.Sigmoid)
-            return values
+        def fetch_on_vector(values, t, d, span):
+            nc.vector.tensor_tensor(values, rows[t][:].indirect(entries_of(d, span)), weight_rows[:, d, span], MULT)
+
+        values = keep.tile([P, D, V], F32, name="values")
+
+        def fetch_on_scalar(d, half):
+            span = pair_of(half)
+            nc.scalar.activation(values[:, d, span], rows[SCALAR_TILE][:].indirect(entries_of(d, span)), ACT.Sigmoid)
+            for c in (2 * half, 2 * half + 1):
+                nc.tensor.transpose(turned[c][:, d, :], values[:, d, pixels(c)], ident[:])
 
         def add_turned(total, parts):
             for i, (quarter, values) in enumerate(parts):
@@ -200,22 +200,14 @@ def tile_picked_ysplat_sigmoid_po_kernel(
                     stop=(i == len(parts) - 1),
                 )
 
-        def turn_scalar(c, values, number):
-            turned = bank(number)
-            for d in range(D):
-                nc.tensor.transpose(turned[:, d, :], values[:, d, within(c)], ident[:])
-            return turned
-
-        def weigh(c, turned):
+        def weigh(c):
             scaled = keep.tile([P, D, P], F32, name=f"scaled{c}")
             for d in range(D):
-                nc.scalar.activation(scaled[:, d, :], turned[:, d, :], ACT.Copy, scale=weight_cols[:, d, c : c + 1])
+                nc.scalar.activation(scaled[:, d, :], turned[c][:, d, :], ACT.Copy, scale=weight_cols[:, d, c : c + 1])
             return scaled
 
-        def turn_vector(c, weighed, number):
-            total = bank(number)
-            add_turned(total, [(t, weighed[t][d][:, within(c)]) for t in range(SCALAR_TILE) for d in range(D)])
-            return total
+        def turn_vector(total, values, t, first, last):
+            nc.tensor.matmul(total[:, t, :], lhsT=values, rhs=ident[:], is_transpose=True, start=first, stop=last)
 
         def leave(c, total):
             sums = keep.tile([P, SCALAR_TILE, P], F32, name=f"sums{c}")
@@ -254,47 +246,65 @@ def tile_picked_ysplat_sigmoid_po_kernel(
                 in_=y_bf[:].rearrange("p v t -> p (v t)"),
             )
 
+        for number in range(6):
+            product(number)
+        turned = {0: bank(1), 1: bank(3)}
+        fetch_on_scalar(0, 0)
+        product(6)
+        fetch_on_scalar(1, 0)
+        product(7)
+
         opener = keep.tile([P, PAIR], F32, name="opener", tag="second")
         first = keep.tile([P, SCALAR_TILE, D, PAIR], F32, name="first")
-        weighed0 = [[opener[:] if (t, d) == (0, 0) else first[:, t, d, :] for d in range(D)] for t in range(SCALAR_TILE)]
-        fetch_on_vector(0, weighed0)
-        values0 = fetch_on_scalar(0, "from_scalar0")
-        turned0 = turn_scalar(0, values0, 0)
-        turned1 = turn_scalar(1, values0, 1)
-        total0 = turn_vector(0, weighed0, 7)
-        total1 = turn_vector(1, weighed0, 6)
+        totals = {0: bank(0), 1: bank(2)}
+        for t in range(SCALAR_TILE):
+            for d in range(D):
+                weighed = opener[:] if (t, d) == (SCALAR_TILE - 1, 0) else first[:, t, d, :]
+                fetch_on_vector(weighed, t, d, pair_of(0))
+                for c in range(2):
+                    turn_vector(totals[c], weighed[:, within(c)], t, (t, d) == (0, 0), (t, d) == (SCALAR_TILE - 1, D - 1))
+            if t == 1:
+                fetch_on_scalar(2, 0)
 
-        second = keep.tile([P, PACK, D, PAIR], F32, name="second", tag="second")
-        weighed1 = [[second[:, t, d, :] for d in range(D)] for t in range(SCALAR_TILE)]
-        fetch_on_vector(1, weighed1)
+        second = keep.tile([P, SCALAR_TILE, D, PAIR], F32, name="second", tag="second")
+        for t in range(SCALAR_TILE):
+            fetch_on_vector(second[:, t, 0, :], t, 0, pair_of(1))
+        for c in (2, DIRECT):
+            for d in range(1, D):
+                for t in range(SCALAR_TILE):
+                    fetch_on_vector(second[:, t, d, within(c)], t, d, pixels(c))
 
-        scaled0 = weigh(0, turned0)
-        scaled1 = weigh(1, turned1)
-        sums0 = leave(0, total0)
-        back0 = turn_back(sums0, scaled0, 2)
-        sums1 = leave(1, total1)
-        back1 = turn_back(sums1, scaled1, 3)
+        turned[2], turned[3] = bank(4), bank(5)
+        fetch_on_scalar(0, 1)
+        scaled0 = weigh(0)
+        scaled1 = weigh(1)
+        sums0 = leave(0, totals[0])
+        back0 = turn_back(sums0, scaled0, 6)
+        sums1 = leave(1, totals[1])
+        back1 = turn_back(sums1, scaled1, 7)
+        fetch_on_scalar(1, 1)
         hand_out(0, back0)
-        values1 = fetch_on_scalar(1, "sums0")
-        turned2 = turn_scalar(2, values1, 0)
-        total2 = turn_vector(2, weighed1, 4)
+        fetch_on_scalar(2, 1)
+        total2 = bank(2)
+        add_turned(total2, [(t, second[:, t, d, within(2)]) for d in range(D) for t in range(SCALAR_TILE)])
         hand_out(1, back1)
-        scaled2 = weigh(2, turned2)
-        y_bf0 = round_on_scalar(0, back0)
+        scaled2 = weigh(2)
         sums2 = leave(2, total2)
-        back2 = turn_back(sums2, scaled2, 5)
-        y_bf1 = round_on_scalar(1, back1)
+        back2 = turn_back(sums2, scaled2, 1)
+        scaled3 = weigh(DIRECT)
+        back3 = bank(3)
+        add_turned(back3, [(0, scaled3[:, d, :]) for d in range(D)])
+        y_bf0 = round_on_scalar(0, back0)
         hand_out(2, back2)
+        y3 = keep.tile([P, PACK, P], F32, name="y3")
+        nc.scalar.copy(y3[:, SCALAR_TILE, :], back3[:, 0, :])
+        y_bf1 = round_on_scalar(1, back1)
         y_bf2 = round_on_scalar(2, back2)
 
         direct = second[:, :, :, within(DIRECT)]
-        nc.vector.tensor_tensor(
-            direct[:, SCALAR_TILE, :, :], values1[:, :, within(DIRECT)], weight_rows[:, :, pixels(DIRECT)], MULT
-        )
-        pair = keep.tile([P, PACK, P], F32, name="pair")
-        y3 = keep.tile([P, PACK, P], F32, name="y3")
+        pair = keep.tile([P, SCALAR_TILE, P], F32, name="pair")
         nc.vector.tensor_tensor(pair[:], direct[:, :, 0, :], direct[:, :, 1, :], ADD)
-        nc.vector.tensor_tensor(y3[:], pair[:], direct[:, :, 2, :], ADD)
+        nc.vector.tensor_tensor(y3[:, 0:SCALAR_TILE, :], pair[:], direct[:, :, 2, :], ADD)
         nc.sync.dma_start(out_rows[:, :, pixels(DIRECT)], y3[:])
         y_bf3 = round_on_vector(DIRECT, y3[:])
         quantise(0, y_bf0)

@@ -125,16 +125,16 @@ def tile_picked_ysplat_sigmoid_po_kernel(
 
         alpha = [turn_alpha(d, 2 + d) for d in range(D)]
         round_w(slice(0, P))
-        nc.vector.tensor_copy(weight_cols[:, 0, :], alpha[0])
         nc.vector.tensor_scalar(through[:, 0, :], alpha[0], -1.0, 1.0, MULT, ADD)
+        nc.vector.tensor_copy(weight_cols[:, 0, :], alpha[0])
         nc.vector.tensor_tensor(weight_cols[:, 1, :], alpha[1], through[:, 0, :], MULT)
-        nc.vector.tensor_tensor(through[:, 1, :], through[:, 0, :], weight_cols[:, 1, :], SUBTRACT)
+        nc.vector.scalar_tensor_tensor(through[:, 1, :], alpha[1], 1.0, through[:, 0, :], SUBTRACT, MULT)
         w_codes = keep.tile([P, N], U32, name="w_codes", tag="op_table", align_bytes=64)
         w_scales = keep.tile([P, N], U8, name="w_scales", align_bytes=64)
         nc.vector.quantize_mx(
             out=w_codes[:].bitcast(FP8X4), scales=w_scales[:], in_=w_bf[:].rearrange("p t m j -> p (t m j)")
         )
-        nc.vector.tensor_tensor(weight_cols[:, 2, :], alpha[2], through[:, 1, :], MULT)
+        nc.vector.scalar_tensor_tensor(weight_cols[:, 2, :], alpha[2], -1.0, through[:, 1, :], MULT, MULT)
         for d in range(D):
             nc.scalar.copy(weight_rows[:, d, :], spread(d, 5 + d))
 
@@ -227,23 +227,21 @@ def tile_picked_ysplat_sigmoid_po_kernel(
             nc.scalar.copy(y[:], total[:])
             nc.sync.dma_start(out_rows[:, :, pixels(c)], y[:])
 
+        y_bf = keep.tile([P, V, PACK], BF16, name="y_bf", align_bytes=64)
+
         def round_on_scalar(c, total):
-            y_bf = keep.tile([P, P, PACK], BF16, name=f"y_bf{c}", align_bytes=64)
-            nc.scalar.copy(y_bf[:], total[:].rearrange("p t v -> p v t"))
-            return y_bf
+            nc.scalar.copy(y_bf[:, pixels(c), :], total[:].rearrange("p t v -> p v t"))
 
         def round_on_vector(c, y):
-            y_bf = keep.tile([P, P, PACK], BF16, name=f"y_bf{c}", align_bytes=64)
             nc.vector.tensor_copy(
-                y_bf[:].rearrange("p (c i) t -> p c t i", i=4), y.rearrange("p t (c i) -> p c t i", i=4)
+                y_bf[:, pixels(c), :].rearrange("p (c i) t -> p c t i", i=4), y.rearrange("p t (c i) -> p c t i", i=4)
             )
-            return y_bf
 
-        def quantise(c, y_bf):
+        def quantise(span):
             nc.vector.quantize_mx(
-                out=y_codes[:, pixels(c)].bitcast(FP8X4),
-                scales=y_scales[:, pixels(c)],
-                in_=y_bf[:].rearrange("p v t -> p (v t)"),
+                out=y_codes[:, span].bitcast(FP8X4),
+                scales=y_scales[:, span],
+                in_=y_bf[:, span, :].rearrange("p v t -> p (v t)"),
             )
 
         for number in range(6):
@@ -294,23 +292,21 @@ def tile_picked_ysplat_sigmoid_po_kernel(
         scaled3 = weigh(DIRECT)
         back3 = bank(3)
         add_turned(back3, [(0, scaled3[:, d, :]) for d in range(D)])
-        y_bf0 = round_on_scalar(0, back0)
+        round_on_scalar(0, back0)
         hand_out(2, back2)
         y3 = keep.tile([P, PACK, P], F32, name="y3")
         nc.scalar.copy(y3[:, SCALAR_TILE, :], back3[:, 0, :])
-        y_bf1 = round_on_scalar(1, back1)
-        y_bf2 = round_on_scalar(2, back2)
+        round_on_scalar(1, back1)
+        round_on_scalar(2, back2)
 
         direct = second[:, :, :, within(DIRECT)]
         pair = keep.tile([P, SCALAR_TILE, P], F32, name="pair")
         nc.vector.tensor_tensor(pair[:], direct[:, :, 0, :], direct[:, :, 1, :], ADD)
         nc.vector.tensor_tensor(y3[:, 0:SCALAR_TILE, :], pair[:], direct[:, :, 2, :], ADD)
         nc.sync.dma_start(out_rows[:, :, pixels(DIRECT)], y3[:])
-        y_bf3 = round_on_vector(DIRECT, y3[:])
-        quantise(0, y_bf0)
-        quantise(DIRECT, y_bf3)
-        quantise(1, y_bf1)
-        quantise(2, y_bf2)
+        round_on_vector(DIRECT, y3[:])
+        quantise(pair_of(0))
+        quantise(pair_of(1))
 
         for half in (slice(0, V // 2), slice(V // 2, V)):
             nc.sync.dma_start(out_words[:, half], y_codes[:, half].bitcast(I32))

@@ -164,77 +164,72 @@ def tile_picked_ysplat_sigmoid_po_kernel(
             else:
                 nc.vector.tensor_copy(rows[t][:, cols], acc)
 
+        y = keep.tile([P, PACK, V], F32, name="y")
+        y_bf = keep.tile([P, V, PACK], BF16, name="y_bf", align_bytes=64)
         y_codes = keep.tile([P, V], U32, name="y_codes", align_bytes=64)
         y_scales = keep.tile([P, V], U8, name="y_scales", align_bytes=64)
         out_rows = out_0.rearrange("(p t) v -> p t v", t=PACK)
         out_words = out_1[0].rearrange("p n j -> p (n j)").bitcast(I32)
+        whole = slice(0, V)
 
         def entries_of(d, span):
             return pos[d][:, span.start // GROUP : span.stop // GROUP]
 
-        def within(c):
-            return pixels(c % 2)
-
-        def pair_of(half):
-            return slice(half * PAIR, (half + 1) * PAIR)
-
         def fetch_on_vector(values, t, d, span):
             nc.vector.tensor_tensor(values, rows[t][:].indirect(entries_of(d, span)), weight_rows[:, d, span], MULT)
 
-        values = keep.tile([P, D, V], F32, name="values")
-
-        def fetch_on_scalar(d, half):
-            span = pair_of(half)
-            nc.scalar.activation(values[:, d, span], rows[SCALAR_TILE][:].indirect(entries_of(d, span)), ACT.Sigmoid)
-            for c in (2 * half, 2 * half + 1):
-                nc.tensor.transpose(turned[c][:, d, :], values[:, d, pixels(c)], ident[:])
-
-        def add_turned(total, parts):
-            for i, (quarter, values) in enumerate(parts):
+        def turn(total, values, first, last):
+            for c in range(CHUNKS):
                 nc.tensor.matmul(
-                    total[:, quarter, :],
-                    lhsT=values,
+                    total[:, c, :],
+                    lhsT=values[:, pixels(c)],
                     rhs=ident[:],
                     is_transpose=True,
-                    start=(i == 0),
-                    stop=(i == len(parts) - 1),
+                    start=first and c == 0,
+                    stop=last and c == CHUNKS - 1,
                 )
 
-        def weigh(c):
-            scaled = keep.tile([P, D, P], F32, name=f"scaled{c}")
-            for d in range(D):
-                nc.scalar.activation(scaled[:, d, :], turned[c][:, d, :], ACT.Copy, scale=weight_cols[:, d, c : c + 1])
-            return scaled
+        def flat(tile):
+            return tile[:].rearrange("p c n -> p (c n)")
 
-        def turn_vector(total, values, t, first, last):
-            nc.tensor.matmul(total[:, t, :], lhsT=values, rhs=ident[:], is_transpose=True, start=first, stop=last)
-
-        def leave(c, total):
-            sums = keep.tile([P, SCALAR_TILE, P], F32, name=f"sums{c}")
-            nc.scalar.copy(sums[:], total[:, 0:SCALAR_TILE, :])
-            return sums
-
-        def turn_back(sums, scaled, number):
+        def sum_turned(t, number):
             total = bank(number)
-            add_turned(
-                total,
-                [(SCALAR_TILE, scaled[:, d, :]) for d in range(D)] + [(t, sums[:, t, :]) for t in range(SCALAR_TILE)],
-            )
+            layers = keep.tile([P, D, V], F32, name=f"layers{t}")
+            for d in range(D):
+                fetch_on_vector(layers[:, d, :], t, d, whole)
+                turn(total, layers[:, d, :], d == 0, d == D - 1)
             return total
 
-        def hand_out(c, total):
-            y = keep.tile([P, PACK, P], F32, name=f"y{c}")
-            nc.scalar.copy(y[:], total[:])
-            nc.sync.dma_start(out_rows[:, :, pixels(c)], y[:])
+        def leave_and_turn_back(t, total, number):
+            sums = keep.tile([P, V], F32, name=f"sums{t}")
+            nc.scalar.copy(sums[:], flat(total))
+            back = bank(number)
+            turn(back, sums[:], True, True)
+            return back
 
-        y_bf = keep.tile([P, V, PACK], BF16, name="y_bf", align_bytes=64)
+        def hand_out(t, back):
+            nc.scalar.copy(y[:, t, :], flat(back))
+            nc.scalar.dma_start(out_rows[:, t, :], y[:, t, :])
 
-        def round_on_scalar(c, total):
-            nc.scalar.copy(y_bf[:, pixels(c), :], total[:].rearrange("p t v -> p v t"))
+        def fetch_on_scalar(d, number):
+            values = keep.tile([P, V], F32, name=f"values{d}")
+            nc.scalar.activation(values[:], rows[SCALAR_TILE][:].indirect(pos[d][:]), ACT.Sigmoid)
+            turned = bank(number)
+            turn(turned, values[:], True, True)
+            return turned
 
-        def round_on_vector(c, y):
-            nc.vector.tensor_copy(
-                y_bf[:, pixels(c), :].rearrange("p (c i) t -> p c t i", i=4), y.rearrange("p t (c i) -> p c t i", i=4)
+        def weigh(d, turned, back):
+            scaled = keep.tile([P, V], F32, name=f"scaled{d}")
+            for c in range(CHUNKS):
+                nc.scalar.activation(
+                    scaled[:, pixels(c)], turned[:, c, :], ACT.Copy, scale=weight_cols[:, d, c : c + 1]
+                )
+            turn(back, scaled[:], d == 0, d == D - 1)
+
+        def round_y(copy, span):
+            copy(
+                y_bf[:, span, :].rearrange("p (c i) t -> p c t i", i=4),
+                y[:, :, span].rearrange("p t (c i) -> p c t i", i=4),
             )
 
         def quantise(span):
@@ -243,73 +238,44 @@ def tile_picked_ysplat_sigmoid_po_kernel(
                 scales=y_scales[:, span],
                 in_=y_bf[:, span, :].rearrange("p v t -> p (v t)"),
             )
+            nc.sync.dma_start(out_words[:, span], y_codes[:, span].bitcast(I32))
 
         for number in range(6):
             product(number)
-        turned = {0: bank(1), 1: bank(3)}
-        fetch_on_scalar(0, 0)
+        total0 = sum_turned(0, 0)
+        turned0 = fetch_on_scalar(0, 1)
         product(6)
-        fetch_on_scalar(1, 0)
         product(7)
-
-        opener = keep.tile([P, PAIR], F32, name="opener", tag="second")
-        first = keep.tile([P, SCALAR_TILE, D, PAIR], F32, name="first")
-        totals = {0: bank(0), 1: bank(2)}
-        for t in range(SCALAR_TILE):
-            for d in range(D):
-                weighed = opener[:] if (t, d) == (SCALAR_TILE - 1, 0) else first[:, t, d, :]
-                fetch_on_vector(weighed, t, d, pair_of(0))
-                for c in range(2):
-                    turn_vector(totals[c], weighed[:, within(c)], t, (t, d) == (0, 0), (t, d) == (SCALAR_TILE - 1, D - 1))
-            if t == 1:
-                fetch_on_scalar(2, 0)
-
-        second = keep.tile([P, SCALAR_TILE, D, PAIR], F32, name="second", tag="second")
-        for t in range(SCALAR_TILE):
-            fetch_on_vector(second[:, t, 0, :], t, 0, pair_of(1))
-        for c in (2, DIRECT):
-            for d in range(1, D):
-                for t in range(SCALAR_TILE):
-                    fetch_on_vector(second[:, t, d, within(c)], t, d, pixels(c))
-
-        turned[2], turned[3] = bank(4), bank(5)
-        fetch_on_scalar(0, 1)
-        scaled0 = weigh(0)
-        scaled1 = weigh(1)
-        sums0 = leave(0, totals[0])
-        back0 = turn_back(sums0, scaled0, 6)
-        sums1 = leave(1, totals[1])
-        back1 = turn_back(sums1, scaled1, 7)
-        fetch_on_scalar(1, 1)
+        turned1 = fetch_on_scalar(1, 3)
+        total1 = sum_turned(1, 4)
+        back3 = bank(6)
+        weigh(0, turned0, back3)
+        back0 = leave_and_turn_back(0, total0, 5)
+        turned2 = fetch_on_scalar(2, 2)
+        weigh(1, turned1, back3)
         hand_out(0, back0)
-        fetch_on_scalar(2, 1)
-        total2 = bank(2)
-        add_turned(total2, [(t, second[:, t, d, within(2)]) for d in range(D) for t in range(SCALAR_TILE)])
+        back1 = leave_and_turn_back(1, total1, 0)
+        weigh(2, turned2, back3)
         hand_out(1, back1)
-        scaled2 = weigh(2)
-        sums2 = leave(2, total2)
-        back2 = turn_back(sums2, scaled2, 1)
-        scaled3 = weigh(DIRECT)
-        back3 = bank(3)
-        add_turned(back3, [(0, scaled3[:, d, :]) for d in range(D)])
-        round_on_scalar(0, back0)
-        hand_out(2, back2)
-        y3 = keep.tile([P, PACK, P], F32, name="y3")
-        nc.scalar.copy(y3[:, SCALAR_TILE, :], back3[:, 0, :])
-        round_on_scalar(1, back1)
-        round_on_scalar(2, back2)
+        hand_out(SCALAR_TILE, back3)
 
-        direct = second[:, :, :, within(DIRECT)]
-        pair = keep.tile([P, SCALAR_TILE, P], F32, name="pair")
-        nc.vector.tensor_tensor(pair[:], direct[:, :, 0, :], direct[:, :, 1, :], ADD)
-        nc.vector.tensor_tensor(y3[:, 0:SCALAR_TILE, :], pair[:], direct[:, :, 2, :], ADD)
-        nc.sync.dma_start(out_rows[:, :, pixels(DIRECT)], y3[:])
-        round_on_vector(DIRECT, y3[:])
-        quantise(pair_of(0))
-        quantise(pair_of(1))
+        spans = [slice(0, 2 * P), pixels(2), pixels(3)]
+        layers = keep.tile([P, D, V], F32, name="layers2")
+        pair = keep.tile([P, V], F32, name="pair")
+        for span in spans:
+            fetch_on_vector(layers[:, 0, span], 2, 0, span)
+            fetch_on_vector(layers[:, 1, span], 2, 1, span)
+            fetch_on_vector(layers[:, 2, span], 2, 2, span)
+            nc.vector.tensor_tensor(pair[:, span], layers[:, 0, span], layers[:, 1, span], ADD)
+            nc.vector.tensor_tensor(y[:, 2, span], pair[:, span], layers[:, 2, span], ADD)
+            nc.sync.dma_start(out_rows[:, 2, span], y[:, 2, span])
 
-        for half in (slice(0, V // 2), slice(V // 2, V)):
-            nc.sync.dma_start(out_words[:, half], y_codes[:, half].bitcast(I32))
+        round_y(nc.scalar.copy, spans[0])
+        round_y(nc.scalar.copy, spans[1])
+        round_y(nc.vector.tensor_copy, spans[2])
+        for span in (spans[0], spans[2], spans[1]):
+            quantise(span)
+
         for q in range(P // QUADRANT):
             queue = nc.scalar if q % 2 else nc.sync
             queue.dma_start(

@@ -28,6 +28,7 @@ PAIR = 2 * P
 HALF = S // 2
 SCALAR_TILE = PACK - 1
 PRODUCTS = [(0, 0), (0, 3), (1, 0), (1, 3), (0, 1), (1, 1), (0, 2), (1, 2)]
+W_BYTES = 2 * N * PACK
 
 
 def tile_picked_ysplat_sigmoid_po_kernel(
@@ -49,24 +50,26 @@ def tile_picked_ysplat_sigmoid_po_kernel(
         picks = keep.tile([P, S // GROUP], U16, name="picks")
         w_raw = keep.tile([P, PACK, N], F32, name="w_raw")
         x_table = keep.tile([P, T], I32, name="x_table")
-        scale_table = keep.tile([P, T], U8, name="scale_table")
-        op_table = keep.tile([P, S], F32, name="op_table", align_bytes=64)
-        fall_rows = keep.tile([P, D * V], F32, name="fall_rows")
+        scale_table = placed.tile([P, T], U8, name="scale_table", offset=W_BYTES, align_bytes=64)
+        op_table = keep.tile([P, S], F32, name="op_table")
+        fall_rows = keep.tile([P, (D - 1) * V], F32, name="fall_rows")
+        last_fall = keep.tile([P, V], F32, name="last_fall")
         ident = keep.tile([P, P], F32, name="ident")
         x_scale_rows = keep.tile([P, S], U8, name="x_scale_rows")
         x_scale = keep.tile([P, S], U8, name="x_scale", align_bytes=64)
 
         nc.sync.dma_start(pos[0][:], pos1)
         nc.sync.dma_start(op_table[P - 1 :, :], op[0:1, :])
-        nc.sync.dma_start(fall_rows[P - 1 :, 0:V], fall[0, 0:1, :])
-        nc.sync.dma_start(picks[:], offs)
-        nc.sync.dma_start(scale_table[P - BLOCKS :, :].bitcast(I32), x_scales[0].bitcast(I32))
-        nc.sync.dma_start(w_raw[:], w1.rearrange("(p j) c -> p j c", j=PACK))
+        nc.sync.dma_start(
+            fall_rows[P - 1 :, :].rearrange("p (d v) -> p d v", d=D - 1),
+            fall[: D - 1, 0:1, :].rearrange("d p v -> p d v"),
+        )
         nc.sync.dma_start(pos[1][:], pos2)
         nc.sync.dma_start(pos[2][:], pos3)
-        nc.sync.dma_start(
-            fall_rows[P - 1 :, V:].rearrange("p (d v) -> p d v", d=D - 1), fall[1:, 0:1, :].rearrange("d p v -> p d v")
-        )
+        nc.sync.dma_start(last_fall[P - 1 :, :], fall[D - 1, 0:1, :])
+        nc.sync.dma_start(w_raw[:], w1.rearrange("(p j) c -> p j c", j=PACK))
+        nc.sync.dma_start(picks[:], offs)
+        nc.sync.dma_start(scale_table[P - BLOCKS :, :].bitcast(I32), x_scales[0].bitcast(I32))
         nc.sync.dma_start(x_table[:], x_words[0].rearrange("p n j -> p (n j)").bitcast(I32))
 
         warm = keep.tile([P, 2], F32, name="warm")
@@ -76,34 +79,17 @@ def tile_picked_ysplat_sigmoid_po_kernel(
         for table, width in ((op_table, S), (fall_rows, V)):
             nc.vector.memset(table[: P - 1, 0 : width - 1], 0.0)
             nc.vector.memset(table[: P - 1, width - 1 : width], 0.0)
-        nc.gpsimd.memset(scale_table[: P - BLOCKS, :].bitcast(I32), 0)
         nc.gpsimd.memset(fall_rows[: P - 1, V:], 0.0)
-        nc.gpsimd.memset(x_scale[:].bitcast(I32), 0)
         make_identity(nc, ident[:])
+        nc.gpsimd.memset(last_fall[: P - 1, :], 0.0)
+        nc.gpsimd.memset(scale_table[: P - BLOCKS, :].bitcast(I32), 0)
+        nc.gpsimd.memset(x_scale[:].bitcast(I32), 0)
 
-        alpha_rows = [keep.tile([P, V], F32, name=f"alpha_rows{d}", align_bytes=64) for d in range(D)]
+        alpha_rows = [keep.tile([P, V], F32, name=f"alpha_rows{d}") for d in range(D)]
+        falloff = [fall_rows[:, 0:V], fall_rows[:, V:], last_fall[:]]
 
-        def look_up_alpha(d):
-            nc.vector.tensor_tensor(
-                alpha_rows[d][:], op_table[:].indirect(pos[d][:]), fall_rows[:, d * V : (d + 1) * V], MULT
-            )
-
-        look_up_alpha(0)
-        nc.vector.tensor_copy(x_scale_rows[:], scale_table[:].indirect(picks[:]))
-        for q in range(P // QUADRANT):
-            first_row = P - BLOCKS + SCALE_ROWS * q
-            nc.sync.dma_start(
-                x_scale[QUADRANT * q : QUADRANT * q + SCALE_ROWS, :].bitcast(I32),
-                x_scale_rows[first_row : first_row + SCALE_ROWS, :].bitcast(I32),
-            )
-        for d in range(1, D):
-            look_up_alpha(d)
-
-        through = placed.tile([P, D - 1, CHUNKS], F32, name="through", offset=2 * K * PACK, align_bytes=64)
-        weight_cols = keep.tile([P, D, CHUNKS], F32, name="weight_cols")
-        weight_rows = keep.tile([P, D, V], F32, name="weight_rows")
-
-        def turn_alpha(d, number):
+        def alpha_columns(d, number):
+            nc.vector.tensor_tensor(alpha_rows[d][:], op_table[:].indirect(pos[d][:]), falloff[d], MULT)
             turned = bank(number)
             for c in range(CHUNKS):
                 nc.tensor.transpose(turned[:, c, :], alpha_rows[d][:, pixels(c)], ident[:])
@@ -112,33 +98,45 @@ def tile_picked_ysplat_sigmoid_po_kernel(
         def spread(d, number):
             rows_of = bank(number)
             for c in range(CHUNKS):
-                nc.tensor.transpose(rows_of[:, c, :], weight_cols[:, d, c : c + 1].to_broadcast([P, P]), ident[:])
-            return rows_of[:].rearrange("p c v -> p (c v)")
+                nc.tensor.transpose(rows_of[:, c, :], weight_cols[d][:, c : c + 1].to_broadcast([P, P]), ident[:])
+            nc.scalar.copy(weight_rows[:, d, :], rows_of[:].rearrange("p c v -> p (c v)"))
 
         w_bf = placed.tile([P, PACK, P, PACK], BF16, name="w_bf", offset=0, align_bytes=64)
+        nc.scalar.copy(
+            w_bf[:].rearrange("p t m j -> p m j t"),
+            w_raw[:].rearrange("p j (m t) -> p m j t", t=PACK),
+        )
+        weight_rows = keep.tile([P, D, V], F32, name="weight_rows", tag="w_raw")
 
-        def round_w(part):
-            nc.scalar.copy(
-                w_bf[:, :, part, :].rearrange("p t m j -> p m j t"),
-                w_raw[:].rearrange("p j (m t) -> p m j t", t=PACK)[:, part, :, :],
+        alpha = [alpha_columns(d, 2 + d) for d in range(D)]
+        first_cols = keep.tile([P, 2, CHUNKS], F32, name="first_cols")
+        second_cols = keep.tile([P, 2, CHUNKS], F32, name="second_cols", tag="last_fall")
+        nc.vector.tensor_scalar(first_cols[:, 1, :], alpha[0], -1.0, 1.0, MULT, ADD)
+        nc.vector.tensor_copy(first_cols[:, 0, :], alpha[0])
+        nc.vector.tensor_tensor(second_cols[:, 0, :], alpha[1], first_cols[:, 1, :], MULT)
+        nc.vector.scalar_tensor_tensor(second_cols[:, 1, :], alpha[1], 1.0, first_cols[:, 1, :], SUBTRACT, MULT)
+
+        nc.vector.tensor_copy(x_scale_rows[:], scale_table[:].indirect(picks[:]))
+        for q in range(P // QUADRANT):
+            first_row = P - BLOCKS + SCALE_ROWS * q
+            nc.sync.dma_start(
+                x_scale[QUADRANT * q : QUADRANT * q + SCALE_ROWS, :].bitcast(I32),
+                x_scale_rows[first_row : first_row + SCALE_ROWS, :].bitcast(I32),
             )
 
-        alpha = [turn_alpha(d, 2 + d) for d in range(D)]
-        round_w(slice(0, P))
-        nc.vector.tensor_scalar(through[:, 0, :], alpha[0], -1.0, 1.0, MULT, ADD)
-        nc.vector.tensor_copy(weight_cols[:, 0, :], alpha[0])
-        nc.vector.tensor_tensor(weight_cols[:, 1, :], alpha[1], through[:, 0, :], MULT)
-        nc.vector.scalar_tensor_tensor(through[:, 1, :], alpha[1], 1.0, through[:, 0, :], SUBTRACT, MULT)
-        w_codes = keep.tile([P, N], U32, name="w_codes", tag="op_table", align_bytes=64)
+        third_cols = placed.tile([P, CHUNKS], F32, name="third_cols", offset=W_BYTES + 64, align_bytes=64)
+        nc.vector.scalar_tensor_tensor(third_cols[:], alpha[2], -1.0, second_cols[:, 1, :], MULT, MULT)
+        weight_cols = [first_cols[:, 0, :], second_cols[:, 0, :], third_cols[:]]
+        for d in range(D):
+            spread(d, 5 + d)
+
+        w_codes = placed.tile([P, N], U32, name="w_codes", offset=W_BYTES + 128, align_bytes=64)
         w_scales = keep.tile([P, N], U8, name="w_scales", align_bytes=64)
         nc.vector.quantize_mx(
             out=w_codes[:].bitcast(FP8X4), scales=w_scales[:], in_=w_bf[:].rearrange("p t m j -> p (t m j)")
         )
-        nc.vector.scalar_tensor_tensor(weight_cols[:, 2, :], alpha[2], -1.0, through[:, 1, :], MULT, MULT)
-        for d in range(D):
-            nc.scalar.copy(weight_rows[:, d, :], spread(d, 5 + d))
 
-        x_words_picked = placed.tile([P, S], U32, name="x_words_picked", offset=64, align_bytes=64)
+        x_words_picked = placed.tile([P, S], U32, name="x_words_picked", offset=0, align_bytes=64)
         x_codes = [x_words_picked[:, h * HALF : (h + 1) * HALF] for h in range(2)]
         for h in range(2):
             entries = picks[:, h * HALF // GROUP : (h + 1) * HALF // GROUP]
@@ -222,7 +220,7 @@ def tile_picked_ysplat_sigmoid_po_kernel(
             scaled = keep.tile([P, V], F32, name=f"scaled{d}")
             for c in range(CHUNKS):
                 nc.scalar.activation(
-                    scaled[:, pixels(c)], turned[:, c, :], ACT.Copy, scale=weight_cols[:, d, c : c + 1]
+                    scaled[:, pixels(c)], turned[:, c, :], ACT.Copy, scale=weight_cols[d][:, c : c + 1]
                 )
             turn(back, scaled[:], d == 0, d == D - 1)
 

@@ -27,7 +27,7 @@ DIRECT = CHUNKS - 1
 PAIR = 2 * P
 HALF = S // 2
 SCALAR_TILE = PACK - 1
-PRODUCTS = [(0, 0), (0, 3), (1, 0), (1, 3), (0, 1), (1, 1), (0, 2), (1, 2)]
+PRODUCTS = [(0, 0), (0, 3), (0, 1), (1, 0), (1, 3), (1, 1), (0, 2), (1, 2)]
 W_BYTES = 2 * N * PACK
 
 
@@ -48,9 +48,9 @@ def tile_picked_ysplat_sigmoid_po_kernel(
 
         pos = [keep.tile([P, V // GROUP], U16, name=f"pos{d}") for d in range(D)]
         picks = keep.tile([P, S // GROUP], U16, name="picks")
-        w_raw = keep.tile([P, PACK, N], F32, name="w_raw")
+        w_raw = placed.tile([P, PACK, N], F32, name="w_raw", offset=W_BYTES, align_bytes=64)
         x_table = keep.tile([P, T], I32, name="x_table")
-        scale_table = placed.tile([P, T], U8, name="scale_table", offset=W_BYTES, align_bytes=64)
+        scale_table = keep.tile([P, T], U8, name="scale_table")
         op_table = keep.tile([P, S], F32, name="op_table")
         fall_rows = keep.tile([P, (D - 1) * V], F32, name="fall_rows")
         last_fall = keep.tile([P, V], F32, name="last_fall")
@@ -65,11 +65,11 @@ def tile_picked_ysplat_sigmoid_po_kernel(
             fall[: D - 1, 0:1, :].rearrange("d p v -> p d v"),
         )
         nc.sync.dma_start(pos[1][:], pos2)
-        nc.sync.dma_start(pos[2][:], pos3)
-        nc.sync.dma_start(last_fall[P - 1 :, :], fall[D - 1, 0:1, :])
-        nc.sync.dma_start(w_raw[:], w1.rearrange("(p j) c -> p j c", j=PACK))
         nc.sync.dma_start(picks[:], offs)
         nc.sync.dma_start(scale_table[P - BLOCKS :, :].bitcast(I32), x_scales[0].bitcast(I32))
+        nc.sync.dma_start(w_raw[:], w1.rearrange("(p j) c -> p j c", j=PACK))
+        nc.sync.dma_start(pos[2][:], pos3)
+        nc.sync.dma_start(last_fall[P - 1 :, :], fall[D - 1, 0:1, :])
         nc.sync.dma_start(x_table[:], x_words[0].rearrange("p n j -> p (n j)").bitcast(I32))
 
         warm = keep.tile([P, 2], F32, name="warm")
@@ -81,9 +81,12 @@ def tile_picked_ysplat_sigmoid_po_kernel(
             nc.vector.memset(table[: P - 1, width - 1 : width], 0.0)
         nc.gpsimd.memset(fall_rows[: P - 1, V:], 0.0)
         make_identity(nc, ident[:])
-        nc.gpsimd.memset(last_fall[: P - 1, :], 0.0)
+        steps = keep.tile([P, 2, CHUNKS], F32, name="steps")
+        for step in range(2):
+            nc.gpsimd.memset(steps[:, step, :], float(step))
         nc.gpsimd.memset(scale_table[: P - BLOCKS, :].bitcast(I32), 0)
         nc.gpsimd.memset(x_scale[:].bitcast(I32), 0)
+        nc.gpsimd.memset(last_fall[: P - 1, :], 0.0)
 
         alpha_rows = [keep.tile([P, V], F32, name=f"alpha_rows{d}") for d in range(D)]
         falloff = [fall_rows[:, 0:V], fall_rows[:, V:], last_fall[:]]
@@ -101,20 +104,10 @@ def tile_picked_ysplat_sigmoid_po_kernel(
                 nc.tensor.transpose(rows_of[:, c, :], weight_cols[d][:, c : c + 1].to_broadcast([P, P]), ident[:])
             nc.scalar.copy(weight_rows[:, d, :], rows_of[:].rearrange("p c v -> p (c v)"))
 
-        w_bf = placed.tile([P, PACK, P, PACK], BF16, name="w_bf", offset=0, align_bytes=64)
-        nc.scalar.copy(
-            w_bf[:].rearrange("p t m j -> p m j t"),
-            w_raw[:].rearrange("p j (m t) -> p m j t", t=PACK),
-        )
-        weight_rows = keep.tile([P, D, V], F32, name="weight_rows", tag="w_raw")
-
-        alpha = [alpha_columns(d, 2 + d) for d in range(D)]
+        alpha0 = alpha_columns(0, 2)
         first_cols = keep.tile([P, 2, CHUNKS], F32, name="first_cols")
-        second_cols = keep.tile([P, 2, CHUNKS], F32, name="second_cols", tag="last_fall")
-        nc.vector.tensor_scalar(first_cols[:, 1, :], alpha[0], -1.0, 1.0, MULT, ADD)
-        nc.vector.tensor_copy(first_cols[:, 0, :], alpha[0])
-        nc.vector.tensor_tensor(second_cols[:, 0, :], alpha[1], first_cols[:, 1, :], MULT)
-        nc.vector.scalar_tensor_tensor(second_cols[:, 1, :], alpha[1], 1.0, first_cols[:, 1, :], SUBTRACT, MULT)
+        nc.vector.tensor_tensor(first_cols[:], alpha0.unsqueeze(1).to_broadcast([P, 2, CHUNKS]), steps[:], SUBTRACT)
+        alpha1 = alpha_columns(1, 3)
 
         nc.vector.tensor_copy(x_scale_rows[:], scale_table[:].indirect(picks[:]))
         for q in range(P // QUADRANT):
@@ -124,17 +117,36 @@ def tile_picked_ysplat_sigmoid_po_kernel(
                 x_scale_rows[first_row : first_row + SCALE_ROWS, :].bitcast(I32),
             )
 
-        third_cols = placed.tile([P, CHUNKS], F32, name="third_cols", offset=W_BYTES + 64, align_bytes=64)
-        nc.vector.scalar_tensor_tensor(third_cols[:], alpha[2], -1.0, second_cols[:, 1, :], MULT, MULT)
-        weight_cols = [first_cols[:, 0, :], second_cols[:, 0, :], third_cols[:]]
-        for d in range(D):
-            spread(d, 5 + d)
+        w_bf = placed.tile([P, PACK, P, PACK], BF16, name="w_bf", offset=0, align_bytes=64)
+        nc.scalar.copy(
+            w_bf[:].rearrange("p t m j -> p m j t"),
+            w_raw[:].rearrange("p j (m t) -> p m j t", t=PACK),
+        )
+        weight_rows = placed.tile([P, D, V], F32, name="weight_rows", offset=W_BYTES, align_bytes=64)
+        behind_rows = W_BYTES + 4 * D * V
+        factors = placed.tile([P, 2, CHUNKS], F32, name="factors", offset=behind_rows, align_bytes=64)
+        nc.scalar.activation(factors[:, 0, :], alpha1, ACT.Copy, scale=-1.0)
+        nc.scalar.activation(factors[:, 1, :], alpha1, ACT.Copy, scale=-1.0, bias=1.0)
+        weight_cols = [first_cols[:, 0, :]]
+        spread(0, 5)
 
-        w_codes = placed.tile([P, N], U32, name="w_codes", offset=W_BYTES + 128, align_bytes=64)
+        alpha2 = alpha_columns(2, 4)
+        second_cols = keep.tile([P, 2, CHUNKS], F32, name="second_cols", tag="last_fall")
+        nc.vector.tensor_tensor(
+            second_cols[:], factors[:], first_cols[:, 1:2, :].to_broadcast([P, 2, CHUNKS]), MULT
+        )
+        weight_cols.append(second_cols[:, 0, :])
+        spread(1, 6)
+
+        w_codes = placed.tile([P, N], U32, name="w_codes", offset=behind_rows, align_bytes=64)
         w_scales = keep.tile([P, N], U8, name="w_scales", align_bytes=64)
         nc.vector.quantize_mx(
             out=w_codes[:].bitcast(FP8X4), scales=w_scales[:], in_=w_bf[:].rearrange("p t m j -> p (t m j)")
         )
+        third_cols = keep.tile([P, CHUNKS], F32, name="third_cols")
+        nc.vector.scalar_tensor_tensor(third_cols[:], alpha2, -1.0, second_cols[:, 1, :], MULT, MULT)
+        weight_cols.append(third_cols[:])
+        spread(2, 7)
 
         x_words_picked = placed.tile([P, S], U32, name="x_words_picked", offset=0, align_bytes=64)
         x_codes = [x_words_picked[:, h * HALF : (h + 1) * HALF] for h in range(2)]
@@ -177,37 +189,40 @@ def tile_picked_ysplat_sigmoid_po_kernel(
             nc.vector.tensor_tensor(values, rows[t][:].indirect(entries_of(d, span)), weight_rows[:, d, span], MULT)
 
         def turn(total, values, first, last):
-            for c in range(CHUNKS):
+            blocks = values.shape[1] // P
+            for c in range(blocks):
                 nc.tensor.matmul(
                     total[:, c, :],
                     lhsT=values[:, pixels(c)],
                     rhs=ident[:],
                     is_transpose=True,
                     start=first and c == 0,
-                    stop=last and c == CHUNKS - 1,
+                    stop=last and c == blocks - 1,
                 )
 
-        def flat(tile):
-            return tile[:].rearrange("p c n -> p (c n)")
+        def flat(tile, span):
+            return tile[:].rearrange("p c n -> p (c n)")[:, 0 : span.stop - span.start]
 
-        def sum_turned(t, number):
+        def sum_turned(t, span, number):
             total = bank(number)
-            layers = keep.tile([P, D, V], F32, name=f"layers{t}")
+            layers = keep.tile([P, D, span.stop - span.start], F32, name=f"layers{t}")
             for d in range(D):
-                fetch_on_vector(layers[:, d, :], t, d, whole)
+                fetch_on_vector(layers[:, d, :], t, d, span)
                 turn(total, layers[:, d, :], d == 0, d == D - 1)
             return total
 
-        def leave_and_turn_back(t, total, number):
-            sums = keep.tile([P, V], F32, name=f"sums{t}")
-            nc.scalar.copy(sums[:], flat(total))
+        def leave_and_turn_back(t, span, total, number):
+            sums = keep.tile([P, span.stop - span.start], F32, name=f"sums{t}")
+            nc.scalar.copy(sums[:], flat(total, span))
             back = bank(number)
             turn(back, sums[:], True, True)
             return back
 
-        def hand_out(t, back):
-            nc.scalar.copy(y[:, t, :], flat(back))
-            nc.scalar.dma_start(out_rows[:, t, :], y[:, t, :])
+        def hand_out(t, span, back):
+            nc.scalar.copy(y[:, t, span], flat(back, span))
+
+        def store(tiles, span):
+            nc.sync.dma_start(out_rows[:, tiles, span], y[:, tiles, span])
 
         def fetch_on_scalar(d, number):
             values = keep.tile([P, V], F32, name=f"values{d}")
@@ -219,9 +234,7 @@ def tile_picked_ysplat_sigmoid_po_kernel(
         def weigh(d, turned, back):
             scaled = keep.tile([P, V], F32, name=f"scaled{d}")
             for c in range(CHUNKS):
-                nc.scalar.activation(
-                    scaled[:, pixels(c)], turned[:, c, :], ACT.Copy, scale=weight_cols[d][:, c : c + 1]
-                )
+                nc.scalar.activation(scaled[:, pixels(c)], turned[:, c, :], ACT.Copy, scale=weight_cols[d][:, c : c + 1])
             turn(back, scaled[:], d == 0, d == D - 1)
 
         def round_y(copy, span):
@@ -238,41 +251,47 @@ def tile_picked_ysplat_sigmoid_po_kernel(
             )
             nc.sync.dma_start(out_words[:, span], y_codes[:, span].bitcast(I32))
 
+        low, high = slice(0, V // 2), slice(V // 2, V)
         for number in range(6):
             product(number)
-        total0 = sum_turned(0, 0)
+        total0 = sum_turned(0, whole, 0)
         turned0 = fetch_on_scalar(0, 1)
         product(6)
         product(7)
-        turned1 = fetch_on_scalar(1, 3)
-        total1 = sum_turned(1, 4)
+        turned1 = fetch_on_scalar(1, 4)
         back3 = bank(6)
         weigh(0, turned0, back3)
-        back0 = leave_and_turn_back(0, total0, 5)
-        turned2 = fetch_on_scalar(2, 2)
+        total1 = sum_turned(1, whole, 1)
+        back0 = leave_and_turn_back(0, whole, total0, 5)
+        turned2 = fetch_on_scalar(2, 3)
         weigh(1, turned1, back3)
-        hand_out(0, back0)
-        back1 = leave_and_turn_back(1, total1, 0)
+        hand_out(0, whole, back0)
+        store(slice(0, 1), whole)
+        total2 = sum_turned(2, low, 4)
+        back1 = leave_and_turn_back(1, whole, total1, 0)
         weigh(2, turned2, back3)
-        hand_out(1, back1)
-        hand_out(SCALAR_TILE, back3)
+        back2 = leave_and_turn_back(2, low, total2, 2)
+        hand_out(1, whole, back1)
+        store(slice(1, 2), whole)
+        hand_out(SCALAR_TILE, whole, back3)
+        hand_out(2, low, back2)
 
-        spans = [slice(0, 2 * P), pixels(2), pixels(3)]
-        layers = keep.tile([P, D, V], F32, name="layers2")
-        pair = keep.tile([P, V], F32, name="pair")
-        for span in spans:
-            fetch_on_vector(layers[:, 0, span], 2, 0, span)
-            fetch_on_vector(layers[:, 1, span], 2, 1, span)
-            fetch_on_vector(layers[:, 2, span], 2, 2, span)
-            nc.vector.tensor_tensor(pair[:, span], layers[:, 0, span], layers[:, 1, span], ADD)
-            nc.vector.tensor_tensor(y[:, 2, span], pair[:, span], layers[:, 2, span], ADD)
-            nc.sync.dma_start(out_rows[:, 2, span], y[:, 2, span])
+        layers = keep.tile([P, D, V // 2], F32, name="direct")
+        pair = keep.tile([P, V // 2], F32, name="pair")
+        for d in range(D):
+            fetch_on_vector(layers[:, d, :], 2, d, high)
+        for c in range(2):
+            nc.vector.tensor_tensor(pair[:, pixels(c)], layers[:, 0, pixels(c)], layers[:, 1, pixels(c)], ADD)
+        for c in range(2):
+            nc.vector.tensor_tensor(y[:, 2, pixels(2 + c)], pair[:, pixels(c)], layers[:, 2, pixels(c)], ADD)
+        store(slice(2, PACK), high)
+        store(slice(2, PACK), low)
 
-        round_y(nc.scalar.copy, spans[0])
-        round_y(nc.scalar.copy, spans[1])
-        round_y(nc.vector.tensor_copy, spans[2])
-        for span in (spans[0], spans[2], spans[1]):
-            quantise(span)
+        round_y(nc.scalar.copy, low)
+        for c in range(2):
+            round_y(nc.vector.tensor_copy, pixels(2 + c))
+        quantise(low)
+        quantise(high)
 
         for q in range(P // QUADRANT):
             queue = nc.scalar if q % 2 else nc.sync

@@ -64,9 +64,9 @@ def tile_picked_ysplat_sigmoid_po_kernel(
             fall_rows[P - 1 :, :].rearrange("p (d v) -> p d v", d=D - 1),
             fall[: D - 1, 0:1, :].rearrange("d p v -> p d v"),
         )
+        nc.sync.dma_start(scale_table[P - BLOCKS :, :].bitcast(I32), x_scales[0].bitcast(I32))
         nc.sync.dma_start(pos[1][:], pos2)
         nc.sync.dma_start(picks[:], offs)
-        nc.sync.dma_start(scale_table[P - BLOCKS :, :].bitcast(I32), x_scales[0].bitcast(I32))
         nc.sync.dma_start(w_raw[:], w1.rearrange("(p j) c -> p j c", j=PACK))
         nc.sync.dma_start(pos[2][:], pos3)
         nc.sync.dma_start(last_fall[P - 1 :, :], fall[D - 1, 0:1, :])
@@ -267,29 +267,37 @@ def tile_picked_ysplat_sigmoid_po_kernel(
         weigh(1, turned1, back3)
         hand_out(0, whole, back0)
         store(slice(0, 1), whole)
-        total2 = sum_turned(2, low, 4)
         back1 = leave_and_turn_back(1, whole, total1, 0)
         weigh(2, turned2, back3)
-        back2 = leave_and_turn_back(2, low, total2, 2)
         hand_out(1, whole, back1)
         store(slice(1, 2), whole)
         hand_out(SCALAR_TILE, whole, back3)
-        hand_out(2, low, back2)
 
-        layers = keep.tile([P, D, V // 2], F32, name="direct")
-        pair = keep.tile([P, V // 2], F32, name="pair")
+        layers = keep.tile([P, D, V], F32, name="direct")
+        pair = keep.tile([P, V], F32, name="pair")
+
+        def add_pair(span):
+            nc.vector.tensor_tensor(pair[:, span], layers[:, 0, span], layers[:, 1, span], ADD)
+
+        def add_last(span):
+            nc.vector.tensor_tensor(y[:, 2, span], pair[:, span], layers[:, 2, span], ADD)
+
         for d in range(D):
-            fetch_on_vector(layers[:, d, :], 2, d, high)
-        for c in range(2):
-            nc.vector.tensor_tensor(pair[:, pixels(c)], layers[:, 0, pixels(c)], layers[:, 1, pixels(c)], ADD)
-        for c in range(2):
-            nc.vector.tensor_tensor(y[:, 2, pixels(2 + c)], pair[:, pixels(c)], layers[:, 2, pixels(c)], ADD)
-        store(slice(2, PACK), high)
+            fetch_on_vector(layers[:, d, low], 2, d, low)
+        add_pair(low)
+        fetch_on_vector(layers[:, 0, high], 2, 0, high)
+        add_last(low)
         store(slice(2, PACK), low)
+        for d in range(1, D):
+            fetch_on_vector(layers[:, d, high], 2, d, high)
+        for step in (add_pair, add_last):
+            for c in (2, 3):
+                step(pixels(c))
+        store(slice(2, PACK), high)
 
         round_y(nc.scalar.copy, low)
-        for c in range(2):
-            round_y(nc.vector.tensor_copy, pixels(2 + c))
+        round_y(nc.scalar.copy, pixels(2))
+        round_y(nc.vector.tensor_copy, pixels(3))
         quantise(low)
         quantise(high)
 

@@ -256,13 +256,13 @@ def tile_picked_ysplat_sigmoid_po_kernel(
             product(number)
         total0 = sum_turned(0, whole, 0)
         turned0 = fetch_on_scalar(0, 1)
-        product(6)
-        product(7)
         turned1 = fetch_on_scalar(1, 4)
-        back3 = bank(6)
+        back3 = bank(2)
         weigh(0, turned0, back3)
-        total1 = sum_turned(1, whole, 1)
+        product(6)
         back0 = leave_and_turn_back(0, whole, total0, 5)
+        product(7)
+        total1 = sum_turned(1, whole, 1)
         turned2 = fetch_on_scalar(2, 3)
         weigh(1, turned1, back3)
         hand_out(0, whole, back0)

@@ -48,12 +48,12 @@ def tile_picked_ysplat_sigmoid_po_kernel(
 
         pos = [keep.tile([P, V // GROUP], U16, name=f"pos{d}") for d in range(D)]
         picks = keep.tile([P, S // GROUP], U16, name="picks")
-        w_raw = placed.tile([P, PACK, N], F32, name="w_raw", offset=W_BYTES, align_bytes=64)
+        w_raw = placed.tile([P, PACK, N], F32, name="w_raw", offset=W_BYTES + 64, align_bytes=64)
         x_table = keep.tile([P, T], I32, name="x_table")
         scale_table = keep.tile([P, T], U8, name="scale_table")
         op_table = keep.tile([P, S], F32, name="op_table")
         fall_rows = keep.tile([P, (D - 1) * V], F32, name="fall_rows")
-        last_fall = keep.tile([P, V], F32, name="last_fall")
+        last_fall = keep.tile([P, V], F32, name="last_fall", align_bytes=64)
         ident = keep.tile([P, P], F32, name="ident")
         x_scale_rows = keep.tile([P, S], U8, name="x_scale_rows")
         x_scale = keep.tile([P, S], U8, name="x_scale", align_bytes=64)
@@ -122,33 +122,31 @@ def tile_picked_ysplat_sigmoid_po_kernel(
             w_bf[:].rearrange("p t m j -> p m j t"),
             w_raw[:].rearrange("p j (m t) -> p m j t", t=PACK),
         )
-        weight_rows = placed.tile([P, D, V], F32, name="weight_rows", offset=W_BYTES, align_bytes=64)
-        behind_rows = W_BYTES + 4 * D * V
-        factors = placed.tile([P, 2, CHUNKS], F32, name="factors", offset=behind_rows, align_bytes=64)
-        nc.scalar.activation(factors[:, 0, :], alpha1, ACT.Copy, scale=-1.0)
-        nc.scalar.activation(factors[:, 1, :], alpha1, ACT.Copy, scale=-1.0, bias=1.0)
+        weight_rows = placed.tile([P, D, V], F32, name="weight_rows", offset=W_BYTES + 64, align_bytes=64)
         weight_cols = [first_cols[:, 0, :]]
         spread(0, 5)
 
-        alpha2 = alpha_columns(2, 4)
-        second_cols = keep.tile([P, 2, CHUNKS], F32, name="second_cols", tag="last_fall")
+        factors = keep.tile([P, 2, CHUNKS], F32, name="factors")
+        nc.vector.tensor_tensor(factors[:], steps[:], alpha1.unsqueeze(1).to_broadcast([P, 2, CHUNKS]), SUBTRACT)
+        second_cols = keep.tile([P, 2, CHUNKS], F32, name="second_cols")
         nc.vector.tensor_tensor(
             second_cols[:], factors[:], first_cols[:, 1:2, :].to_broadcast([P, 2, CHUNKS]), MULT
         )
         weight_cols.append(second_cols[:, 0, :])
+        alpha2 = alpha_columns(2, 4)
         spread(1, 6)
 
-        w_codes = placed.tile([P, N], U32, name="w_codes", offset=behind_rows, align_bytes=64)
+        w_codes = keep.tile([P, N], U32, name="w_codes", tag="last_fall", align_bytes=64)
         w_scales = keep.tile([P, N], U8, name="w_scales", align_bytes=64)
         nc.vector.quantize_mx(
             out=w_codes[:].bitcast(FP8X4), scales=w_scales[:], in_=w_bf[:].rearrange("p t m j -> p (t m j)")
         )
-        third_cols = keep.tile([P, CHUNKS], F32, name="third_cols")
+        third_cols = placed.tile([P, CHUNKS], F32, name="third_cols", offset=0, align_bytes=64)
         nc.vector.scalar_tensor_tensor(third_cols[:], alpha2, -1.0, second_cols[:, 1, :], MULT, MULT)
         weight_cols.append(third_cols[:])
         spread(2, 7)
 
-        x_words_picked = placed.tile([P, S], U32, name="x_words_picked", offset=0, align_bytes=64)
+        x_words_picked = placed.tile([P, S], U32, name="x_words_picked", offset=64, align_bytes=64)
         x_codes = [x_words_picked[:, h * HALF : (h + 1) * HALF] for h in range(2)]
         for h in range(2):
             entries = picks[:, h * HALF // GROUP : (h + 1) * HALF // GROUP]

@@ -27,7 +27,7 @@ DIRECT = CHUNKS - 1
 PAIR = 2 * P
 HALF = S // 2
 SCALAR_TILE = PACK - 1
-PRODUCTS = [(0, 0), (0, 3), (0, 1), (1, 0), (1, 3), (1, 1), (0, 2), (1, 2)]
+PRODUCTS = [(0, 0), (0, 3), (1, 0), (1, 3), (0, 1), (1, 1), (0, 2), (1, 2)]
 W_BYTES = 2 * N * PACK
 
 
@@ -254,14 +254,14 @@ def tile_picked_ysplat_sigmoid_po_kernel(
             product(number)
         total0 = sum_turned(0, whole, 0)
         turned0 = fetch_on_scalar(0, 1)
-        turned1 = fetch_on_scalar(1, 4)
+        turned1 = fetch_on_scalar(1, 3)
         back3 = bank(2)
         weigh(0, turned0, back3)
         product(6)
         back0 = leave_and_turn_back(0, whole, total0, 5)
         product(7)
         total1 = sum_turned(1, whole, 1)
-        turned2 = fetch_on_scalar(2, 3)
+        turned2 = fetch_on_scalar(2, 4)
         weigh(1, turned1, back3)
         hand_out(0, whole, back0)
         store(slice(0, 1), whole)
@@ -294,8 +294,8 @@ def tile_picked_ysplat_sigmoid_po_kernel(
         store(slice(2, PACK), high)
 
         round_y(nc.scalar.copy, low)
-        round_y(nc.scalar.copy, pixels(2))
-        round_y(nc.vector.tensor_copy, pixels(3))
+        round_y(nc.scalar.copy, pixels(3))
+        round_y(nc.vector.tensor_copy, pixels(2))
         quantise(low)
         quantise(high)
 

@@ -23,12 +23,11 @@ QUADRANT = 32
 SCALE_ROWS = 4
 BLOCKS = K // 32
 CHUNKS = V // P
-DIRECT = CHUNKS - 1
-PAIR = 2 * P
 HALF = S // 2
-SCALAR_TILE = PACK - 1
-PRODUCTS = [(0, 0), (0, 3), (1, 0), (1, 3), (0, 1), (1, 1), (0, 2), (1, 2)]
-W_BYTES = 2 * N * PACK
+FIRST, SECOND, ON_SCALAR, LAST = range(PACK)
+SLOT = {FIRST: 0, ON_SCALAR: 1, LAST: 2, SECOND: 3}
+PRODUCT_BANK = {FIRST: 0, ON_SCALAR: 2, SECOND: 4, LAST: 6}
+FALL_PIECES = D * CHUNKS
 
 
 def tile_picked_ysplat_sigmoid_po_kernel(
@@ -37,7 +36,6 @@ def tile_picked_ysplat_sigmoid_po_kernel(
     nc = tc.nc
     with ExitStack() as ctx:
         keep = ctx.enter_context(tc.tile_pool(name="keep", bufs=1))
-        placed = ctx.enter_context(tc.tile_pool(name="placed", bufs=1))
         psum = ctx.enter_context(tc.psum_pool(name="psum", bufs=1))
 
         def bank(number):
@@ -48,66 +46,43 @@ def tile_picked_ysplat_sigmoid_po_kernel(
 
         pos = [keep.tile([P, V // GROUP], U16, name=f"pos{d}") for d in range(D)]
         picks = keep.tile([P, S // GROUP], U16, name="picks")
-        w_raw = placed.tile([P, PACK, N], F32, name="w_raw", offset=W_BYTES + 64, align_bytes=64)
+        w_raw = [keep.tile([P, PACK, N // 2], F32, name=f"w_raw{half}") for half in range(2)]
         x_table = keep.tile([P, T], I32, name="x_table")
         scale_table = keep.tile([P, T], U8, name="scale_table")
         op_table = keep.tile([P, S], F32, name="op_table")
-        fall_rows = keep.tile([P, (D - 1) * V], F32, name="fall_rows")
-        last_fall = keep.tile([P, V], F32, name="last_fall", align_bytes=64)
+        fall_rows = keep.tile([P, P], F32, name="fall_rows")
         ident = keep.tile([P, P], F32, name="ident")
         x_scale_rows = keep.tile([P, S], U8, name="x_scale_rows")
         x_scale = keep.tile([P, S], U8, name="x_scale", align_bytes=64)
 
-        nc.sync.dma_start(pos[0][:], pos1)
-        nc.sync.dma_start(op_table[P - 1 :, :], op[0:1, :])
-        nc.sync.dma_start(
-            fall_rows[P - 1 :, :].rearrange("p (d v) -> p d v", d=D - 1),
-            fall[: D - 1, 0:1, :].rearrange("d p v -> p d v"),
-        )
-        nc.sync.dma_start(scale_table[P - BLOCKS :, :].bitcast(I32), x_scales[0].bitcast(I32))
-        nc.sync.dma_start(pos[1][:], pos2)
+        x_source = x_words[0].rearrange("p n j -> p (n j)").bitcast(I32)
+        fall_pieces = fall.rearrange("d p (c v) -> (d p c) v", v=P)[0 : D * P * CHUNKS : P + 1, :]
+        first_piece = P - FALL_PIECES
         nc.sync.dma_start(picks[:], offs)
-        nc.sync.dma_start(w_raw[:], w1.rearrange("(p j) c -> p j c", j=PACK))
+        nc.sync.dma_start(scale_table[P - BLOCKS :, :].bitcast(I32), x_scales[0].bitcast(I32))
+        nc.sync.dma_start(op_table[P - 1 :, :], op[0:1, :])
+        nc.sync.dma_start(pos[0][:], pos1)
+        nc.sync.dma_start(pos[1][:], pos2)
+        nc.sync.dma_start(fall_rows[first_piece : first_piece + 8, :], fall_pieces[0:8, :])
+        nc.sync.dma_start(fall_rows[first_piece + 8 :, :], fall_pieces[8:, :])
+        nc.sync.dma_start(x_table[:, : T // 2], x_source[:, : T // 2])
         nc.sync.dma_start(pos[2][:], pos3)
-        nc.sync.dma_start(last_fall[P - 1 :, :], fall[D - 1, 0:1, :])
-        nc.sync.dma_start(x_table[:], x_words[0].rearrange("p n j -> p (n j)").bitcast(I32))
+        nc.sync.dma_start(x_table[:, T // 2 :], x_source[:, T // 2 :])
+        for half in range(2):
+            w_cols = slice(half * N // 2, (half + 1) * N // 2)
+            nc.sync.dma_start(w_raw[half][:], w1.rearrange("(p j) c -> p j c", j=PACK)[:, :, w_cols])
 
         warm = keep.tile([P, 2], F32, name="warm")
         nc.vector.memset(warm[:, 0:1], 0.0)
         nc.scalar.activation(warm[:, 1:2], warm[:, 0:1], ACT.Sigmoid)
 
-        for table, width in ((op_table, S), (fall_rows, V)):
-            nc.vector.memset(table[: P - 1, 0 : width - 1], 0.0)
-            nc.vector.memset(table[: P - 1, width - 1 : width], 0.0)
-        nc.gpsimd.memset(fall_rows[: P - 1, V:], 0.0)
+        for table, rows_free in ((scale_table[:].bitcast(I32), P - BLOCKS), (fall_rows[:], first_piece)):
+            width = table.shape[1]
+            nc.vector.memset(table[:rows_free, 0 : width - 1], 0)
+            nc.vector.memset(table[:rows_free, width - 1 : width], 0)
+        nc.gpsimd.memset(op_table[: P - 1, :], 0.0)
         make_identity(nc, ident[:])
-        steps = keep.tile([P, 2, CHUNKS], F32, name="steps")
-        for step in range(2):
-            nc.gpsimd.memset(steps[:, step, :], float(step))
-        nc.gpsimd.memset(scale_table[: P - BLOCKS, :].bitcast(I32), 0)
         nc.gpsimd.memset(x_scale[:].bitcast(I32), 0)
-        nc.gpsimd.memset(last_fall[: P - 1, :], 0.0)
-
-        alpha_rows = [keep.tile([P, V], F32, name=f"alpha_rows{d}") for d in range(D)]
-        falloff = [fall_rows[:, 0:V], fall_rows[:, V:], last_fall[:]]
-
-        def alpha_columns(d, number):
-            nc.vector.tensor_tensor(alpha_rows[d][:], op_table[:].indirect(pos[d][:]), falloff[d], MULT)
-            turned = bank(number)
-            for c in range(CHUNKS):
-                nc.tensor.transpose(turned[:, c, :], alpha_rows[d][:, pixels(c)], ident[:])
-            return turned[:, :, P - 1]
-
-        def spread(d, number):
-            rows_of = bank(number)
-            for c in range(CHUNKS):
-                nc.tensor.transpose(rows_of[:, c, :], weight_cols[d][:, c : c + 1].to_broadcast([P, P]), ident[:])
-            nc.scalar.copy(weight_rows[:, d, :], rows_of[:].rearrange("p c v -> p (c v)"))
-
-        alpha0 = alpha_columns(0, 2)
-        first_cols = keep.tile([P, 2, CHUNKS], F32, name="first_cols")
-        nc.vector.tensor_tensor(first_cols[:], alpha0.unsqueeze(1).to_broadcast([P, 2, CHUNKS]), steps[:], SUBTRACT)
-        alpha1 = alpha_columns(1, 3)
 
         nc.vector.tensor_copy(x_scale_rows[:], scale_table[:].indirect(picks[:]))
         for q in range(P // QUADRANT):
@@ -117,60 +92,90 @@ def tile_picked_ysplat_sigmoid_po_kernel(
                 x_scale_rows[first_row : first_row + SCALE_ROWS, :].bitcast(I32),
             )
 
-        w_bf = placed.tile([P, PACK, P, PACK], BF16, name="w_bf", offset=0, align_bytes=64)
-        nc.scalar.copy(
-            w_bf[:].rearrange("p t m j -> p m j t"),
-            w_raw[:].rearrange("p j (m t) -> p m j t", t=PACK),
-        )
-        weight_rows = placed.tile([P, D, V], F32, name="weight_rows", offset=W_BYTES + 64, align_bytes=64)
-        weight_cols = [first_cols[:, 0, :]]
-        spread(0, 5)
+        fall_turned = bank(7)
+        nc.tensor.transpose(fall_turned[:, 0, :], fall_rows[:], ident[:])
+        fall_cols = keep.tile([P, D, CHUNKS], F32, name="fall_cols")
+        nc.vector.tensor_copy(fall_cols[:].rearrange("p d c -> p (d c)"), fall_turned[:, 0, first_piece:])
 
-        factors = keep.tile([P, 2, CHUNKS], F32, name="factors")
-        nc.vector.tensor_tensor(factors[:], steps[:], alpha1.unsqueeze(1).to_broadcast([P, 2, CHUNKS]), SUBTRACT)
-        second_cols = keep.tile([P, 2, CHUNKS], F32, name="second_cols")
-        nc.vector.tensor_tensor(
-            second_cols[:], factors[:], first_cols[:, 1:2, :].to_broadcast([P, 2, CHUNKS]), MULT
-        )
-        weight_cols.append(second_cols[:, 0, :])
-        alpha2 = alpha_columns(2, 4)
-        spread(1, 6)
+        def opacity_columns(d, number):
+            looked_up = keep.tile([P, V], F32, name=f"opacity{d}")
+            nc.scalar.activation(looked_up[:], op_table[:].indirect(pos[d][:]), ACT.Copy)
+            turned = bank(number)
+            for c in range(CHUNKS):
+                nc.tensor.transpose(turned[:, c, :], looked_up[:, pixels(c)], ident[:])
+            return turned[:, :, P - 1]
 
-        w_codes = keep.tile([P, N], U32, name="w_codes", tag="last_fall", align_bytes=64)
-        w_scales = keep.tile([P, N], U8, name="w_scales", align_bytes=64)
-        nc.vector.quantize_mx(
-            out=w_codes[:].bitcast(FP8X4), scales=w_scales[:], in_=w_bf[:].rearrange("p t m j -> p (t m j)")
-        )
-        third_cols = placed.tile([P, CHUNKS], F32, name="third_cols", offset=0, align_bytes=64)
-        nc.vector.scalar_tensor_tensor(third_cols[:], alpha2, -1.0, second_cols[:, 1, :], MULT, MULT)
-        weight_cols.append(third_cols[:])
-        spread(2, 7)
+        weight_cols = [keep.tile([P, CHUNKS], F32, name=f"weight_cols{d}") for d in range(D)]
+        weight_rows = keep.tile([P, D, V], F32, name="weight_rows")
 
-        x_words_picked = placed.tile([P, S], U32, name="x_words_picked", offset=64, align_bytes=64)
-        x_codes = [x_words_picked[:, h * HALF : (h + 1) * HALF] for h in range(2)]
+        def spread(d, number):
+            rows_of = bank(number)
+            for c in range(CHUNKS):
+                nc.tensor.transpose(rows_of[:, c, :], weight_cols[d][:, c : c + 1].to_broadcast([P, P]), ident[:])
+            nc.scalar.copy(weight_rows[:, d, :], rows_of[:].rearrange("p c v -> p (c v)"))
+
+        opacity = [opacity_columns(d, d) for d in range(D)]
+        nc.vector.tensor_tensor(weight_cols[0][:], opacity[0], fall_cols[:, 0, :], MULT)
+        behind0 = keep.tile([P, CHUNKS], F32, name="behind0")
+        nc.vector.scalar_tensor_tensor(behind0[:], weight_cols[0][:], 1.0, fall_cols[:, 1, :], SUBTRACT, MULT)
+        spread(0, 3)
+        nc.vector.scalar_tensor_tensor(weight_cols[1][:], opacity[1], -1.0, behind0[:], MULT, MULT)
+        seen = keep.tile([P, CHUNKS], F32, name="seen")
+        nc.vector.scalar_tensor_tensor(seen[:], weight_cols[0][:], 1.0, weight_cols[1][:], SUBTRACT, ADD)
+        behind1 = keep.tile([P, CHUNKS], F32, name="behind1")
+        nc.vector.tensor_tensor(behind1[:], seen[:], fall_cols[:, 2, :], MULT)
+        spread(1, 4)
+        nc.vector.scalar_tensor_tensor(weight_cols[2][:], opacity[2], -1.0, behind1[:], MULT, MULT)
+        spread(2, 5)
+
+        x_codes = keep.tile([P, S], U32, name="x_codes", align_bytes=64)
         for h in range(2):
             entries = picks[:, h * HALF // GROUP : (h + 1) * HALF // GROUP]
-            nc.vector.tensor_copy(x_codes[h], x_table[:].bitcast(U32).indirect(entries))
+            nc.vector.tensor_copy(x_codes[:, h * HALF : (h + 1) * HALF], x_table[:].bitcast(U32).indirect(entries))
+
+        w_bf = keep.tile([P, N, PACK], BF16, name="w_bf", align_bytes=64)
+        w_codes = keep.tile([P, N], U32, name="w_codes", align_bytes=64)
+        w_scales = keep.tile([P, N], U8, name="w_scales", align_bytes=64)
+
+        def round_w(copy, half, pair_of_t):
+            source = w_raw[half][:].rearrange("p j (m t) -> p m j t", t=PACK)[:, :, :, 2 * pair_of_t : 2 * pair_of_t + 2]
+            if pair_of_t == 0:
+                target = w_bf[:, pixels(SLOT[half]), :].rearrange("p (t m) j -> p m j t", t=2)
+            else:
+                both = w_bf[:, SLOT[ON_SCALAR] * P : (SLOT[LAST] + 1) * P, :].rearrange("p (t m) j -> p m j t", t=2)
+                target = both[:, half * P // 2 : (half + 1) * P // 2, :, :]
+            copy(target, source)
+
+        def quantise_w(t, count):
+            cols = slice(SLOT[t] * P, (SLOT[t] + count) * P)
+            nc.vector.quantize_mx(
+                out=w_codes[:, cols].bitcast(FP8X4), scales=w_scales[:, cols], in_=w_bf[:, cols, :].rearrange("p m j -> p (m j)")
+            )
+
+        round_w(nc.scalar.copy, 0, 0)
+        round_w(nc.scalar.copy, 0, 1)
+        quantise_w(FIRST, 1)
+        round_w(nc.vector.tensor_copy, 1, 1)
+        round_w(nc.vector.tensor_copy, 1, 0)
+        quantise_w(ON_SCALAR, 2)
+        quantise_w(SECOND, 1)
 
         rows = [keep.tile([P, S], F32, name=f"rows{t}") for t in range(PACK)]
 
-        def product(number):
-            h, t = PRODUCTS[number]
-            cols = slice(h * HALF, (h + 1) * HALF)
-            acc = bank(number)[:].rearrange("p c n -> p (c n)")
-            nc.tensor.matmul_mx(
-                out=acc,
-                lhsT=w_codes[:, t * P : (t + 1) * P].bitcast(FP8X4),
-                lhsT_scale=w_scales[:, t * P : (t + 1) * P],
-                rhs=x_codes[h].bitcast(FP8X4),
-                rhs_scale=x_scale[:, cols],
-                start=True,
-                stop=True,
-            )
-            if t != SCALAR_TILE:
+        def features(t):
+            for h in range(2):
+                cols = slice(h * HALF, (h + 1) * HALF)
+                acc = bank(PRODUCT_BANK[t] + h)[:].rearrange("p c n -> p (c n)")
+                nc.tensor.matmul_mx(
+                    out=acc,
+                    lhsT=w_codes[:, pixels(SLOT[t])].bitcast(FP8X4),
+                    lhsT_scale=w_scales[:, pixels(SLOT[t])],
+                    rhs=x_codes[:, cols].bitcast(FP8X4),
+                    rhs_scale=x_scale[:, cols],
+                    start=True,
+                    stop=True,
+                )
                 nc.scalar.activation(rows[t][:, cols], acc, ACT.Sigmoid)
-            else:
-                nc.vector.tensor_copy(rows[t][:, cols], acc)
 
         y = keep.tile([P, PACK, V], F32, name="y")
         y_bf = keep.tile([P, V, PACK], BF16, name="y_bf", align_bytes=64)
@@ -198,42 +203,49 @@ def tile_picked_ysplat_sigmoid_po_kernel(
                     stop=last and c == blocks - 1,
                 )
 
-        def flat(tile, span):
-            return tile[:].rearrange("p c n -> p (c n)")[:, 0 : span.stop - span.start]
+        def flat(tile):
+            return tile[:].rearrange("p c n -> p (c n)")
 
-        def sum_turned(t, span, number):
+        def sum_turned(t, number):
             total = bank(number)
-            layers = keep.tile([P, D, span.stop - span.start], F32, name=f"layers{t}")
+            layers = keep.tile([P, D, V], F32, name=f"layers{t}")
             for d in range(D):
-                fetch_on_vector(layers[:, d, :], t, d, span)
+                fetch_on_vector(layers[:, d, :], t, d, whole)
                 turn(total, layers[:, d, :], d == 0, d == D - 1)
             return total
 
-        def leave_and_turn_back(t, span, total, number):
-            sums = keep.tile([P, span.stop - span.start], F32, name=f"sums{t}")
-            nc.scalar.copy(sums[:], flat(total, span))
-            back = bank(number)
-            turn(back, sums[:], True, True)
-            return back
+        sums = keep.tile([P, 2, CHUNKS, P], F32, name="sums")
 
-        def hand_out(t, span, back):
-            nc.scalar.copy(y[:, t, span], flat(back, span))
+        def leave(half, total):
+            nc.scalar.copy(
+                sums[:, :, :, half * P // 2 : (half + 1) * P // 2].rearrange("v t c m -> v c t m"),
+                total[:].rearrange("v c (t m) -> v c t m", t=2),
+            )
+
+        def turn_back(t, number):
+            back = bank(number)
+            turn(back, sums[:, t, :, :].rearrange("v c p -> v (c p)"), True, True)
+            return back
 
         def store(tiles, span):
             nc.sync.dma_start(out_rows[:, tiles, span], y[:, tiles, span])
 
+        def hand_out(t, span, source):
+            nc.scalar.copy(y[:, t, span], source)
+
         def fetch_on_scalar(d, number):
             values = keep.tile([P, V], F32, name=f"values{d}")
-            nc.scalar.activation(values[:], rows[SCALAR_TILE][:].indirect(pos[d][:]), ACT.Sigmoid)
+            nc.scalar.activation(values[:], rows[ON_SCALAR][:].indirect(pos[d][:]), ACT.Copy)
             turned = bank(number)
             turn(turned, values[:], True, True)
             return turned
 
-        def weigh(d, turned, back):
-            scaled = keep.tile([P, V], F32, name=f"scaled{d}")
-            for c in range(CHUNKS):
-                nc.scalar.activation(scaled[:, pixels(c)], turned[:, c, :], ACT.Copy, scale=weight_cols[d][:, c : c + 1])
-            turn(back, scaled[:], d == 0, d == D - 1)
+        scaled = keep.tile([P, D, V], F32, name="scaled")
+
+        def weigh(d, span, turned, back):
+            for c in range(span.start // P, span.stop // P):
+                nc.scalar.activation(scaled[:, d, pixels(c)], turned[:, c, :], ACT.Copy, scale=weight_cols[d][:, c : c + 1])
+            turn(back, scaled[:, d, span], d == 0, d == D - 1)
 
         def round_y(copy, span):
             copy(
@@ -250,26 +262,28 @@ def tile_picked_ysplat_sigmoid_po_kernel(
             nc.sync.dma_start(out_words[:, span], y_codes[:, span].bitcast(I32))
 
         low, high = slice(0, V // 2), slice(V // 2, V)
-        for number in range(6):
-            product(number)
-        total0 = sum_turned(0, whole, 0)
+        for t in (FIRST, ON_SCALAR, SECOND):
+            features(t)
+        total_first = sum_turned(FIRST, 0)
         turned0 = fetch_on_scalar(0, 1)
-        turned1 = fetch_on_scalar(1, 3)
-        back3 = bank(2)
-        weigh(0, turned0, back3)
-        product(6)
-        back0 = leave_and_turn_back(0, whole, total0, 5)
-        product(7)
-        total1 = sum_turned(1, whole, 1)
-        turned2 = fetch_on_scalar(2, 4)
-        weigh(1, turned1, back3)
-        hand_out(0, whole, back0)
-        store(slice(0, 1), whole)
-        back1 = leave_and_turn_back(1, whole, total1, 0)
-        weigh(2, turned2, back3)
-        hand_out(1, whole, back1)
-        store(slice(1, 2), whole)
-        hand_out(SCALAR_TILE, whole, back3)
+        turned1 = fetch_on_scalar(1, 2)
+        leave(0, total_first)
+        features(LAST)
+        total_second = sum_turned(SECOND, 5)
+        back_low, back_high = bank(3), bank(6)
+        weigh(0, low, turned0, back_low)
+        weigh(0, high, turned0, back_high)
+        turned2 = fetch_on_scalar(2, 0)
+        leave(1, total_second)
+        backs = [turn_back(0, 4), turn_back(1, 1)]
+        for span, back in ((low, back_low), (high, back_high)):
+            weigh(1, span, turned1, back)
+            weigh(2, span, turned2, back)
+            if span == low:
+                for t in range(2):
+                    hand_out(t, whole, flat(backs[t]))
+                store(slice(0, 2), whole)
+            hand_out(ON_SCALAR, span, flat(back)[:, low])
 
         layers = keep.tile([P, D, V], F32, name="direct")
         pair = keep.tile([P, V], F32, name="pair")
@@ -278,25 +292,23 @@ def tile_picked_ysplat_sigmoid_po_kernel(
             nc.vector.tensor_tensor(pair[:, span], layers[:, 0, span], layers[:, 1, span], ADD)
 
         def add_last(span):
-            nc.vector.tensor_tensor(y[:, 2, span], pair[:, span], layers[:, 2, span], ADD)
+            nc.vector.tensor_tensor(y[:, LAST, span], pair[:, span], layers[:, 2, span], ADD)
 
         for d in range(D):
-            fetch_on_vector(layers[:, d, low], 2, d, low)
+            fetch_on_vector(layers[:, d, low], LAST, d, low)
         add_pair(low)
-        fetch_on_vector(layers[:, 0, high], 2, 0, high)
+        fetch_on_vector(layers[:, 0, high], LAST, 0, high)
         add_last(low)
-        store(slice(2, PACK), low)
+        store(slice(ON_SCALAR, PACK), low)
         for d in range(1, D):
-            fetch_on_vector(layers[:, d, high], 2, d, high)
-        for step in (add_pair, add_last):
-            for c in (2, 3):
-                step(pixels(c))
-        store(slice(2, PACK), high)
-
-        round_y(nc.scalar.copy, low)
+            fetch_on_vector(layers[:, d, high], LAST, d, high)
+        add_pair(high)
+        round_y(nc.vector.tensor_copy, low)
+        add_last(high)
+        store(slice(ON_SCALAR, PACK), high)
+        quantise(low)
         round_y(nc.scalar.copy, pixels(3))
         round_y(nc.vector.tensor_copy, pixels(2))
-        quantise(low)
         quantise(high)
 
         for q in range(P // QUADRANT):

@@ -28,6 +28,8 @@ FIRST, SECOND, ON_SCALAR, LAST = range(PACK)
 SLOT = {FIRST: 0, ON_SCALAR: 1, LAST: 2, SECOND: 3}
 PRODUCT_BANK = {FIRST: 0, ON_SCALAR: 2, SECOND: 4, LAST: 6}
 FALL_PIECES = D * CHUNKS
+HALF_W_BYTES = 4 * PACK * N // 2
+X_AHEAD = 3 * T // 8
 
 
 def tile_picked_ysplat_sigmoid_po_kernel(
@@ -36,6 +38,7 @@ def tile_picked_ysplat_sigmoid_po_kernel(
     nc = tc.nc
     with ExitStack() as ctx:
         keep = ctx.enter_context(tc.tile_pool(name="keep", bufs=1))
+        placed = ctx.enter_context(tc.tile_pool(name="placed", bufs=1))
         psum = ctx.enter_context(tc.psum_pool(name="psum", bufs=1))
 
         def bank(number):
@@ -46,7 +49,7 @@ def tile_picked_ysplat_sigmoid_po_kernel(
 
         pos = [keep.tile([P, V // GROUP], U16, name=f"pos{d}") for d in range(D)]
         picks = keep.tile([P, S // GROUP], U16, name="picks")
-        w_raw = [keep.tile([P, PACK, N // 2], F32, name=f"w_raw{half}") for half in range(2)]
+        w_raw = [placed.tile([P, PACK, N // 2], F32, name=f"w_raw{half}", offset=half * HALF_W_BYTES) for half in range(2)]
         x_table = keep.tile([P, T], I32, name="x_table")
         scale_table = keep.tile([P, T], U8, name="scale_table")
         op_table = keep.tile([P, S], F32, name="op_table")
@@ -58,16 +61,16 @@ def tile_picked_ysplat_sigmoid_po_kernel(
         x_source = x_words[0].rearrange("p n j -> p (n j)").bitcast(I32)
         fall_pieces = fall.rearrange("d p (c v) -> (d p c) v", v=P)[0 : D * P * CHUNKS : P + 1, :]
         first_piece = P - FALL_PIECES
-        nc.sync.dma_start(picks[:], offs)
-        nc.sync.dma_start(scale_table[P - BLOCKS :, :].bitcast(I32), x_scales[0].bitcast(I32))
         nc.sync.dma_start(op_table[P - 1 :, :], op[0:1, :])
         nc.sync.dma_start(pos[0][:], pos1)
+        nc.sync.dma_start(picks[:], offs)
+        nc.sync.dma_start(scale_table[P - BLOCKS :, :].bitcast(I32), x_scales[0].bitcast(I32))
         nc.sync.dma_start(pos[1][:], pos2)
+        nc.sync.dma_start(x_table[:, :X_AHEAD], x_source[:, :X_AHEAD])
         nc.sync.dma_start(fall_rows[first_piece : first_piece + 8, :], fall_pieces[0:8, :])
         nc.sync.dma_start(fall_rows[first_piece + 8 :, :], fall_pieces[8:, :])
-        nc.sync.dma_start(x_table[:, : T // 2], x_source[:, : T // 2])
         nc.sync.dma_start(pos[2][:], pos3)
-        nc.sync.dma_start(x_table[:, T // 2 :], x_source[:, T // 2 :])
+        nc.sync.dma_start(x_table[:, X_AHEAD:], x_source[:, X_AHEAD:])
         for half in range(2):
             w_cols = slice(half * N // 2, (half + 1) * N // 2)
             nc.sync.dma_start(w_raw[half][:], w1.rearrange("(p j) c -> p j c", j=PACK)[:, :, w_cols])
@@ -106,27 +109,28 @@ def tile_picked_ysplat_sigmoid_po_kernel(
             return turned[:, :, P - 1]
 
         weight_cols = [keep.tile([P, CHUNKS], F32, name=f"weight_cols{d}") for d in range(D)]
-        weight_rows = keep.tile([P, D, V], F32, name="weight_rows")
+        weight_rows = [keep.tile([P, V], F32, name=f"weight_rows{d}") for d in range(D - 1)]
 
         def spread(d, number):
             rows_of = bank(number)
             for c in range(CHUNKS):
                 nc.tensor.transpose(rows_of[:, c, :], weight_cols[d][:, c : c + 1].to_broadcast([P, P]), ident[:])
-            nc.scalar.copy(weight_rows[:, d, :], rows_of[:].rearrange("p c v -> p (c v)"))
+            return rows_of[:].rearrange("p c v -> p (c v)")
 
         opacity = [opacity_columns(d, d) for d in range(D)]
         nc.vector.tensor_tensor(weight_cols[0][:], opacity[0], fall_cols[:, 0, :], MULT)
         behind0 = keep.tile([P, CHUNKS], F32, name="behind0")
         nc.vector.scalar_tensor_tensor(behind0[:], weight_cols[0][:], 1.0, fall_cols[:, 1, :], SUBTRACT, MULT)
-        spread(0, 3)
+        nc.scalar.copy(weight_rows[0][:], spread(0, 3))
         nc.vector.scalar_tensor_tensor(weight_cols[1][:], opacity[1], -1.0, behind0[:], MULT, MULT)
         seen = keep.tile([P, CHUNKS], F32, name="seen")
         nc.vector.scalar_tensor_tensor(seen[:], weight_cols[0][:], 1.0, weight_cols[1][:], SUBTRACT, ADD)
         behind1 = keep.tile([P, CHUNKS], F32, name="behind1")
-        nc.vector.tensor_tensor(behind1[:], seen[:], fall_cols[:, 2, :], MULT)
-        spread(1, 4)
-        nc.vector.scalar_tensor_tensor(weight_cols[2][:], opacity[2], -1.0, behind1[:], MULT, MULT)
-        spread(2, 5)
+        nc.vector.scalar_tensor_tensor(behind1[:], seen[:], -1.0, fall_cols[:, 2, :], MULT, MULT)
+        nc.scalar.copy(weight_rows[1][:], spread(1, 4))
+        for c in range(CHUNKS):
+            nc.scalar.activation(weight_cols[2][:, c : c + 1], opacity[2][:, c : c + 1], ACT.Copy, scale=behind1[:, c : c + 1])
+        last_spread = spread(2, 5)
 
         x_codes = keep.tile([P, S], U32, name="x_codes", align_bytes=64)
         for h in range(2):
@@ -154,9 +158,11 @@ def tile_picked_ysplat_sigmoid_po_kernel(
 
         round_w(nc.scalar.copy, 0, 0)
         round_w(nc.scalar.copy, 0, 1)
+        weight_rows.append(placed.tile([P, V], F32, name="weight_rows2", offset=0))
+        nc.scalar.copy(weight_rows[2][:], last_spread)
         quantise_w(FIRST, 1)
         round_w(nc.vector.tensor_copy, 1, 1)
-        round_w(nc.vector.tensor_copy, 1, 0)
+        round_w(nc.scalar.copy, 1, 0)
         quantise_w(ON_SCALAR, 2)
         quantise_w(SECOND, 1)
 
@@ -189,7 +195,7 @@ def tile_picked_ysplat_sigmoid_po_kernel(
             return pos[d][:, span.start // GROUP : span.stop // GROUP]
 
         def fetch_on_vector(values, t, d, span):
-            nc.vector.tensor_tensor(values, rows[t][:].indirect(entries_of(d, span)), weight_rows[:, d, span], MULT)
+            nc.vector.tensor_tensor(values, rows[t][:].indirect(entries_of(d, span)), weight_rows[d][:, span], MULT)
 
         def turn(total, values, first, last):
             blocks = values.shape[1] // P

@@ -95,11 +95,6 @@ def tile_picked_ysplat_sigmoid_po_kernel(
                 x_scale_rows[first_row : first_row + SCALE_ROWS, :].bitcast(I32),
             )
 
-        fall_turned = bank(7)
-        nc.tensor.transpose(fall_turned[:, 0, :], fall_rows[:], ident[:])
-        fall_cols = keep.tile([P, D, CHUNKS], F32, name="fall_cols")
-        nc.vector.tensor_copy(fall_cols[:].rearrange("p d c -> p (d c)"), fall_turned[:, 0, first_piece:])
-
         def opacity_columns(d, number):
             looked_up = keep.tile([P, V], F32, name=f"opacity{d}")
             nc.scalar.activation(looked_up[:], op_table[:].indirect(pos[d][:]), ACT.Copy)
@@ -117,7 +112,12 @@ def tile_picked_ysplat_sigmoid_po_kernel(
                 nc.tensor.transpose(rows_of[:, c, :], weight_cols[d][:, c : c + 1].to_broadcast([P, P]), ident[:])
             return rows_of[:].rearrange("p c v -> p (c v)")
 
-        opacity = [opacity_columns(d, d) for d in range(D)]
+        opacity = [opacity_columns(0, 0)]
+        fall_turned = bank(7)
+        nc.tensor.transpose(fall_turned[:, 0, :], fall_rows[:], ident[:])
+        fall_cols = keep.tile([P, D, CHUNKS], F32, name="fall_cols")
+        nc.vector.tensor_copy(fall_cols[:].rearrange("p d c -> p (d c)"), fall_turned[:, 0, first_piece:])
+        opacity.append(opacity_columns(1, 1))
         nc.vector.tensor_tensor(weight_cols[0][:], opacity[0], fall_cols[:, 0, :], MULT)
         behind0 = keep.tile([P, CHUNKS], F32, name="behind0")
         nc.vector.scalar_tensor_tensor(behind0[:], weight_cols[0][:], 1.0, fall_cols[:, 1, :], SUBTRACT, MULT)
@@ -128,6 +128,7 @@ def tile_picked_ysplat_sigmoid_po_kernel(
         behind1 = keep.tile([P, CHUNKS], F32, name="behind1")
         nc.vector.scalar_tensor_tensor(behind1[:], seen[:], -1.0, fall_cols[:, 2, :], MULT, MULT)
         nc.scalar.copy(weight_rows[1][:], spread(1, 4))
+        opacity.append(opacity_columns(2, 1))
         for c in range(CHUNKS):
             nc.scalar.activation(weight_cols[2][:, c : c + 1], opacity[2][:, c : c + 1], ACT.Copy, scale=behind1[:, c : c + 1])
         last_spread = spread(2, 5)
@@ -162,7 +163,7 @@ def tile_picked_ysplat_sigmoid_po_kernel(
         nc.scalar.copy(weight_rows[2][:], last_spread)
         quantise_w(FIRST, 1)
         round_w(nc.vector.tensor_copy, 1, 1)
-        round_w(nc.scalar.copy, 1, 0)
+        round_w(nc.vector.tensor_copy, 1, 0)
         quantise_w(ON_SCALAR, 2)
         quantise_w(SECOND, 1)
 

@@ -289,7 +289,7 @@ def tile_picked_ysplat_sigmoid_po_kernel(
             if span == low:
                 for t in range(2):
                     hand_out(t, whole, flat(backs[t]))
-                store(slice(0, 2), whole)
+                    store(slice(t, t + 1), whole)
             hand_out(ON_SCALAR, span, flat(back)[:, low])
 
         layers = keep.tile([P, D, V], F32, name="direct")

@@ -185,7 +185,7 @@ def tile_picked_ysplat_sigmoid_po_kernel(
                 nc.scalar.activation(rows[t][:, cols], acc, ACT.Sigmoid)
 
         y = keep.tile([P, PACK, V], F32, name="y")
-        y_bf = keep.tile([P, V, PACK], BF16, name="y_bf", align_bytes=64)
+        y_bf = placed.tile([P, V, PACK], BF16, name="y_bf", align_bytes=64, offset=2 * HALF_W_BYTES)
         y_codes = keep.tile([P, V], U32, name="y_codes", align_bytes=64)
         y_scales = keep.tile([P, V], U8, name="y_scales", align_bytes=64)
         out_rows = out_0.rearrange("(p t) v -> p t v", t=PACK)
@@ -213,25 +213,23 @@ def tile_picked_ysplat_sigmoid_po_kernel(
         def flat(tile):
             return tile[:].rearrange("p c n -> p (c n)")
 
-        def sum_turned(t, number):
-            total = bank(number)
-            layers = keep.tile([P, D, V], F32, name=f"layers{t}")
-            for d in range(D):
-                fetch_on_vector(layers[:, d, :], t, d, whole)
-                turn(total, layers[:, d, :], d == 0, d == D - 1)
-            return total
+        def blocks_of(span):
+            return range(span.start // P, span.stop // P)
 
         sums = keep.tile([P, 2, CHUNKS, P], F32, name="sums")
 
-        def leave(half, total):
+        def leave(half, total, span):
+            chunks = slice(span.start // P, span.stop // P)
             nc.scalar.copy(
-                sums[:, :, :, half * P // 2 : (half + 1) * P // 2].rearrange("v t c m -> v c t m"),
-                total[:].rearrange("v c (t m) -> v c t m", t=2),
+                sums[:, :, chunks, half * P // 2 : (half + 1) * P // 2].rearrange("v t c m -> v c t m"),
+                total[:, 0 : len(blocks_of(span)), :].rearrange("v c (t m) -> v c t m", t=2),
             )
 
-        def turn_back(t, number):
+        def turn_back(span, number):
             back = bank(number)
-            turn(back, sums[:, t, :, :].rearrange("v c p -> v (c p)"), True, True)
+            for t in range(2):
+                for i, c in enumerate(blocks_of(span)):
+                    nc.tensor.transpose(back[:, 2 * t + i, :], sums[:, t, c, :], ident[:])
             return back
 
         def store(tiles, span):
@@ -247,7 +245,7 @@ def tile_picked_ysplat_sigmoid_po_kernel(
             turn(turned, values[:], True, True)
             return turned
 
-        scaled = keep.tile([P, D, V], F32, name="scaled")
+        scaled = placed.tile([P, D, V], F32, name="scaled", offset=2 * HALF_W_BYTES)
 
         def weigh(d, span, turned, back):
             for c in range(span.start // P, span.stop // P):
@@ -269,28 +267,46 @@ def tile_picked_ysplat_sigmoid_po_kernel(
             nc.sync.dma_start(out_words[:, span], y_codes[:, span].bitcast(I32))
 
         low, high = slice(0, V // 2), slice(V // 2, V)
+
+        def hand_out_turned(span, back):
+            nc.scalar.copy(y[:, 0:2, span], back[:].rearrange("p (t c) v -> p t (c v)", t=2))
+            store(slice(0, 2), span)
+
         for t in (FIRST, ON_SCALAR, SECOND):
             features(t)
-        total_first = sum_turned(FIRST, 0)
+        total_first = bank(0)
+        layers_first = keep.tile([P, D, V], F32, name="layers_first")
+        for d in range(D):
+            fetch_on_vector(layers_first[:, d, :], FIRST, d, whole)
+            turn(total_first, layers_first[:, d, :], d == 0, d == D - 1)
         turned0 = fetch_on_scalar(0, 1)
         turned1 = fetch_on_scalar(1, 2)
-        leave(0, total_first)
+        leave(0, total_first, whole)
         features(LAST)
-        total_second = sum_turned(SECOND, 5)
-        back_low, back_high = bank(3), bank(6)
-        weigh(0, low, turned0, back_low)
-        weigh(0, high, turned0, back_high)
         turned2 = fetch_on_scalar(2, 0)
-        leave(1, total_second)
-        backs = [turn_back(0, 4), turn_back(1, 1)]
-        for span, back in ((low, back_low), (high, back_high)):
-            weigh(1, span, turned1, back)
-            weigh(2, span, turned2, back)
-            if span == low:
-                for t in range(2):
-                    hand_out(t, whole, flat(backs[t]))
-                    store(slice(t, t + 1), whole)
-            hand_out(ON_SCALAR, span, flat(back)[:, low])
+        totals = {low.start: bank(5), high.start: bank(4)}
+        layers_second = keep.tile([P, D, V], F32, name="layers_second")
+        for d in range(D):
+            if d < D - 1:
+                fetch_on_vector(layers_second[:, d, :], SECOND, d, whole)
+            for span in (low, high):
+                if d == D - 1:
+                    fetch_on_vector(layers_second[:, d, span], SECOND, d, span)
+                turn(totals[span.start], layers_second[:, d, span], d == 0, d == D - 1)
+        back_low, back_high = bank(3), bank(6)
+        leave(1, totals[low.start], low)
+        first_low = turn_back(low, 7)
+        weigh(0, low, turned0, back_low)
+        leave(1, totals[high.start], high)
+        first_high = turn_back(high, 5)
+        weigh(1, low, turned1, back_low)
+        hand_out_turned(low, first_low)
+        weigh(2, low, turned2, back_low)
+        hand_out_turned(high, first_high)
+        hand_out(ON_SCALAR, low, flat(back_low)[:, low])
+        for d, turned in enumerate((turned0, turned1, turned2)):
+            weigh(d, high, turned, back_high)
+        hand_out(ON_SCALAR, high, flat(back_high)[:, low])
 
         layers = keep.tile([P, D, V], F32, name="direct")
         pair = keep.tile([P, V], F32, name="pair")
@@ -301,21 +317,21 @@ def tile_picked_ysplat_sigmoid_po_kernel(
         def add_last(span):
             nc.vector.tensor_tensor(y[:, LAST, span], pair[:, span], layers[:, 2, span], ADD)
 
-        for d in range(D):
-            fetch_on_vector(layers[:, d, low], LAST, d, low)
+        for d in range(D - 1):
+            fetch_on_vector(layers[:, d, :], LAST, d, whole)
+        fetch_on_vector(layers[:, 2, low], LAST, 2, low)
         add_pair(low)
-        fetch_on_vector(layers[:, 0, high], LAST, 0, high)
+        fetch_on_vector(layers[:, 2, high], LAST, 2, high)
         add_last(low)
         store(slice(ON_SCALAR, PACK), low)
-        for d in range(1, D):
-            fetch_on_vector(layers[:, d, high], LAST, d, high)
-        add_pair(high)
-        round_y(nc.vector.tensor_copy, low)
-        add_last(high)
+        for add in (add_pair, add_last):
+            for c in (2, 3):
+                add(pixels(c))
         store(slice(ON_SCALAR, PACK), high)
-        quantise(low)
+        round_y(nc.vector.tensor_copy, low)
         round_y(nc.scalar.copy, pixels(3))
         round_y(nc.vector.tensor_copy, pixels(2))
+        quantise(low)
         quantise(high)
 
         for q in range(P // QUADRANT):

from contextlib import ExitStack

import concourse.mybir as mybir
from concourse.masks import make_identity

K, T, S, V, N, D = 512, 4096, 1024, 512, 512, 3
FLOPS = 2 * K * N * S

F32 = mybir.dt.float32
BF16 = mybir.dt.bfloat16
I32 = mybir.dt.int32
U32 = mybir.dt.uint32
U16 = mybir.dt.uint16
U8 = mybir.dt.uint8
FP8X4 = mybir.dt.float8_e4m3fn_x4
ACT = mybir.ActivationFunctionType
MULT, ADD, SUBTRACT = mybir.AluOpType.mult, mybir.AluOpType.add, mybir.AluOpType.subtract

P = 128
PACK = 4
GROUP = 16
QUADRANT = 32
SCALE_ROWS = 4
BLOCKS = K // 32
CHUNKS = V // P
HALF = S // 2
FIRST, SECOND, ON_SCALAR, LAST = range(PACK)
SLOT = {FIRST: 0, ON_SCALAR: 1, LAST: 2, SECOND: 3}
PRODUCT_BANK = {FIRST: 0, ON_SCALAR: 2, SECOND: 4, LAST: 6}
FALL_PIECES = D * CHUNKS
HALF_W_BYTES = 4 * PACK * N // 2
X_AHEAD = 3 * T // 8


def tile_picked_ysplat_sigmoid_po_kernel(
    tc, x_words, x_scales, w1, op, fall, offs, pos1, pos2, pos3, out_0, out_1, out_2
):
    nc = tc.nc
    with ExitStack() as ctx:
        keep = ctx.enter_context(tc.tile_pool(name="keep", bufs=1))
        placed = ctx.enter_context(tc.tile_pool(name="placed", bufs=1))
        psum = ctx.enter_context(tc.psum_pool(name="psum", bufs=1))

        def bank(number):
            return psum.tile([P, 4, P], F32, name=f"bank{number}")

        def pixels(c):
            return slice(c * P, (c + 1) * P)

        pos = [keep.tile([P, V // GROUP], U16, name=f"pos{d}") for d in range(D)]
        picks = keep.tile([P, S // GROUP], U16, name="picks")
        w_raw = [placed.tile([P, PACK, N // 2], F32, name=f"w_raw{half}", offset=half * HALF_W_BYTES) for half in range(2)]
        x_table = keep.tile([P, T], I32, name="x_table")
        scale_table = keep.tile([P, T], U8, name="scale_table")
        op_table = keep.tile([P, S], F32, name="op_table")
        fall_rows = keep.tile([P, P], F32, name="fall_rows")
        ident = keep.tile([P, P], F32, name="ident")
        x_scale_rows = keep.tile([P, S], U8, name="x_scale_rows")
        x_scale = keep.tile([P, S], U8, name="x_scale", align_bytes=64)

        x_source = x_words[0].rearrange("p n j -> p (n j)").bitcast(I32)
        fall_pieces = fall.rearrange("d p (c v) -> (d p c) v", v=P)[0 : D * P * CHUNKS : P + 1, :]
        first_piece = P - FALL_PIECES
        nc.sync.dma_start(op_table[P - 1 :, :], op[0:1, :])
        nc.sync.dma_start(pos[0][:], pos1)
        nc.sync.dma_start(picks[:], offs)
        nc.sync.dma_start(scale_table[P - BLOCKS :, :].bitcast(I32), x_scales[0].bitcast(I32))
        nc.sync.dma_start(pos[1][:], pos2)
        nc.sync.dma_start(x_table[:, :X_AHEAD], x_source[:, :X_AHEAD])
        nc.sync.dma_start(fall_rows[first_piece : first_piece + 8, :], fall_pieces[0:8, :])
        nc.sync.dma_start(fall_rows[first_piece + 8 :, :], fall_pieces[8:, :])
        nc.sync.dma_start(pos[2][:], pos3)
        nc.sync.dma_start(x_table[:, X_AHEAD:], x_source[:, X_AHEAD:])
        for half in range(2):
            w_cols = slice(half * N // 2, (half + 1) * N // 2)
            nc.sync.dma_start(w_raw[half][:], w1.rearrange("(p j) c -> p j c", j=PACK)[:, :, w_cols])

        warm = keep.tile([P, 2], F32, name="warm")
        nc.vector.memset(warm[:, 0:1], 0.0)
        nc.scalar.activation(warm[:, 1:2], warm[:, 0:1], ACT.Sigmoid)

        for table, rows_free in ((scale_table[:].bitcast(I32), P - BLOCKS), (fall_rows[:], first_piece)):
            width = table.shape[1]
            nc.vector.memset(table[:rows_free, 0 : width - 1], 0)
            nc.vector.memset(table[:rows_free, width - 1 : width], 0)
        nc.gpsimd.memset(op_table[: P - 1, :], 0.0)
        make_identity(nc, ident[:])
        nc.gpsimd.memset(x_scale[:].bitcast(I32), 0)

        nc.vector.tensor_copy(x_scale_rows[:], scale_table[:].indirect(picks[:]))
        for q in range(P // QUADRANT):
            first_row = P - BLOCKS + SCALE_ROWS * q
            nc.sync.dma_start(
                x_scale[QUADRANT * q : QUADRANT * q + SCALE_ROWS, :].bitcast(I32),
                x_scale_rows[first_row : first_row + SCALE_ROWS, :].bitcast(I32),
            )

        def opacity_columns(d, number):
            looked_up = keep.tile([P, V], F32, name=f"opacity{d}")
            nc.scalar.activation(looked_up[:], op_table[:].indirect(pos[d][:]), ACT.Copy)
            turned = bank(number)
            for c in range(CHUNKS):
                nc.tensor.transpose(turned[:, c, :], looked_up[:, pixels(c)], ident[:])
            return turned[:, :, P - 1]

        weight_cols = [keep.tile([P, CHUNKS], F32, name=f"weight_cols{d}") for d in range(D)]
        weight_rows = [keep.tile([P, V], F32, name=f"weight_rows{d}") for d in range(D - 1)]

        def spread(d, number):
            rows_of = bank(number)
            for c in range(CHUNKS):
                nc.tensor.transpose(rows_of[:, c, :], weight_cols[d][:, c : c + 1].to_broadcast([P, P]), ident[:])
            return rows_of[:].rearrange("p c v -> p (c v)")

        opacity = [opacity_columns(0, 0)]
        fall_turned = bank(7)
        nc.tensor.transpose(fall_turned[:, 0, :], fall_rows[:], ident[:])
        fall_cols = keep.tile([P, D, CHUNKS], F32, name="fall_cols")
        nc.vector.tensor_copy(fall_cols[:].rearrange("p d c -> p (d c)"), fall_turned[:, 0, first_piece:])
        opacity.append(opacity_columns(1, 1))
        nc.vector.tensor_tensor(weight_cols[0][:], opacity[0], fall_cols[:, 0, :], MULT)
        behind0 = keep.tile([P, CHUNKS], F32, name="behind0")
        nc.vector.scalar_tensor_tensor(behind0[:], weight_cols[0][:], 1.0, fall_cols[:, 1, :], SUBTRACT, MULT)
        nc.scalar.copy(weight_rows[0][:], spread(0, 3))
        nc.vector.scalar_tensor_tensor(weight_cols[1][:], opacity[1], -1.0, behind0[:], MULT, MULT)
        seen = keep.tile([P, CHUNKS], F32, name="seen")
        nc.vector.scalar_tensor_tensor(seen[:], weight_cols[0][:], 1.0, weight_cols[1][:], SUBTRACT, ADD)
        behind1 = keep.tile([P, CHUNKS], F32, name="behind1")
        nc.vector.scalar_tensor_tensor(behind1[:], seen[:], -1.0, fall_cols[:, 2, :], MULT, MULT)
        nc.scalar.copy(weight_rows[1][:], spread(1, 4))
        opacity.append(opacity_columns(2, 1))
        for c in range(CHUNKS):
            nc.scalar.activation(weight_cols[2][:, c : c + 1], opacity[2][:, c : c + 1], ACT.Copy, scale=behind1[:, c : c + 1])
        last_spread = spread(2, 5)

        x_codes = keep.tile([P, S], U32, name="x_codes", align_bytes=64)
        for h in range(2):
            entries = picks[:, h * HALF // GROUP : (h + 1) * HALF // GROUP]
            nc.vector.tensor_copy(x_codes[:, h * HALF : (h + 1) * HALF], x_table[:].bitcast(U32).indirect(entries))

        w_bf = keep.tile([P, N, PACK], BF16, name="w_bf", align_bytes=64)
        w_codes = keep.tile([P, N], U32, name="w_codes", align_bytes=64)
        w_scales = keep.tile([P, N], U8, name="w_scales", align_bytes=64)

        def round_w(copy, half, pair_of_t):
            source = w_raw[half][:].rearrange("p j (m t) -> p m j t", t=PACK)[:, :, :, 2 * pair_of_t : 2 * pair_of_t + 2]
            if pair_of_t == 0:
                target = w_bf[:, pixels(SLOT[half]), :].rearrange("p (t m) j -> p m j t", t=2)
            else:
                both = w_bf[:, SLOT[ON_SCALAR] * P : (SLOT[LAST] + 1) * P, :].rearrange("p (t m) j -> p m j t", t=2)
                target = both[:, half * P // 2 : (half + 1) * P // 2, :, :]
            copy(target, source)

        def quantise_w(t, count):
            cols = slice(SLOT[t] * P, (SLOT[t] + count) * P)
            nc.vector.quantize_mx(
                out=w_codes[:, cols].bitcast(FP8X4), scales=w_scales[:, cols], in_=w_bf[:, cols, :].rearrange("p m j -> p (m j)")
            )

        round_w(nc.scalar.copy, 0, 0)
        round_w(nc.scalar.copy, 0, 1)
        weight_rows.append(placed.tile([P, V], F32, name="weight_rows2", offset=0))
        nc.scalar.copy(weight_rows[2][:], last_spread)
        quantise_w(FIRST, 1)
        round_w(nc.vector.tensor_copy, 1, 1)
        round_w(nc.vector.tensor_copy, 1, 0)
        quantise_w(ON_SCALAR, 2)
        quantise_w(SECOND, 1)

        rows = [keep.tile([P, S], F32, name=f"rows{t}") for t in range(PACK)]

        def features(t):
            for h in range(2):
                cols = slice(h * HALF, (h + 1) * HALF)
                acc = bank(PRODUCT_BANK[t] + h)[:].rearrange("p c n -> p (c n)")
                nc.tensor.matmul_mx(
                    out=acc,
                    lhsT=w_codes[:, pixels(SLOT[t])].bitcast(FP8X4),
                    lhsT_scale=w_scales[:, pixels(SLOT[t])],
                    rhs=x_codes[:, cols].bitcast(FP8X4),
                    rhs_scale=x_scale[:, cols],
                    start=True,
                    stop=True,
                )
                nc.scalar.activation(rows[t][:, cols], acc, ACT.Sigmoid)

        y = keep.tile([P, PACK, V], F32, name="y")
        y_bf = placed.tile([P, V, PACK], BF16, name="y_bf", align_bytes=64, offset=2 * HALF_W_BYTES)
        y_codes = keep.tile([P, V], U32, name="y_codes", align_bytes=64)
        y_scales = keep.tile([P, V], U8, name="y_scales", align_bytes=64)
        out_rows = out_0.rearrange("(p t) v -> p t v", t=PACK)
        out_words = out_1[0].rearrange("p n j -> p (n j)").bitcast(I32)
        whole = slice(0, V)

        def entries_of(d, span):
            return pos[d][:, span.start // GROUP : span.stop // GROUP]

        def fetch_on_vector(values, t, d, span):
            nc.vector.tensor_tensor(values, rows[t][:].indirect(entries_of(d, span)), weight_rows[d][:, span], MULT)

        def turn(total, values, first, last):
            blocks = values.shape[1] // P
            for c in range(blocks):
                nc.tensor.matmul(
                    total[:, c, :],
                    lhsT=values[:, pixels(c)],
                    rhs=ident[:],
                    is_transpose=True,
                    start=first and c == 0,
                    stop=last and c == blocks - 1,
                )

        def flat(tile):
            return tile[:].rearrange("p c n -> p (c n)")

        def blocks_of(span):
            return range(span.start // P, span.stop // P)

        sums = keep.tile([P, 2, CHUNKS, P], F32, name="sums")

        def leave(half, total, span):
            chunks = slice(span.start // P, span.stop // P)
            nc.scalar.copy(
                sums[:, :, chunks, half * P // 2 : (half + 1) * P // 2].rearrange("v t c m -> v c t m"),
                total[:, 0 : len(blocks_of(span)), :].rearrange("v c (t m) -> v c t m", t=2),
            )

        def turn_back(span, number):
            back = bank(number)
            for t in range(2):
                for i, c in enumerate(blocks_of(span)):
                    nc.tensor.transpose(back[:, 2 * t + i, :], sums[:, t, c, :], ident[:])
            return back

        def store(tiles, span):
            nc.sync.dma_start(out_rows[:, tiles, span], y[:, tiles, span])

        def hand_out(t, span, source):
            nc.scalar.copy(y[:, t, span], source)

        def fetch_on_scalar(d, number):
            values = keep.tile([P, V], F32, name=f"values{d}")
            nc.scalar.activation(values[:], rows[ON_SCALAR][:].indirect(pos[d][:]), ACT.Copy)
            turned = bank(number)
            turn(turned, values[:], True, True)
            return turned

        scaled = placed.tile([P, D, V], F32, name="scaled", offset=2 * HALF_W_BYTES)

        def weigh(d, span, turned, back):
            for c in range(span.start // P, span.stop // P):
                nc.scalar.activation(scaled[:, d, pixels(c)], turned[:, c, :], ACT.Copy, scale=weight_cols[d][:, c : c + 1])
            turn(back, scaled[:, d, span], d == 0, d == D - 1)

        def round_y(copy, span):
            copy(
                y_bf[:, span, :].rearrange("p (c i) t -> p c t i", i=4),
                y[:, :, span].rearrange("p t (c i) -> p c t i", i=4),
            )

        def quantise(span):
            nc.vector.quantize_mx(
                out=y_codes[:, span].bitcast(FP8X4),
                scales=y_scales[:, span],
                in_=y_bf[:, span, :].rearrange("p v t -> p (v t)"),
            )
            nc.sync.dma_start(out_words[:, span], y_codes[:, span].bitcast(I32))

        low, high = slice(0, V // 2), slice(V // 2, V)

        def hand_out_turned(span, back):
            nc.scalar.copy(y[:, 0:2, span], back[:].rearrange("p (t c) v -> p t (c v)", t=2))
            store(slice(0, 2), span)

        for t in (FIRST, ON_SCALAR, SECOND):
            features(t)
        total_first = bank(0)
        layers_first = keep.tile([P, D, V], F32, name="layers_first")
        for d in range(D):
            fetch_on_vector(layers_first[:, d, :], FIRST, d, whole)
            turn(total_first, layers_first[:, d, :], d == 0, d == D - 1)
        turned0 = fetch_on_scalar(0, 1)
        turned1 = fetch_on_scalar(1, 2)
        leave(0, total_first, whole)
        features(LAST)
        turned2 = fetch_on_scalar(2, 0)
        totals = {low.start: bank(5), high.start: bank(4)}
        layers_second = keep.tile([P, D, V], F32, name="layers_second")
        for d in range(D):
            if d < D - 1:
                fetch_on_vector(layers_second[:, d, :], SECOND, d, whole)
            for span in (low, high):
                if d == D - 1:
                    fetch_on_vector(layers_second[:, d, span], SECOND, d, span)
                turn(totals[span.start], layers_second[:, d, span], d == 0, d == D - 1)
        back_low, back_high = bank(3), bank(6)
        leave(1, totals[low.start], low)
        first_low = turn_back(low, 7)
        weigh(0, low, turned0, back_low)
        leave(1, totals[high.start], high)
        first_high = turn_back(high, 5)
        weigh(1, low, turned1, back_low)
        hand_out_turned(low, first_low)
        weigh(2, low, turned2, back_low)
        hand_out_turned(high, first_high)
        hand_out(ON_SCALAR, low, flat(back_low)[:, low])
        for d, turned in enumerate((turned0, turned1, turned2)):
            weigh(d, high, turned, back_high)
        hand_out(ON_SCALAR, high, flat(back_high)[:, low])

        layers = keep.tile([P, D, V], F32, name="direct")
        pair = keep.tile([P, V], F32, name="pair")

        def add_pair(span):
            nc.vector.tensor_tensor(pair[:, span], layers[:, 0, span], layers[:, 1, span], ADD)

        def add_last(span):
            nc.vector.tensor_tensor(y[:, LAST, span], pair[:, span], layers[:, 2, span], ADD)

        for d in range(D - 1):
            fetch_on_vector(layers[:, d, :], LAST, d, whole)
        fetch_on_vector(layers[:, 2, low], LAST, 2, low)
        add_pair(low)
        fetch_on_vector(layers[:, 2, high], LAST, 2, high)
        add_last(low)
        store(slice(ON_SCALAR, PACK), low)
        for add in (add_pair, add_last):
            for c in (2, 3):
                add(pixels(c))
        store(slice(ON_SCALAR, PACK), high)
        round_y(nc.vector.tensor_copy, low)
        round_y(nc.scalar.copy, pixels(3))
        round_y(nc.vector.tensor_copy, pixels(2))
        quantise(low)
        quantise(high)

        for q in range(P // QUADRANT):
            queue = nc.scalar if q % 2 else nc.sync
            queue.dma_start(
                out_2[0, SCALE_ROWS * q : SCALE_ROWS * (q + 1), :].bitcast(I32),
                y_scales[QUADRANT * q : QUADRANT * q + SCALE_ROWS, :].bitcast(I32),
            )
